import numpy as np
import ml_dtypes


def mxq(x, axis, fmt="e4m3"):
    dtype, down = {"e4m3": (ml_dtypes.float8_e4m3fn, 7), "e5m2": (ml_dtypes.float8_e5m2, 14)}[fmt]
    v = np.moveaxis(np.asarray(x, np.float32).astype(ml_dtypes.bfloat16).astype(np.float64), axis, -1)
    blocks = v.reshape(v.shape[:-1] + (-1, 32))
    amax = np.abs(blocks).max(-1, keepdims=True)
    byte = np.maximum(np.where(amax > 0, np.frexp(amax)[1] - 1 + 127, 0) - down, 1)
    scale = np.exp2(byte - 127.0)
    codes = (blocks / scale).astype(np.float32).astype(dtype).astype(np.float64)
    return np.moveaxis((codes * scale).reshape(v.shape), -1, axis)


WIDE = False


def mx_kscale(k):
    if not WIDE:
        return np.ones(k)
    levels = np.array([10, -10, 5, -5, 0])
    if k % 512:
        return np.exp2(np.random.permutation(np.resize(levels, k // 32))).repeat(32)
    a = np.empty((k // 512, 16))
    for p in range(k // 512):
        a[p, :8] = np.random.permutation(np.resize(levels, 8))
        for g in range(8):
            far = levels[np.abs(levels - a[p, g]) >= 10]
            a[p, g + 8] = far[np.random.randint(len(far))]
    return np.exp2(a.ravel()).repeat(32)


def f64(x):
    return np.asarray(x).astype(np.float64)


def striped(idx):
    return np.tile(np.asarray(idx).reshape(-1, 16).T, (8, 1)).astype(np.uint16)


def unstriped(offs):
    return offs[:16].T.reshape(-1).astype(np.int64)


E2M1 = np.array([0.0, 0.5, 1.0, 1.5, 2.0, 3.0, 4.0, 6.0, -0.0, -0.5, -1.0, -1.5, -2.0, -3.0, -4.0, -6.0])


def pack_weight(w, fmt):
    k, n = w.shape
    w = f64(np.asarray(w, np.float32).astype(ml_dtypes.bfloat16)).reshape(k // 32, 32, n)
    amax = np.abs(w).max(1)
    if fmt == "e4m3":
        byte = np.frexp(amax)[1] - 1 + 127 - 7
    else:
        mant, ex = np.frexp(amax / 6.0)
        byte = np.where(mant > 0.5, ex, ex - 1) + 127
    byte = np.clip(np.where(amax > 0, byte, 1), 1, 254)
    scaled = (w * np.exp2(127.0 - byte)[:, None, :]).reshape(k, n).astype(np.float32)
    by_word = np.ascontiguousarray(scaled.reshape(k // 512, 128, 4, n).transpose(0, 1, 3, 2))
    if fmt == "e4m3":
        words = by_word.astype(ml_dtypes.float8_e4m3fn).view(np.uint8)
    else:
        c = by_word.astype(ml_dtypes.float4_e2m1fn).view(np.uint8) & 0xF
        words = (c[..., 0::2] | (c[..., 1::2] << 4)).reshape(k // 512, 128, 2 * n)
    return np.ascontiguousarray(words), np.ascontiguousarray(byte.astype(np.uint8).reshape(k // 512, 16, n))


def unpack_weight(words, scales, fmt):
    g, _, n = scales.shape
    words = np.ascontiguousarray(words).reshape(g, 128, n, -1)
    if fmt == "e4m3":
        vals = words.view(ml_dtypes.float8_e4m3fn).astype(np.float64)
    else:
        nib = np.empty((g, 128, n, 4), np.uint8)
        nib[..., 0::2] = words & 0xF
        nib[..., 1::2] = words >> 4
        vals = E2M1[nib]
    vals = vals * np.repeat(np.exp2(scales.astype(np.float64) - 127.0), 8, axis=1)[..., None]
    return vals.transpose(0, 1, 3, 2).reshape(g * 512, n)


B, N, T, D, DV, NQ = 1, 1024, 4096, 1024, 256, 128
PAGE = 512


def setup_inputs():
    n = np.random.standard_normal
    pages = np.random.permutation(T // PAGE)[:B * N // PAGE]
    idx = (pages[:, None] * PAGE + np.arange(PAGE)[None, :]).reshape(-1)
    s = mx_kscale(D)[:, None]
    u = np.ones(T)
    u[idx] = mx_kscale(B * N)
    r = np.random.uniform(0.5, 2.0, T)
    k = n((D, T)) / s
    v = n((DV, T)) / (u * r)
    kp = pack_weight(k, "e2m1")
    vp = pack_weight(v.T, "e4m3")
    return {
        "qT": (n((B, D, NQ)) * s * (1.30 / np.sqrt(D))).astype(np.float32),
        "k_words": np.ascontiguousarray(kp[0].reshape(D // 1024, 2, 128, T, 2).transpose(0, 2, 3, 1, 4)).reshape(D // 1024, 128, T, 4),
        "k_scales": kp[1],
        "v_words": vp[0],
        "v_scales": vp[1],
        "vs": np.tile(u * r, (128, 1)).astype(np.float32),
        "kb": np.tile(n(T), (128, 1)).astype(np.float32),
        "offs": striped(idx),
        "voffs": striped((pages[:, None] * DV + np.arange(DV)[None, :]).reshape(-1)),
    }


def reference(qT, k_words, k_scales, v_words, v_scales, vs, kb, offs, voffs):
    idx = unstriped(offs)
    k = unpack_weight(k_words.reshape(D // 1024, 128, T, 2, 2).transpose(0, 3, 1, 2, 4).reshape(D // 512, 128, 2 * T), k_scales, "e2m1")
    v = unpack_weight(v_words, v_scales, "e4m3")
    v = v.reshape(T // 512, 512, DV)[unstriped(voffs)[::DV] // DV].reshape(B, N, DV)
    pick = lambda x: x[:, idx].reshape(x.shape[0], B, N).transpose(1, 0, 2)
    q = f64(qT)
    score = mxq(q, 1, "e4m3").transpose(0, 2, 1) @ pick(k)
    score = score + pick(f64(kb))[:, :1, :]
    p = 1.0 / (1.0 + np.exp(-score))
    w = p * pick(f64(vs))[:, :1, :]
    y = mxq(w, 2, "e4m3") @ v
    y = y / 16.0
    return y

@@ -1,0 +1,183 @@
+from contextlib import ExitStack
+
+import concourse.mybir as mybir
+from concourse.masks import make_identity
+
+F32 = mybir.dt.float32
+BF16 = mybir.dt.bfloat16
+I32 = mybir.dt.int32
+U32 = mybir.dt.uint32
+U16 = mybir.dt.uint16
+U8 = mybir.dt.uint8
+FP8X4 = mybir.dt.float8_e4m3fn_x4
+FP4X4 = mybir.dt.float4_e2m1fn_x4
+SIGMOID = mybir.ActivationFunctionType.Sigmoid
+COPY = mybir.ActivationFunctionType.Copy
+MULT = mybir.AluOpType.mult
+
+P = 128
+PACK = 4
+N, T, D, DV, NQ = 1024, 4096, 1024, 256, 128
+PAGE = 512
+PAGES = N // PAGE
+POOL_PAGES = T // PAGE
+PASSES = D // (P * PACK)
+ROW = P - 1
+SHIFT = 16
+
+FLOPS = 2 * NQ * N * D + 2 * NQ * N * DV
+BYTES = 4 * D * NQ + 4 * P * T + 32 * T + 4 * P * POOL_PAGES * DV + 16 * POOL_PAGES * DV + 8 * T + 2 * P * (N + PAGES * DV) // 16 + 4 * NQ * DV
+
+
+def tile_attend_pkv4_sigmoid_bias_kernel(tc, qT, k_words, k_scales, v_words, v_scales, vs, kb, offs, voffs, out):
+    nc = tc.nc
+    with ExitStack() as ctx:
+        lists = ctx.enter_context(tc.tile_pool(name="lists", bufs=1))
+        sb = ctx.enter_context(tc.tile_pool(name="sb", bufs=1))
+        shared = ctx.enter_context(tc.tile_pool(name="shared", bufs=1))
+        ps = ctx.enter_context(tc.psum_pool(name="ps", bufs=1))
+
+        offs_sb = lists.tile([P, N // 16], U16, name="offs_sb")
+        voffs_sb = lists.tile([P, PAGES * DV // 16], U16, name="voffs_sb")
+        nc.sync.dma_start(offs_sb[:], offs)
+        nc.sync.dma_start(voffs_sb[:], voffs)
+
+        q_raw = sb.tile([P, PASSES, PACK, NQ], F32, name="q_raw")
+        nc.sync.dma_start(q_raw[:], qT[0].rearrange("(o p j) q -> p o j q", o=PASSES, j=PACK))
+        kw_win = sb.tile([P, T], I32, name="kw_win")
+        nc.sync.dma_start(kw_win[:], k_words[0].rearrange("p t b -> p (t b)").bitcast(I32))
+
+        kb_win = sb.tile([P, T], F32, name="kb_win")
+        vs_win = shared.tile([P, T], F32, name="vs_win", offset=0)
+        vs_fill = sb.tile([P, 8], F32, name="vs_fill")
+        nc.scalar.dma_start(vs_fill[:], vs[:, 0:8])
+        nc.scalar.dma_start(kb_win[ROW:P, :], kb[0:1, :])
+        nc.scalar.dma_start(vs_win[ROW:P, :], vs[0:1, :])
+        zero = sb.tile([P, 8], F32, name="zero")
+        nc.vector.memset(zero[:], 0.0)
+        warm = sb.tile([P, 8], F32, name="warm")
+        nc.scalar.activation(warm[:], zero[:], SIGMOID)
+
+        ks_win = sb.tile([P, T // 4], I32, name="ks_win")
+        nc.vector.memset(ks_win[:], 0)
+        ks_rows = k_scales.rearrange("o (u r) t -> r u o t", r=4)
+        for r in range(4):
+            nc.scalar.dma_start(ks_win[r:P:SHIFT, :], ks_rows[r].bitcast(I32))
+
+        nc.scalar.copy(vs_win[0:ROW, :], vs_fill[0:ROW, 0:1].to_broadcast([ROW, T]))
+        for h in range(2):
+            nc.vector.memset(kb_win[0:ROW, h * T // 2 : (h + 1) * T // 2], 0.0)
+
+        ks_last = sb.tile([P, N // 4], I32, name="ks_last", align_bytes=64)
+        vsc_win = sb.tile([P, POOL_PAGES * DV // 4], I32, name="vsc_win")
+        nc.vector.memset(vsc_win[:], 0)
+        ident = sb.tile([P, P], F32, name="ident")
+        make_identity(nc, ident[:])
+        vsc_rows = v_scales.rearrange("g (u r) e -> r u g e", r=4)
+        for r in range(4):
+            nc.gpsimd.dma_start(vsc_win[r:P:32, :].rearrange("p (g e) -> p g e", g=POOL_PAGES), vsc_rows[r].bitcast(I32))
+
+        kb_got = sb.tile([P, N], F32, name="kb_got")
+        nc.vector.tensor_copy(kb_got[:], kb_win[:].indirect(offs_sb[:]))
+        kb_col = sb.tile([P, PAGES * PACK], F32, name="kb_col")
+        for g in range(PAGES):
+            kb_turned = ps.tile([P, PACK, P], F32, name="kb_turned", tag="early", bufs=2)
+            for t in range(PACK):
+                nc.tensor.transpose(kb_turned[:, t, :], kb_got[:, g * PAGE + t : (g + 1) * PAGE : PACK], ident[:])
+            nc.scalar.copy(kb_col[:, g * PACK : (g + 1) * PACK], kb_turned[:, :, ROW])
+
+        ks_got = shared.tile([P, N], U8, name="ks_got", offset=20480 - 512)
+        nc.vector.tensor_copy(ks_got[:], ks_win[:].bitcast(U8).indirect(offs_sb[:]))
+        ks_first = sb.tile([P, N // 4], I32, name="ks_first", align_bytes=64)
+        nc.vector.tensor_copy(
+            ks_first[:].bitcast(U8).rearrange("p (g t m) -> p g m t", g=PAGES, t=PACK),
+            ks_got[:].rearrange("p (g m t) -> p g m t", g=PAGES, t=PACK),
+        )
+        nc.sync.dma_start(ks_last[0 : P - SHIFT, :], ks_first[SHIFT:P, :])
+        ks_planes = [ks_first[:].bitcast(U8), ks_last[:].bitcast(U8)]
+
+        vw_win = shared.tile([P, POOL_PAGES * DV], I32, name="vw_win", offset=20480)
+        nc.sync.dma_start(
+            vw_win[:].rearrange("p (g e) -> p g e", g=POOL_PAGES),
+            v_words.rearrange("g p e b -> p g (e b)").bitcast(I32),
+        )
+
+        vs_got = shared.tile([P, N], F32, name="vs_got", offset=16384)
+        nc.vector.tensor_copy(vs_got[:], vs_win[:].indirect(offs_sb[:]))
+        vs_turned = []
+        for g in range(PAGES):
+            turned = ps.tile([P, PACK, P], F32, name="vs_turned%d" % g)
+            for t in range(PACK):
+                nc.tensor.transpose(turned[:, t, :], vs_got[:, g * PAGE + t : (g + 1) * PAGE : PACK], ident[:])
+            vs_turned.append(turned)
+
+        q_bf = sb.tile([P, PASSES, NQ, PACK], BF16, name="q_bf", align_bytes=64)
+        for o in range(PASSES):
+            nc.scalar.copy(
+                q_bf[:, o].rearrange("p (c i) j -> p c j i", i=4),
+                q_raw[:, o].rearrange("p j (c i) -> p c j i", i=4),
+            )
+        q_codes = shared.tile([P, PASSES * NQ], U32, name="q_codes", align_bytes=64, offset=5120)
+        q_scales = sb.tile([P, PASSES * NQ], U8, name="q_scales", align_bytes=64)
+        nc.vector.quantize_mx(out=q_codes[:].bitcast(FP8X4), scales=q_scales[:], in_=q_bf[:].rearrange("p o q j -> p (o q j)"))
+
+        probs = []
+        for g in range(PAGES):
+            kw_got = shared.tile([P, PAGE], U32, name="kw_got%d" % g, offset=2048 * g)
+            cols = slice(g * PAGE // 16, (g + 1) * PAGE // 16)
+            nc.vector.tensor_copy(kw_got[:], kw_win[:].bitcast(U32).indirect(offs_sb[:, cols]))
+            keys = sb.tile([P, PASSES * PACK * P * 2], U8, name="keys%d" % g, align_bytes=64)
+            nc.vector.tensor_copy(
+                keys[:].bitcast(U16).rearrange("p (o t m) -> p o m t", o=PASSES, t=PACK),
+                kw_got[:].bitcast(U16).rearrange("p (m t o) -> p o m t", t=PACK, o=PASSES),
+            )
+            prob = sb.tile([P, PACK, NQ], F32, name="prob%d" % g)
+            for half in range(2):
+                score = ps.tile([P, 2, NQ], F32, name="score%d" % (2 * g + half))
+                for u in range(2):
+                    t = 2 * half + u
+                    for o in range(PASSES):
+                        nc.tensor.matmul_mx(
+                            out=score[:, u, :],
+                            lhsT=keys[:, (o * PACK + t) * 2 * P : (o * PACK + t + 1) * 2 * P].bitcast(FP4X4),
+                            lhsT_scale=ks_planes[o][:, g * PAGE + t * P : g * PAGE + (t + 1) * P],
+                            rhs=q_codes[:, o * NQ : (o + 1) * NQ].bitcast(FP8X4),
+                            rhs_scale=q_scales[:, o * NQ : (o + 1) * NQ],
+                            start=(o == 0),
+                            stop=(o == PASSES - 1),
+                        )
+                for u in range(2):
+                    t = 2 * half + u
+                    nc.scalar.activation(prob[:, t, :], score[:, u, :], SIGMOID, bias=kb_col[:, g * PACK + t : g * PACK + t + 1])
+            probs.append(prob)
+
+        vsc_got = shared.tile([P, PAGES * DV], U8, name="vsc_got", align_bytes=64, offset=4096)
+        nc.vector.tensor_copy(vsc_got[:], vsc_win[:].bitcast(U8).indirect(voffs_sb[:]))
+        vw_got = sb.tile([P, PAGES * DV], U32, name="vw_got", align_bytes=64)
+
+        y = ps.tile([P, DV], F32, name="y", tag="early", bufs=2)
+        for g in range(PAGES):
+            w_bf = sb.tile([P, NQ, PACK], BF16, name="w_bf%d" % g, align_bytes=64)
+            nc.vector.tensor_tensor(
+                w_bf[:].rearrange("p (c i) t -> p c t i", i=4),
+                probs[g][:].rearrange("p t (c i) -> p c t i", i=4),
+                vs_turned[g][:, :, ROW:P].unsqueeze(1).to_broadcast([P, NQ // 4, PACK, 4]),
+                MULT,
+            )
+            if g == 0:
+                nc.vector.tensor_copy(vw_got[:], vw_win[:].bitcast(U32).indirect(voffs_sb[:]))
+            w_codes = sb.tile([P, NQ], U32, name="w_codes%d" % g, align_bytes=64)
+            w_scales = sb.tile([P, NQ], U8, name="w_scales%d" % g, align_bytes=64)
+            nc.vector.quantize_mx(out=w_codes[:].bitcast(FP8X4), scales=w_scales[:], in_=w_bf[:].rearrange("p q t -> p (q t)"))
+            nc.tensor.matmul_mx(
+                out=y[:],
+                lhsT=w_codes[:].bitcast(FP8X4),
+                lhsT_scale=w_scales[:],
+                rhs=vw_got[:, g * DV : (g + 1) * DV].bitcast(FP8X4),
+                rhs_scale=vsc_got[:, g * DV : (g + 1) * DV],
+                start=(g == 0),
+                stop=(g == PAGES - 1),
+            )
+        result = sb.tile([P, DV], F32, name="result")
+        nc.scalar.activation(result[:], y[:], COPY, scale=1.0 / 16.0)
+        nc.sync.dma_start(out[0], result[:])

@@ -1,7 +1,6 @@
 from contextlib import ExitStack
 
 import concourse.mybir as mybir
-from concourse.masks import make_identity
 
 F32 = mybir.dt.float32
 BF16 = mybir.dt.bfloat16
@@ -37,66 +36,54 @@ def tile_attend_pkv4_sigmoid_bias_kernel(tc, qT, k_words, k_scales, v_words, v_s
         shared = ctx.enter_context(tc.tile_pool(name="shared", bufs=1))
         ps = ctx.enter_context(tc.psum_pool(name="ps", bufs=1))
 
+        vs_fill = sb.tile([P, 8], F32, name="vs_fill")
+        nc.sync.dma_start(vs_fill[:], vs[:, 0:8])
         offs_sb = lists.tile([P, N // 16], U16, name="offs_sb")
         voffs_sb = lists.tile([P, PAGES * DV // 16], U16, name="voffs_sb")
         nc.sync.dma_start(offs_sb[:], offs)
-        nc.sync.dma_start(voffs_sb[:], voffs)
-
+        kb_win = sb.tile([P, T], F32, name="kb_win")
+        nc.sync.dma_start(kb_win[ROW:P, :], kb[0:1, :])
         q_raw = sb.tile([P, PASSES, PACK, NQ], F32, name="q_raw")
         nc.sync.dma_start(q_raw[:], qT[0].rearrange("(o p j) q -> p o j q", o=PASSES, j=PACK))
-        kw_win = sb.tile([P, T], I32, name="kw_win")
-        nc.sync.dma_start(kw_win[:], k_words[0].rearrange("p t b -> p (t b)").bitcast(I32))
-
-        kb_win = sb.tile([P, T], F32, name="kb_win")
         vs_win = shared.tile([P, T], F32, name="vs_win", offset=0)
-        vs_fill = sb.tile([P, 8], F32, name="vs_fill")
-        nc.scalar.dma_start(vs_fill[:], vs[:, 0:8])
-        nc.scalar.dma_start(kb_win[ROW:P, :], kb[0:1, :])
-        nc.scalar.dma_start(vs_win[ROW:P, :], vs[0:1, :])
-        zero = sb.tile([P, 8], F32, name="zero")
-        nc.vector.memset(zero[:], 0.0)
-        warm = sb.tile([P, 8], F32, name="warm")
-        nc.scalar.activation(warm[:], zero[:], SIGMOID)
+        nc.sync.dma_start(vs_win[ROW:P, :], vs[0:1, :])
 
-        ks_win = sb.tile([P, T // 4], I32, name="ks_win")
+        ks_win = shared.tile([P, T // 4], I32, name="ks_win", offset=21504)
         nc.vector.memset(ks_win[:], 0)
         ks_rows = k_scales.rearrange("o (u r) t -> r u o t", r=4)
         for r in range(4):
-            nc.scalar.dma_start(ks_win[r:P:SHIFT, :], ks_rows[r].bitcast(I32))
+            nc.sync.dma_start(ks_win[r:P:SHIFT, :], ks_rows[r].bitcast(I32))
+        kw_win = sb.tile([P, T], I32, name="kw_win")
+        nc.sync.dma_start(kw_win[:], k_words[0].rearrange("p t b -> p (t b)").bitcast(I32))
+        nc.sync.dma_start(voffs_sb[:], voffs)
 
+        zero = sb.tile([P, 8], F32, name="zero")
+        nc.gpsimd.memset(zero[:], 0.0)
+        warm = sb.tile([P, 8], F32, name="warm")
+        nc.scalar.activation(warm[:], zero[:], SIGMOID)
         nc.scalar.copy(vs_win[0:ROW, :], vs_fill[0:ROW, 0:1].to_broadcast([ROW, T]))
-        for h in range(2):
-            nc.vector.memset(kb_win[0:ROW, h * T // 2 : (h + 1) * T // 2], 0.0)
-
-        ks_last = sb.tile([P, N // 4], I32, name="ks_last", align_bytes=64)
-        vsc_win = sb.tile([P, POOL_PAGES * DV // 4], I32, name="vsc_win")
-        nc.vector.memset(vsc_win[:], 0)
-        ident = sb.tile([P, P], F32, name="ident")
-        make_identity(nc, ident[:])
-        vsc_rows = v_scales.rearrange("g (u r) e -> r u g e", r=4)
-        for r in range(4):
-            nc.gpsimd.dma_start(vsc_win[r:P:32, :].rearrange("p (g e) -> p g e", g=POOL_PAGES), vsc_rows[r].bitcast(I32))
+        nc.vector.memset(kb_win[0:ROW, :], 0.0)
 
         kb_got = sb.tile([P, N], F32, name="kb_got")
         nc.vector.tensor_copy(kb_got[:], kb_win[:].indirect(offs_sb[:]))
-        kb_col = sb.tile([P, PAGES * PACK], F32, name="kb_col")
+        kb_col = sb.tile([P, PAGES, 8], F32, name="kb_col")
         for g in range(PAGES):
-            kb_turned = ps.tile([P, PACK, P], F32, name="kb_turned", tag="early", bufs=2)
-            for t in range(PACK):
-                nc.tensor.transpose(kb_turned[:, t, :], kb_got[:, g * PAGE + t : (g + 1) * PAGE : PACK], ident[:])
-            nc.scalar.copy(kb_col[:, g * PACK : (g + 1) * PACK], kb_turned[:, :, ROW])
+            nc.sync.dma_start(kb_col[:, g, 0:PACK], kb_got[ROW:P, g * PAGE : (g + 1) * PAGE])
 
-        ks_got = shared.tile([P, N], U8, name="ks_got", offset=20480 - 512)
+        ks_got = shared.tile([P, N], U8, name="ks_got", offset=16384)
         nc.vector.tensor_copy(ks_got[:], ks_win[:].bitcast(U8).indirect(offs_sb[:]))
+        vsc_win = shared.tile([P, POOL_PAGES * DV // 4], I32, name="vsc_win", offset=21504)
+        nc.vector.memset(vsc_win[:], 0)
         ks_first = sb.tile([P, N // 4], I32, name="ks_first", align_bytes=64)
         nc.vector.tensor_copy(
-            ks_first[:].bitcast(U8).rearrange("p (g t m) -> p g m t", g=PAGES, t=PACK),
-            ks_got[:].rearrange("p (g m t) -> p g m t", g=PAGES, t=PACK),
+            ks_first[:].bitcast(U8).rearrange("p (g t m) -> p g t m", g=PAGES, t=PACK),
+            ks_got[:].rearrange("p (g m t) -> p g t m", g=PAGES, t=PACK),
         )
-        nc.sync.dma_start(ks_last[0 : P - SHIFT, :], ks_first[SHIFT:P, :])
+        ks_last = sb.tile([P, N // 4], I32, name="ks_last", align_bytes=64)
+        nc.scalar.dma_start(ks_last[0 : P - SHIFT, :], ks_first[SHIFT:P, :])
         ks_planes = [ks_first[:].bitcast(U8), ks_last[:].bitcast(U8)]
 
-        vw_win = shared.tile([P, POOL_PAGES * DV], I32, name="vw_win", offset=20480)
+        vw_win = shared.tile([P, POOL_PAGES * DV], I32, name="vw_win", offset=25600)
         nc.sync.dma_start(
             vw_win[:].rearrange("p (g e) -> p g e", g=POOL_PAGES),
             v_words.rearrange("g p e b -> p g (e b)").bitcast(I32),
@@ -104,12 +91,13 @@ def tile_attend_pkv4_sigmoid_bias_kernel(tc, qT, k_words, k_scales, v_words, v_s
 
         vs_got = shared.tile([P, N], F32, name="vs_got", offset=16384)
         nc.vector.tensor_copy(vs_got[:], vs_win[:].indirect(offs_sb[:]))
-        vs_turned = []
+        vs_col = sb.tile([P, PAGES, 8], F32, name="vs_col")
         for g in range(PAGES):
-            turned = ps.tile([P, PACK, P], F32, name="vs_turned%d" % g)
-            for t in range(PACK):
-                nc.tensor.transpose(turned[:, t, :], vs_got[:, g * PAGE + t : (g + 1) * PAGE : PACK], ident[:])
-            vs_turned.append(turned)
+            nc.scalar.dma_start(vs_col[:, g, 0:PACK], vs_got[ROW:P, g * PAGE : (g + 1) * PAGE])
+
+        vsc_rows = v_scales.rearrange("g (u r) e -> r u g e", r=4)
+        for r in range(4):
+            nc.sync.dma_start(vsc_win[r:P:32, :].rearrange("p (g e) -> p g e", g=POOL_PAGES), vsc_rows[r].bitcast(I32))
 
         q_bf = sb.tile([P, PASSES, NQ, PACK], BF16, name="q_bf", align_bytes=64)
         for o in range(PASSES):
@@ -119,27 +107,32 @@ def tile_attend_pkv4_sigmoid_bias_kernel(tc, qT, k_words, k_scales, v_words, v_s
             )
         q_codes = shared.tile([P, PASSES * NQ], U32, name="q_codes", align_bytes=64, offset=5120)
         q_scales = sb.tile([P, PASSES * NQ], U8, name="q_scales", align_bytes=64)
+
         nc.vector.quantize_mx(out=q_codes[:].bitcast(FP8X4), scales=q_scales[:], in_=q_bf[:].rearrange("p o q j -> p (o q j)"))
 
-        probs = []
+        kw_pages = []
         for g in range(PAGES):
             kw_got = shared.tile([P, PAGE], U32, name="kw_got%d" % g, offset=2048 * g)
             cols = slice(g * PAGE // 16, (g + 1) * PAGE // 16)
             nc.vector.tensor_copy(kw_got[:], kw_win[:].bitcast(U32).indirect(offs_sb[:, cols]))
-            keys = sb.tile([P, PASSES * PACK * P * 2], U8, name="keys%d" % g, align_bytes=64)
-            nc.vector.tensor_copy(
-                keys[:].bitcast(U16).rearrange("p (o t m) -> p o m t", o=PASSES, t=PACK),
-                kw_got[:].bitcast(U16).rearrange("p (m t o) -> p o m t", t=PACK, o=PASSES),
-            )
+            kw_pages.append(kw_got)
+        probs = []
+        for g in range(PAGES):
+            kw_got = kw_pages[g]
             prob = sb.tile([P, PACK, NQ], F32, name="prob%d" % g)
             for half in range(2):
+                keys = sb.tile([P, PASSES * 2 * P * 2], U8, name="keys%d" % (2 * g + half), align_bytes=64)
+                nc.vector.tensor_copy(
+                    keys[:].bitcast(U16).rearrange("p (o u m) -> p o m u", o=PASSES, u=2),
+                    kw_got[:].bitcast(U16).rearrange("p (m t o) -> p o m t", t=PACK, o=PASSES)[:, :, :, 2 * half : 2 * half + 2],
+                )
                 score = ps.tile([P, 2, NQ], F32, name="score%d" % (2 * g + half))
                 for u in range(2):
                     t = 2 * half + u
                     for o in range(PASSES):
                         nc.tensor.matmul_mx(
                             out=score[:, u, :],
-                            lhsT=keys[:, (o * PACK + t) * 2 * P : (o * PACK + t + 1) * 2 * P].bitcast(FP4X4),
+                            lhsT=keys[:, (o * 2 + u) * 2 * P : (o * 2 + u + 1) * 2 * P].bitcast(FP4X4),
                             lhsT_scale=ks_planes[o][:, g * PAGE + t * P : g * PAGE + (t + 1) * P],
                             rhs=q_codes[:, o * NQ : (o + 1) * NQ].bitcast(FP8X4),
                             rhs_scale=q_scales[:, o * NQ : (o + 1) * NQ],
@@ -148,25 +141,24 @@ def tile_attend_pkv4_sigmoid_bias_kernel(tc, qT, k_words, k_scales, v_words, v_s
                         )
                 for u in range(2):
                     t = 2 * half + u
-                    nc.scalar.activation(prob[:, t, :], score[:, u, :], SIGMOID, bias=kb_col[:, g * PACK + t : g * PACK + t + 1])
+                    nc.scalar.activation(prob[:, t, :], score[:, u, :], SIGMOID, bias=kb_col[:, g, t : t + 1])
             probs.append(prob)
 
+        vw_got = sb.tile([P, PAGES * DV], U32, name="vw_got", align_bytes=64)
+        nc.vector.tensor_copy(vw_got[:], vw_win[:].bitcast(U32).indirect(voffs_sb[:]))
         vsc_got = shared.tile([P, PAGES * DV], U8, name="vsc_got", align_bytes=64, offset=4096)
         nc.vector.tensor_copy(vsc_got[:], vsc_win[:].bitcast(U8).indirect(voffs_sb[:]))
-        vw_got = sb.tile([P, PAGES * DV], U32, name="vw_got", align_bytes=64)
 
-        y = ps.tile([P, DV], F32, name="y", tag="early", bufs=2)
+        y = ps.tile([P, DV], F32, name="y")
         for g in range(PAGES):
-            w_bf = sb.tile([P, NQ, PACK], BF16, name="w_bf%d" % g, align_bytes=64)
+            w_bf = shared.tile([P, NQ, PACK], BF16, name="w_bf%d" % g, align_bytes=64, offset=(25600, 22016)[g])
             nc.vector.tensor_tensor(
                 w_bf[:].rearrange("p (c i) t -> p c t i", i=4),
                 probs[g][:].rearrange("p t (c i) -> p c t i", i=4),
-                vs_turned[g][:, :, ROW:P].unsqueeze(1).to_broadcast([P, NQ // 4, PACK, 4]),
+                vs_col[:, g, 0:PACK].unsqueeze(1).unsqueeze(3).to_broadcast([P, NQ // 4, PACK, 4]),
                 MULT,
             )
-            if g == 0:
-                nc.vector.tensor_copy(vw_got[:], vw_win[:].bitcast(U32).indirect(voffs_sb[:]))
-            w_codes = sb.tile([P, NQ], U32, name="w_codes%d" % g, align_bytes=64)
+            w_codes = shared.tile([P, NQ], U32, name="w_codes%d" % g, align_bytes=64, offset=(21504, 23040)[g])
             w_scales = sb.tile([P, NQ], U8, name="w_scales%d" % g, align_bytes=64)
             nc.vector.quantize_mx(out=w_codes[:].bitcast(FP8X4), scales=w_scales[:], in_=w_bf[:].rearrange("p q t -> p (q t)"))
             nc.tensor.matmul_mx(

@@ -43,16 +43,16 @@ def tile_attend_pkv4_sigmoid_bias_kernel(tc, qT, k_words, k_scales, v_words, v_s
         nc.sync.dma_start(offs_sb[:], offs)
         kb_win = sb.tile([P, T], F32, name="kb_win")
         nc.sync.dma_start(kb_win[ROW:P, :], kb[0:1, :])
-        q_raw = sb.tile([P, PASSES, PACK, NQ], F32, name="q_raw")
-        nc.sync.dma_start(q_raw[:], qT[0].rearrange("(o p j) q -> p o j q", o=PASSES, j=PACK))
-        vs_win = shared.tile([P, T], F32, name="vs_win", offset=0)
-        nc.sync.dma_start(vs_win[ROW:P, :], vs[0:1, :])
 
         ks_win = shared.tile([P, T // 4], I32, name="ks_win", offset=21504)
         nc.vector.memset(ks_win[:], 0)
         ks_rows = k_scales.rearrange("o (u r) t -> r u o t", r=4)
         for r in range(4):
             nc.sync.dma_start(ks_win[r:P:SHIFT, :], ks_rows[r].bitcast(I32))
+        q_raw = sb.tile([P, PASSES, PACK, NQ], F32, name="q_raw")
+        nc.sync.dma_start(q_raw[:], qT[0].rearrange("(o p j) q -> p o j q", o=PASSES, j=PACK))
+        vs_win = shared.tile([P, T], F32, name="vs_win", offset=0)
+        nc.sync.dma_start(vs_win[ROW:P, :], vs[0:1, :])
         kw_win = sb.tile([P, T], I32, name="kw_win")
         nc.sync.dma_start(kw_win[:], k_words[0].rearrange("p t b -> p (t b)").bitcast(I32))
         nc.sync.dma_start(voffs_sb[:], voffs)
@@ -61,8 +61,11 @@ def tile_attend_pkv4_sigmoid_bias_kernel(tc, qT, k_words, k_scales, v_words, v_s
         nc.gpsimd.memset(zero[:], 0.0)
         warm = sb.tile([P, 8], F32, name="warm")
         nc.scalar.activation(warm[:], zero[:], SIGMOID)
-        nc.scalar.copy(vs_win[0:ROW, :], vs_fill[0:ROW, 0:1].to_broadcast([ROW, T]))
-        nc.vector.memset(kb_win[0:ROW, :], 0.0)
+        nc.scalar.copy(
+            vs_win[0:ROW, :].rearrange("p (a b) -> p a b", b=8),
+            vs_fill[0:ROW, :].unsqueeze(1).to_broadcast([ROW, T // 8, 8]),
+        )
+        nc.vector.memset(kb_win[0:ROW, :].bitcast(I32), 0)
 
         kb_got = sb.tile([P, N], F32, name="kb_got")
         nc.vector.tensor_copy(kb_got[:], kb_win[:].indirect(offs_sb[:]))

@@ -36,8 +36,8 @@ def tile_attend_pkv4_sigmoid_bias_kernel(tc, qT, k_words, k_scales, v_words, v_s
         shared = ctx.enter_context(tc.tile_pool(name="shared", bufs=1))
         ps = ctx.enter_context(tc.psum_pool(name="ps", bufs=1))
 
-        vs_fill = sb.tile([P, 8], F32, name="vs_fill")
-        nc.sync.dma_start(vs_fill[:], vs[:, 0:8])
+        vs_own = sb.tile([P, POOL_PAGES, 8], F32, name="vs_own")
+        nc.scalar.dma_start(vs_own[:, :, 0:PACK], vs[0].rearrange("(u p t) -> p u t", u=POOL_PAGES, t=PACK))
         offs_sb = lists.tile([P, N // 16], U16, name="offs_sb")
         voffs_sb = lists.tile([P, PAGES * DV // 16], U16, name="voffs_sb")
         nc.sync.dma_start(offs_sb[:], offs)
@@ -49,21 +49,25 @@ def tile_attend_pkv4_sigmoid_bias_kernel(tc, qT, k_words, k_scales, v_words, v_s
         ks_rows = k_scales.rearrange("o (u r) t -> r u o t", r=4)
         for r in range(4):
             nc.sync.dma_start(ks_win[r:P:SHIFT, :], ks_rows[r].bitcast(I32))
+        nc.sync.dma_start(voffs_sb[:], voffs)
         q_raw = sb.tile([P, PASSES, PACK, NQ], F32, name="q_raw")
         nc.sync.dma_start(q_raw[:], qT[0].rearrange("(o p j) q -> p o j q", o=PASSES, j=PACK))
-        vs_win = shared.tile([P, T], F32, name="vs_win", offset=0)
-        nc.sync.dma_start(vs_win[ROW:P, :], vs[0:1, :])
         kw_win = sb.tile([P, T], I32, name="kw_win")
         nc.sync.dma_start(kw_win[:], k_words[0].rearrange("p t b -> p (t b)").bitcast(I32))
-        nc.sync.dma_start(voffs_sb[:], voffs)
 
         zero = sb.tile([P, 8], F32, name="zero")
         nc.gpsimd.memset(zero[:], 0.0)
         warm = sb.tile([P, 8], F32, name="warm")
         nc.scalar.activation(warm[:], zero[:], SIGMOID)
+        vs_run = sb.tile([P, POOL_PAGES * PACK, 8], F32, name="vs_run")
         nc.scalar.copy(
-            vs_win[0:ROW, :].rearrange("p (a b) -> p a b", b=8),
-            vs_fill[0:ROW, :].unsqueeze(1).to_broadcast([ROW, T // 8, 8]),
+            vs_run[:].rearrange("p (u t) i -> p u t i", t=PACK),
+            vs_own[:, :, 0:PACK].unsqueeze(3).to_broadcast([P, POOL_PAGES, PACK, 8]),
+        )
+        vs_win = shared.tile([P, T], F32, name="vs_win", offset=0)
+        nc.scalar.copy(
+            vs_win[:].rearrange("p (a c i) -> p a c i", a=POOL_PAGES * PACK, i=8),
+            vs_run[:].unsqueeze(2).to_broadcast([P, POOL_PAGES * PACK, NQ // 8, 8]),
         )
         nc.vector.memset(kb_win[0:ROW, :].bitcast(I32), 0)
 
@@ -94,9 +98,6 @@ def tile_attend_pkv4_sigmoid_bias_kernel(tc, qT, k_words, k_scales, v_words, v_s
 
         vs_got = shared.tile([P, N], F32, name="vs_got", offset=16384)
         nc.vector.tensor_copy(vs_got[:], vs_win[:].indirect(offs_sb[:]))
-        vs_col = sb.tile([P, PAGES, 8], F32, name="vs_col")
-        for g in range(PAGES):
-            nc.scalar.dma_start(vs_col[:, g, 0:PACK], vs_got[ROW:P, g * PAGE : (g + 1) * PAGE])
 
         vsc_rows = v_scales.rearrange("g (u r) e -> r u g e", r=4)
         for r in range(4):
@@ -158,7 +159,7 @@ def tile_attend_pkv4_sigmoid_bias_kernel(tc, qT, k_words, k_scales, v_words, v_s
             nc.vector.tensor_tensor(
                 w_bf[:].rearrange("p (c i) t -> p c t i", i=4),
                 probs[g][:].rearrange("p t (c i) -> p c t i", i=4),
-                vs_col[:, g, 0:PACK].unsqueeze(1).unsqueeze(3).to_broadcast([P, NQ // 4, PACK, 4]),
+                vs_got[:, g * PAGE : (g + 1) * PAGE].rearrange("p (t c i) -> p c t i", t=PACK, i=4),
                 MULT,
             )
             w_codes = shared.tile([P, NQ], U32, name="w_codes%d" % g, align_bytes=64, offset=(21504, 23040)[g])

@@ -43,41 +43,33 @@ def tile_attend_pkv4_sigmoid_bias_kernel(tc, qT, k_words, k_scales, v_words, v_s
         nc.sync.dma_start(offs_sb[:], offs)
         kb_win = sb.tile([P, T], F32, name="kb_win")
         nc.sync.dma_start(kb_win[ROW:P, :], kb[0:1, :])
+        q_raw = sb.tile([P, PASSES, PACK, NQ], F32, name="q_raw")
+        nc.sync.dma_start(q_raw[:], qT[0].rearrange("(o p j) q -> p o j q", o=PASSES, j=PACK))
 
         ks_win = shared.tile([P, T // 4], I32, name="ks_win", offset=21504)
         nc.vector.memset(ks_win[:], 0)
         ks_rows = k_scales.rearrange("o (u r) t -> r u o t", r=4)
         for r in range(4):
             nc.sync.dma_start(ks_win[r:P:SHIFT, :], ks_rows[r].bitcast(I32))
-        nc.sync.dma_start(voffs_sb[:], voffs)
-        q_raw = sb.tile([P, PASSES, PACK, NQ], F32, name="q_raw")
-        nc.sync.dma_start(q_raw[:], qT[0].rearrange("(o p j) q -> p o j q", o=PASSES, j=PACK))
         kw_win = sb.tile([P, T], I32, name="kw_win")
         nc.sync.dma_start(kw_win[:], k_words[0].rearrange("p t b -> p (t b)").bitcast(I32))
+        nc.sync.dma_start(voffs_sb[:], voffs)
 
         zero = sb.tile([P, 8], F32, name="zero")
         nc.gpsimd.memset(zero[:], 0.0)
         warm = sb.tile([P, 8], F32, name="warm")
         nc.scalar.activation(warm[:], zero[:], SIGMOID)
-        vs_run = sb.tile([P, POOL_PAGES * PACK, 8], F32, name="vs_run")
-        nc.scalar.copy(
-            vs_run[:].rearrange("p (u t) i -> p u t i", t=PACK),
-            vs_own[:, :, 0:PACK].unsqueeze(3).to_broadcast([P, POOL_PAGES, PACK, 8]),
-        )
         vs_win = shared.tile([P, T], F32, name="vs_win", offset=0)
         nc.scalar.copy(
-            vs_win[:].rearrange("p (a c i) -> p a c i", a=POOL_PAGES * PACK, i=8),
-            vs_run[:].unsqueeze(2).to_broadcast([P, POOL_PAGES * PACK, NQ // 8, 8]),
+            vs_win[:].rearrange("p (u q t) -> p u q t", u=POOL_PAGES, t=PACK),
+            vs_own[:, :, 0:PACK].unsqueeze(2).to_broadcast([P, POOL_PAGES, NQ, PACK]),
         )
         nc.vector.memset(kb_win[0:ROW, :].bitcast(I32), 0)
 
         kb_got = sb.tile([P, N], F32, name="kb_got")
         nc.vector.tensor_copy(kb_got[:], kb_win[:].indirect(offs_sb[:]))
-        kb_col = sb.tile([P, PAGES, 8], F32, name="kb_col")
-        for g in range(PAGES):
-            nc.sync.dma_start(kb_col[:, g, 0:PACK], kb_got[ROW:P, g * PAGE : (g + 1) * PAGE])
 
-        ks_got = shared.tile([P, N], U8, name="ks_got", offset=16384)
+        ks_got = shared.tile([P, N], U8, name="ks_got", offset=36864)
         nc.vector.tensor_copy(ks_got[:], ks_win[:].bitcast(U8).indirect(offs_sb[:]))
         vsc_win = shared.tile([P, POOL_PAGES * DV // 4], I32, name="vsc_win", offset=21504)
         nc.vector.memset(vsc_win[:], 0)
@@ -88,31 +80,33 @@ def tile_attend_pkv4_sigmoid_bias_kernel(tc, qT, k_words, k_scales, v_words, v_s
         )
         ks_last = sb.tile([P, N // 4], I32, name="ks_last", align_bytes=64)
         nc.scalar.dma_start(ks_last[0 : P - SHIFT, :], ks_first[SHIFT:P, :])
+        kb_col = shared.tile([P, PAGES, 8], F32, name="kb_col", offset=36864 + 256)
+        for g in range(PAGES):
+            nc.scalar.dma_start(kb_col[:, g, 0:PACK], kb_got[ROW:P, g * PAGE : (g + 1) * PAGE])
         ks_planes = [ks_first[:].bitcast(U8), ks_last[:].bitcast(U8)]
 
-        vw_win = shared.tile([P, POOL_PAGES * DV], I32, name="vw_win", offset=25600)
+        vw_win = shared.tile([P, POOL_PAGES * DV], I32, name="vw_win", offset=40960)
         nc.sync.dma_start(
             vw_win[:].rearrange("p (g e) -> p g e", g=POOL_PAGES),
             v_words.rearrange("g p e b -> p g (e b)").bitcast(I32),
         )
 
-        vs_got = shared.tile([P, N], F32, name="vs_got", offset=16384)
+        q_bf = shared.tile([P, PASSES, NQ, PACK], BF16, name="q_bf", align_bytes=64, offset=36864 + 512)
+        nc.vector.tensor_copy(
+            q_bf[:].rearrange("p o (c i) j -> p o c j i", i=4),
+            q_raw[:].rearrange("p o j (c i) -> p o c j i", i=4),
+        )
+        q_codes = sb.tile([P, PASSES * NQ], U32, name="q_codes", align_bytes=64)
+        q_scales = sb.tile([P, PASSES * NQ], U8, name="q_scales", align_bytes=64)
+
+        nc.vector.quantize_mx(out=q_codes[:].bitcast(FP8X4), scales=q_scales[:], in_=q_bf[:].rearrange("p o q j -> p (o q j)"))
+
+        vs_got = shared.tile([P, N], F32, name="vs_got", offset=36864 + 256 - 4096)
         nc.vector.tensor_copy(vs_got[:], vs_win[:].indirect(offs_sb[:]))
 
         vsc_rows = v_scales.rearrange("g (u r) e -> r u g e", r=4)
         for r in range(4):
             nc.sync.dma_start(vsc_win[r:P:32, :].rearrange("p (g e) -> p g e", g=POOL_PAGES), vsc_rows[r].bitcast(I32))
-
-        q_bf = sb.tile([P, PASSES, NQ, PACK], BF16, name="q_bf", align_bytes=64)
-        for o in range(PASSES):
-            nc.scalar.copy(
-                q_bf[:, o].rearrange("p (c i) j -> p c j i", i=4),
-                q_raw[:, o].rearrange("p j (c i) -> p c j i", i=4),
-            )
-        q_codes = shared.tile([P, PASSES * NQ], U32, name="q_codes", align_bytes=64, offset=5120)
-        q_scales = sb.tile([P, PASSES * NQ], U8, name="q_scales", align_bytes=64)
-
-        nc.vector.quantize_mx(out=q_codes[:].bitcast(FP8X4), scales=q_scales[:], in_=q_bf[:].rearrange("p o q j -> p (o q j)"))
 
         kw_pages = []
         for g in range(PAGES):
@@ -155,11 +149,11 @@ def tile_attend_pkv4_sigmoid_bias_kernel(tc, qT, k_words, k_scales, v_words, v_s
 
         y = ps.tile([P, DV], F32, name="y")
         for g in range(PAGES):
-            w_bf = shared.tile([P, NQ, PACK], BF16, name="w_bf%d" % g, align_bytes=64, offset=(25600, 22016)[g])
+            w_bf = shared.tile([P, NQ, PACK], BF16, name="w_bf%d" % g, align_bytes=64, offset=(40960, 22016)[g])
             nc.vector.tensor_tensor(
                 w_bf[:].rearrange("p (c i) t -> p c t i", i=4),
                 probs[g][:].rearrange("p t (c i) -> p c t i", i=4),
-                vs_got[:, g * PAGE : (g + 1) * PAGE].rearrange("p (t c i) -> p c t i", t=PACK, i=4),
+                vs_got[:, g * PAGE : (g + 1) * PAGE].rearrange("p (c i t) -> p c t i", t=PACK, i=4),
                 MULT,
             )
             w_codes = shared.tile([P, NQ], U32, name="w_codes%d" % g, align_bytes=64, offset=(21504, 23040)[g])

@@ -36,24 +36,28 @@ def tile_attend_pkv4_sigmoid_bias_kernel(tc, qT, k_words, k_scales, v_words, v_s
         shared = ctx.enter_context(tc.tile_pool(name="shared", bufs=1))
         ps = ctx.enter_context(tc.psum_pool(name="ps", bufs=1))
 
-        vs_own = sb.tile([P, POOL_PAGES, 8], F32, name="vs_own")
-        nc.scalar.dma_start(vs_own[:, :, 0:PACK], vs[0].rearrange("(u p t) -> p u t", u=POOL_PAGES, t=PACK))
         offs_sb = lists.tile([P, N // 16], U16, name="offs_sb")
         voffs_sb = lists.tile([P, PAGES * DV // 16], U16, name="voffs_sb")
         nc.sync.dma_start(offs_sb[:], offs)
+        vs_own = sb.tile([P, POOL_PAGES, 8], F32, name="vs_own")
+        nc.scalar.dma_start(vs_own[:, :, 0:PACK], vs[0].rearrange("(u p t) -> p u t", u=POOL_PAGES, t=PACK))
         kb_win = sb.tile([P, T], F32, name="kb_win")
         nc.sync.dma_start(kb_win[ROW:P, :], kb[0:1, :])
-        q_raw = sb.tile([P, PASSES, PACK, NQ], F32, name="q_raw")
-        nc.sync.dma_start(q_raw[:], qT[0].rearrange("(o p j) q -> p o j q", o=PASSES, j=PACK))
 
         ks_win = shared.tile([P, T // 4], I32, name="ks_win", offset=21504)
         nc.vector.memset(ks_win[:], 0)
         ks_rows = k_scales.rearrange("o (u r) t -> r u o t", r=4)
         for r in range(4):
             nc.sync.dma_start(ks_win[r:P:SHIFT, :], ks_rows[r].bitcast(I32))
+        nc.sync.dma_start(voffs_sb[:], voffs)
         kw_win = sb.tile([P, T], I32, name="kw_win")
         nc.sync.dma_start(kw_win[:], k_words[0].rearrange("p t b -> p (t b)").bitcast(I32))
-        nc.sync.dma_start(voffs_sb[:], voffs)
+        q_rows = qT[0].rearrange("(o p j) q -> o p j q", o=PASSES, j=PACK)
+        q_raws = []
+        for o in range(PASSES):
+            q_raw = sb.tile([P, PACK, NQ], F32, name="q_raw%d" % o)
+            nc.sync.dma_start(q_raw[:], q_rows[o])
+            q_raws.append(q_raw)
 
         zero = sb.tile([P, 8], F32, name="zero")
         nc.gpsimd.memset(zero[:], 0.0)
@@ -91,16 +95,6 @@ def tile_attend_pkv4_sigmoid_bias_kernel(tc, qT, k_words, k_scales, v_words, v_s
             v_words.rearrange("g p e b -> p g (e b)").bitcast(I32),
         )
 
-        q_bf = shared.tile([P, PASSES, NQ, PACK], BF16, name="q_bf", align_bytes=64, offset=36864 + 512)
-        nc.vector.tensor_copy(
-            q_bf[:].rearrange("p o (c i) j -> p o c j i", i=4),
-            q_raw[:].rearrange("p o j (c i) -> p o c j i", i=4),
-        )
-        q_codes = sb.tile([P, PASSES * NQ], U32, name="q_codes", align_bytes=64)
-        q_scales = sb.tile([P, PASSES * NQ], U8, name="q_scales", align_bytes=64)
-
-        nc.vector.quantize_mx(out=q_codes[:].bitcast(FP8X4), scales=q_scales[:], in_=q_bf[:].rearrange("p o q j -> p (o q j)"))
-
         vs_got = shared.tile([P, N], F32, name="vs_got", offset=36864 + 256 - 4096)
         nc.vector.tensor_copy(vs_got[:], vs_win[:].indirect(offs_sb[:]))
 
@@ -108,18 +102,28 @@ def tile_attend_pkv4_sigmoid_bias_kernel(tc, qT, k_words, k_scales, v_words, v_s
         for r in range(4):
             nc.sync.dma_start(vsc_win[r:P:32, :].rearrange("p (g e) -> p g e", g=POOL_PAGES), vsc_rows[r].bitcast(I32))
 
+        q_bf = shared.tile([P, PASSES, NQ, PACK], BF16, name="q_bf", align_bytes=64, offset=49152)
+        for o in range(PASSES):
+            nc.scalar.copy(
+                q_bf[:, o].rearrange("p (c i) j -> p c j i", i=4),
+                q_raws[o][:].rearrange("p j (c i) -> p c j i", i=4),
+            )
+        q_codes = sb.tile([P, PASSES * NQ], U32, name="q_codes", align_bytes=64)
+        q_scales = sb.tile([P, PASSES * NQ], U8, name="q_scales", align_bytes=64)
+
         kw_pages = []
         for g in range(PAGES):
             kw_got = shared.tile([P, PAGE], U32, name="kw_got%d" % g, offset=2048 * g)
             cols = slice(g * PAGE // 16, (g + 1) * PAGE // 16)
             nc.vector.tensor_copy(kw_got[:], kw_win[:].bitcast(U32).indirect(offs_sb[:, cols]))
             kw_pages.append(kw_got)
+        nc.vector.quantize_mx(out=q_codes[:].bitcast(FP8X4), scales=q_scales[:], in_=q_bf[:].rearrange("p o q j -> p (o q j)"))
         probs = []
         for g in range(PAGES):
             kw_got = kw_pages[g]
             prob = sb.tile([P, PACK, NQ], F32, name="prob%d" % g)
             for half in range(2):
-                keys = sb.tile([P, PASSES * 2 * P * 2], U8, name="keys%d" % (2 * g + half), align_bytes=64)
+                keys = shared.tile([P, PASSES * 2 * P * 2], U8, name="keys%d" % (2 * g + half), align_bytes=64, offset=51200 - 2048 * g + 1024 * half)
                 nc.vector.tensor_copy(
                     keys[:].bitcast(U16).rearrange("p (o u m) -> p o m u", o=PASSES, u=2),
                     kw_got[:].bitcast(U16).rearrange("p (m t o) -> p o m t", t=PACK, o=PASSES)[:, :, :, 2 * half : 2 * half + 2],

@@ -1,6 +1,7 @@
 from contextlib import ExitStack
 
 import concourse.mybir as mybir
+from concourse.masks import make_identity
 
 F32 = mybir.dt.float32
 BF16 = mybir.dt.bfloat16
@@ -39,13 +40,14 @@ def tile_attend_pkv4_sigmoid_bias_kernel(tc, qT, k_words, k_scales, v_words, v_s
         offs_sb = lists.tile([P, N // 16], U16, name="offs_sb")
         voffs_sb = lists.tile([P, PAGES * DV // 16], U16, name="voffs_sb")
         nc.sync.dma_start(offs_sb[:], offs)
-        vs_own = sb.tile([P, POOL_PAGES, 8], F32, name="vs_own")
-        nc.scalar.dma_start(vs_own[:, :, 0:PACK], vs[0].rearrange("(u p t) -> p u t", u=POOL_PAGES, t=PACK))
+        vs_pages = sb.tile([P, PAGE], F32, name="vs_pages")
+        nc.scalar.dma_start(vs_pages[P - POOL_PAGES : P, :], vs[0].rearrange("(u x) -> u x", u=POOL_PAGES))
         kb_win = sb.tile([P, T], F32, name="kb_win")
         nc.sync.dma_start(kb_win[ROW:P, :], kb[0:1, :])
 
         ks_win = shared.tile([P, T // 4], I32, name="ks_win", offset=21504)
         nc.vector.memset(ks_win[:], 0)
+        nc.vector.memset(vs_pages[0 : P - POOL_PAGES, :].bitcast(I32), 0)
         ks_rows = k_scales.rearrange("o (u r) t -> r u o t", r=4)
         for r in range(4):
             nc.sync.dma_start(ks_win[r:P:SHIFT, :], ks_rows[r].bitcast(I32))
@@ -59,15 +61,18 @@ def tile_attend_pkv4_sigmoid_bias_kernel(tc, qT, k_words, k_scales, v_words, v_s
             nc.sync.dma_start(q_raw[:], q_rows[o])
             q_raws.append(q_raw)
 
-        zero = sb.tile([P, 8], F32, name="zero")
-        nc.gpsimd.memset(zero[:], 0.0)
+        ident = sb.tile([P, P], F32, name="ident")
+        make_identity(nc, ident[:])
         warm = sb.tile([P, 8], F32, name="warm")
-        nc.scalar.activation(warm[:], zero[:], SIGMOID)
+        nc.scalar.activation(warm[:], ident[:, 0:8], SIGMOID)
         vs_win = shared.tile([P, T], F32, name="vs_win", offset=0)
-        nc.scalar.copy(
-            vs_win[:].rearrange("p (u q t) -> p u q t", u=POOL_PAGES, t=PACK),
-            vs_own[:, :, 0:PACK].unsqueeze(2).to_broadcast([P, POOL_PAGES, NQ, PACK]),
-        )
+        for t in range(PACK):
+            turned = ps.tile([P, P], F32, name="turned%d" % t, tag="bank%d" % t)
+            nc.tensor.transpose(turned[:], vs_pages[:, t:PAGE:PACK], ident[:])
+            nc.scalar.copy(
+                vs_win[:].rearrange("p (u t q) -> p t u q", u=POOL_PAGES, t=PACK)[:, t],
+                turned[:, P - POOL_PAGES : P].unsqueeze(2).to_broadcast([P, POOL_PAGES, NQ]),
+            )
         nc.vector.memset(kb_win[0:ROW, :].bitcast(I32), 0)
 
         kb_got = sb.tile([P, N], F32, name="kb_got")
@@ -128,7 +133,7 @@ def tile_attend_pkv4_sigmoid_bias_kernel(tc, qT, k_words, k_scales, v_words, v_s
                     keys[:].bitcast(U16).rearrange("p (o u m) -> p o m u", o=PASSES, u=2),
                     kw_got[:].bitcast(U16).rearrange("p (m t o) -> p o m t", t=PACK, o=PASSES)[:, :, :, 2 * half : 2 * half + 2],
                 )
-                score = ps.tile([P, 2, NQ], F32, name="score%d" % (2 * g + half))
+                score = ps.tile([P, 2, NQ], F32, name="score%d" % (2 * g + half), tag="bank%d" % (2 * g + half))
                 for u in range(2):
                     t = 2 * half + u
                     for o in range(PASSES):
@@ -157,7 +162,7 @@ def tile_attend_pkv4_sigmoid_bias_kernel(tc, qT, k_words, k_scales, v_words, v_s
             nc.vector.tensor_tensor(
                 w_bf[:].rearrange("p (c i) t -> p c t i", i=4),
                 probs[g][:].rearrange("p t (c i) -> p c t i", i=4),
-                vs_got[:, g * PAGE : (g + 1) * PAGE].rearrange("p (c i t) -> p c t i", t=PACK, i=4),
+                vs_got[:, g * PAGE : (g + 1) * PAGE].rearrange("p (t c i) -> p c t i", t=PACK, i=4),
                 MULT,
             )
             w_codes = shared.tile([P, NQ], U32, name="w_codes%d" % g, align_bytes=64, offset=(21504, 23040)[g])

@@ -107,7 +107,7 @@ def tile_attend_pkv4_sigmoid_bias_kernel(tc, qT, k_words, k_scales, v_words, v_s
         for r in range(4):
             nc.sync.dma_start(vsc_win[r:P:32, :].rearrange("p (g e) -> p g e", g=POOL_PAGES), vsc_rows[r].bitcast(I32))
 
-        q_bf = shared.tile([P, PASSES, NQ, PACK], BF16, name="q_bf", align_bytes=64, offset=49152)
+        q_bf = shared.tile([P, PASSES, NQ, PACK], BF16, name="q_bf", align_bytes=64, offset=50176)
         for o in range(PASSES):
             nc.scalar.copy(
                 q_bf[:, o].rearrange("p (c i) j -> p c j i", i=4),
@@ -128,7 +128,7 @@ def tile_attend_pkv4_sigmoid_bias_kernel(tc, qT, k_words, k_scales, v_words, v_s
             kw_got = kw_pages[g]
             prob = sb.tile([P, PACK, NQ], F32, name="prob%d" % g)
             for half in range(2):
-                keys = shared.tile([P, PASSES * 2 * P * 2], U8, name="keys%d" % (2 * g + half), align_bytes=64, offset=51200 - 2048 * g + 1024 * half)
+                keys = shared.tile([P, PASSES * 2 * P * 2], U8, name="keys%d" % (2 * g + half), align_bytes=64, offset=49408 + 1024 * ((2 * g + half - 1) % 4))
                 nc.vector.tensor_copy(
                     keys[:].bitcast(U16).rearrange("p (o u m) -> p o m u", o=PASSES, u=2),
                     kw_got[:].bitcast(U16).rearrange("p (m t o) -> p o m t", t=PACK, o=PASSES)[:, :, :, 2 * half : 2 * half + 2],

@@ -44,28 +44,24 @@ def tile_attend_pkv4_sigmoid_bias_kernel(tc, qT, k_words, k_scales, v_words, v_s
         nc.scalar.dma_start(vs_pages[P - POOL_PAGES : P, :], vs[0].rearrange("(u x) -> u x", u=POOL_PAGES))
         kb_win = sb.tile([P, T], F32, name="kb_win")
         nc.sync.dma_start(kb_win[ROW:P, :], kb[0:1, :])
+        q_raw = sb.tile([P, PASSES, PACK * NQ], F32, name="q_raw")
+        nc.sync.dma_start(q_raw[:], qT[0].rearrange("(o p j) q -> p o (j q)", o=PASSES, j=PACK))
+        kw_win = shared.tile([P, T], I32, name="kw_win", offset=0)
+        nc.sync.dma_start(kw_win[:], k_words[0].rearrange("p t b -> p (t b)").bitcast(I32))
 
-        ks_win = shared.tile([P, T // 4], I32, name="ks_win", offset=21504)
+        ks_win = shared.tile([P, T // 4], I32, name="ks_win", offset=16384)
         nc.vector.memset(ks_win[:], 0)
         nc.vector.memset(vs_pages[0 : P - POOL_PAGES, :].bitcast(I32), 0)
+        nc.vector.memset(kb_win[0:ROW, :].bitcast(I32), 0)
         ks_rows = k_scales.rearrange("o (u r) t -> r u o t", r=4)
         for r in range(4):
-            nc.sync.dma_start(ks_win[r:P:SHIFT, :], ks_rows[r].bitcast(I32))
-        nc.sync.dma_start(voffs_sb[:], voffs)
-        kw_win = sb.tile([P, T], I32, name="kw_win")
-        nc.sync.dma_start(kw_win[:], k_words[0].rearrange("p t b -> p (t b)").bitcast(I32))
-        q_rows = qT[0].rearrange("(o p j) q -> o p j q", o=PASSES, j=PACK)
-        q_raws = []
-        for o in range(PASSES):
-            q_raw = sb.tile([P, PACK, NQ], F32, name="q_raw%d" % o)
-            nc.sync.dma_start(q_raw[:], q_rows[o])
-            q_raws.append(q_raw)
+            nc.scalar.dma_start(ks_win[r:P:SHIFT, :], ks_rows[r].bitcast(I32))
 
         ident = sb.tile([P, P], F32, name="ident")
         make_identity(nc, ident[:])
-        warm = sb.tile([P, 8], F32, name="warm")
-        nc.scalar.activation(warm[:], ident[:, 0:8], SIGMOID)
-        vs_win = shared.tile([P, T], F32, name="vs_win", offset=0)
+        warm = sb.tile([32, 8], F32, name="warm")
+        nc.scalar.activation(warm[:], vs_pages[0:32, 0:8], SIGMOID)
+        vs_win = sb.tile([P, T], F32, name="vs_win")
         for t in range(PACK):
             turned = ps.tile([P, P], F32, name="turned%d" % t, tag="bank%d" % t)
             nc.tensor.transpose(turned[:], vs_pages[:, t:PAGE:PACK], ident[:])
@@ -73,14 +69,16 @@ def tile_attend_pkv4_sigmoid_bias_kernel(tc, qT, k_words, k_scales, v_words, v_s
                 vs_win[:].rearrange("p (u t q) -> p t u q", u=POOL_PAGES, t=PACK)[:, t],
                 turned[:, P - POOL_PAGES : P].unsqueeze(2).to_broadcast([P, POOL_PAGES, NQ]),
             )
-        nc.vector.memset(kb_win[0:ROW, :].bitcast(I32), 0)
 
         kb_got = sb.tile([P, N], F32, name="kb_got")
         nc.vector.tensor_copy(kb_got[:], kb_win[:].indirect(offs_sb[:]))
+        kb_col = sb.tile([P, PAGES, 8], F32, name="kb_col")
+        for g in range(PAGES):
+            nc.scalar.dma_start(kb_col[:, g, 0:PACK], kb_got[ROW:P, g * PAGE : (g + 1) * PAGE])
 
-        ks_got = shared.tile([P, N], U8, name="ks_got", offset=36864)
+        ks_got = sb.tile([P, N], U8, name="ks_got")
         nc.vector.tensor_copy(ks_got[:], ks_win[:].bitcast(U8).indirect(offs_sb[:]))
-        vsc_win = shared.tile([P, POOL_PAGES * DV // 4], I32, name="vsc_win", offset=21504)
+        vsc_win = shared.tile([P, POOL_PAGES * DV // 4], I32, name="vsc_win", offset=16384)
         nc.vector.memset(vsc_win[:], 0)
         ks_first = sb.tile([P, N // 4], I32, name="ks_first", align_bytes=64)
         nc.vector.tensor_copy(
@@ -88,47 +86,40 @@ def tile_attend_pkv4_sigmoid_bias_kernel(tc, qT, k_words, k_scales, v_words, v_s
             ks_got[:].rearrange("p (g m t) -> p g t m", g=PAGES, t=PACK),
         )
         ks_last = sb.tile([P, N // 4], I32, name="ks_last", align_bytes=64)
-        nc.scalar.dma_start(ks_last[0 : P - SHIFT, :], ks_first[SHIFT:P, :])
-        kb_col = shared.tile([P, PAGES, 8], F32, name="kb_col", offset=36864 + 256)
-        for g in range(PAGES):
-            nc.scalar.dma_start(kb_col[:, g, 0:PACK], kb_got[ROW:P, g * PAGE : (g + 1) * PAGE])
+        nc.sync.dma_start(ks_last[0 : P - SHIFT, :], ks_first[SHIFT:P, :])
         ks_planes = [ks_first[:].bitcast(U8), ks_last[:].bitcast(U8)]
 
-        vw_win = shared.tile([P, POOL_PAGES * DV], I32, name="vw_win", offset=40960)
+        nc.sync.dma_start(voffs_sb[:], voffs)
+        vw_win = sb.tile([P, POOL_PAGES * DV], I32, name="vw_win")
         nc.sync.dma_start(
             vw_win[:].rearrange("p (g e) -> p g e", g=POOL_PAGES),
             v_words.rearrange("g p e b -> p g (e b)").bitcast(I32),
         )
-
-        vs_got = shared.tile([P, N], F32, name="vs_got", offset=36864 + 256 - 4096)
-        nc.vector.tensor_copy(vs_got[:], vs_win[:].indirect(offs_sb[:]))
-
         vsc_rows = v_scales.rearrange("g (u r) e -> r u g e", r=4)
         for r in range(4):
-            nc.sync.dma_start(vsc_win[r:P:32, :].rearrange("p (g e) -> p g e", g=POOL_PAGES), vsc_rows[r].bitcast(I32))
+            nc.scalar.dma_start(vsc_win[r:P:32, :].rearrange("p (g e) -> p g e", g=POOL_PAGES), vsc_rows[r].bitcast(I32))
 
-        q_bf = shared.tile([P, PASSES, NQ, PACK], BF16, name="q_bf", align_bytes=64, offset=50176)
-        for o in range(PASSES):
-            nc.scalar.copy(
-                q_bf[:, o].rearrange("p (c i) j -> p c j i", i=4),
-                q_raws[o][:].rearrange("p j (c i) -> p c j i", i=4),
-            )
+        q_bf = sb.tile([P, PASSES, NQ, PACK], BF16, name="q_bf", align_bytes=64)
+        nc.vector.tensor_copy(
+            q_bf[:].rearrange("p o (c i) j -> p o c j i", i=4),
+            q_raw[:].rearrange("p o (j c i) -> p o c j i", j=PACK, i=4),
+        )
         q_codes = sb.tile([P, PASSES * NQ], U32, name="q_codes", align_bytes=64)
         q_scales = sb.tile([P, PASSES * NQ], U8, name="q_scales", align_bytes=64)
+        nc.vector.quantize_mx(out=q_codes[:].bitcast(FP8X4), scales=q_scales[:], in_=q_bf[:].rearrange("p o q j -> p (o q j)"))
 
         kw_pages = []
         for g in range(PAGES):
-            kw_got = shared.tile([P, PAGE], U32, name="kw_got%d" % g, offset=2048 * g)
+            kw_got = sb.tile([P, PAGE], U32, name="kw_got%d" % g)
             cols = slice(g * PAGE // 16, (g + 1) * PAGE // 16)
             nc.vector.tensor_copy(kw_got[:], kw_win[:].bitcast(U32).indirect(offs_sb[:, cols]))
             kw_pages.append(kw_got)
-        nc.vector.quantize_mx(out=q_codes[:].bitcast(FP8X4), scales=q_scales[:], in_=q_bf[:].rearrange("p o q j -> p (o q j)"))
         probs = []
         for g in range(PAGES):
             kw_got = kw_pages[g]
             prob = sb.tile([P, PACK, NQ], F32, name="prob%d" % g)
             for half in range(2):
-                keys = shared.tile([P, PASSES * 2 * P * 2], U8, name="keys%d" % (2 * g + half), align_bytes=64, offset=49408 + 1024 * ((2 * g + half - 1) % 4))
+                keys = sb.tile([P, PASSES * 2 * P * 2], U8, name="keys%d" % (2 * g + half), align_bytes=64)
                 nc.vector.tensor_copy(
                     keys[:].bitcast(U16).rearrange("p (o u m) -> p o m u", o=PASSES, u=2),
                     kw_got[:].bitcast(U16).rearrange("p (m t o) -> p o m t", t=PACK, o=PASSES)[:, :, :, 2 * half : 2 * half + 2],
@@ -151,23 +142,36 @@ def tile_attend_pkv4_sigmoid_bias_kernel(tc, qT, k_words, k_scales, v_words, v_s
                     nc.scalar.activation(prob[:, t, :], score[:, u, :], SIGMOID, bias=kb_col[:, g, t : t + 1])
             probs.append(prob)
 
-        vw_got = sb.tile([P, PAGES * DV], U32, name="vw_got", align_bytes=64)
-        nc.vector.tensor_copy(vw_got[:], vw_win[:].bitcast(U32).indirect(voffs_sb[:]))
-        vsc_got = shared.tile([P, PAGES * DV], U8, name="vsc_got", align_bytes=64, offset=4096)
-        nc.vector.tensor_copy(vsc_got[:], vsc_win[:].bitcast(U8).indirect(voffs_sb[:]))
-
-        y = ps.tile([P, DV], F32, name="y")
+        vs_gots = []
         for g in range(PAGES):
-            w_bf = shared.tile([P, NQ, PACK], BF16, name="w_bf%d" % g, align_bytes=64, offset=(40960, 22016)[g])
+            vs_got = shared.tile([P, PAGE], F32, name="vs_got%d" % g, offset=2048 * g)
+            cols = slice(g * PAGE // 16, (g + 1) * PAGE // 16)
+            nc.vector.tensor_copy(vs_got[:], vs_win[:].indirect(offs_sb[:, cols]))
+            vs_gots.append(vs_got)
+
+        vw_got = sb.tile([P, PAGES * DV], U32, name="vw_got", align_bytes=64)
+        vsc_got = sb.tile([P, PAGES * DV], U8, name="vsc_got", align_bytes=64)
+        weights = []
+        for g in range(PAGES):
+            w_bf = sb.tile([P, NQ, PACK], BF16, name="w_bf%d" % g, align_bytes=64)
             nc.vector.tensor_tensor(
                 w_bf[:].rearrange("p (c i) t -> p c t i", i=4),
                 probs[g][:].rearrange("p t (c i) -> p c t i", i=4),
-                vs_got[:, g * PAGE : (g + 1) * PAGE].rearrange("p (t c i) -> p c t i", t=PACK, i=4),
+                vs_gots[g][:].rearrange("p (t c i) -> p c t i", t=PACK, i=4),
                 MULT,
             )
-            w_codes = shared.tile([P, NQ], U32, name="w_codes%d" % g, align_bytes=64, offset=(21504, 23040)[g])
+            if g == 0:
+                nc.vector.tensor_copy(vsc_got[:], vsc_win[:].bitcast(U8).indirect(voffs_sb[:]))
+            else:
+                nc.vector.tensor_copy(vw_got[:], vw_win[:].bitcast(U32).indirect(voffs_sb[:]))
+            w_codes = sb.tile([P, NQ], U32, name="w_codes%d" % g, align_bytes=64)
             w_scales = sb.tile([P, NQ], U8, name="w_scales%d" % g, align_bytes=64)
             nc.vector.quantize_mx(out=w_codes[:].bitcast(FP8X4), scales=w_scales[:], in_=w_bf[:].rearrange("p q t -> p (q t)"))
+            weights.append((w_codes, w_scales))
+
+        y = ps.tile([P, DV], F32, name="y")
+        for g in range(PAGES):
+            w_codes, w_scales = weights[g]
             nc.tensor.matmul_mx(
                 out=y[:],
                 lhsT=w_codes[:].bitcast(FP8X4),

@@ -23,7 +23,7 @@ PAGES = N // PAGE
 POOL_PAGES = T // PAGE
 PASSES = D // (P * PACK)
 ROW = P - 1
-SHIFT = 16
+KS_ROW = P - 16 * PASSES
 
 FLOPS = 2 * NQ * N * D + 2 * NQ * N * DV
 BYTES = 4 * D * NQ + 4 * P * T + 32 * T + 4 * P * POOL_PAGES * DV + 16 * POOL_PAGES * DV + 8 * T + 2 * P * (N + PAGES * DV) // 16 + 4 * NQ * DV
@@ -44,18 +44,21 @@ def tile_attend_pkv4_sigmoid_bias_kernel(tc, qT, k_words, k_scales, v_words, v_s
         nc.scalar.dma_start(vs_pages[P - POOL_PAGES : P, :], vs[0].rearrange("(u x) -> u x", u=POOL_PAGES))
         kb_win = sb.tile([P, T], F32, name="kb_win")
         nc.sync.dma_start(kb_win[ROW:P, :], kb[0:1, :])
-        q_raw = sb.tile([P, PASSES, PACK * NQ], F32, name="q_raw")
-        nc.sync.dma_start(q_raw[:], qT[0].rearrange("(o p j) q -> p o (j q)", o=PASSES, j=PACK))
-        kw_win = shared.tile([P, T], I32, name="kw_win", offset=0)
-        nc.sync.dma_start(kw_win[:], k_words[0].rearrange("p t b -> p (t b)").bitcast(I32))
-
         ks_win = shared.tile([P, T // 4], I32, name="ks_win", offset=16384)
-        nc.vector.memset(ks_win[:], 0)
+        nc.sync.dma_start(ks_win[KS_ROW:P, :], k_scales.rearrange("o f t -> f o t").bitcast(I32))
+        nc.sync.dma_start(voffs_sb[:], voffs)
+        kw_win = sb.tile([P, T], I32, name="kw_win")
+        nc.sync.dma_start(kw_win[:], k_words[0].rearrange("p t b -> p (t b)").bitcast(I32))
+        q_rows = qT[0].rearrange("(o p j) q -> o p j q", o=PASSES, j=PACK)
+        q_raws = []
+        for o in range(PASSES):
+            q_raw = sb.tile([P, PACK, NQ], F32, name="q_raw%d" % o)
+            nc.sync.dma_start(q_raw[:], q_rows[o])
+            q_raws.append(q_raw)
+
         nc.vector.memset(vs_pages[0 : P - POOL_PAGES, :].bitcast(I32), 0)
+        nc.vector.memset(ks_win[0:KS_ROW, :], 0)
         nc.vector.memset(kb_win[0:ROW, :].bitcast(I32), 0)
-        ks_rows = k_scales.rearrange("o (u r) t -> r u o t", r=4)
-        for r in range(4):
-            nc.scalar.dma_start(ks_win[r:P:SHIFT, :], ks_rows[r].bitcast(I32))
 
         ident = sb.tile([P, P], F32, name="ident")
         make_identity(nc, ident[:])
@@ -74,36 +77,37 @@ def tile_attend_pkv4_sigmoid_bias_kernel(tc, qT, k_words, k_scales, v_words, v_s
         nc.vector.tensor_copy(kb_got[:], kb_win[:].indirect(offs_sb[:]))
         kb_col = sb.tile([P, PAGES, 8], F32, name="kb_col")
         for g in range(PAGES):
-            nc.scalar.dma_start(kb_col[:, g, 0:PACK], kb_got[ROW:P, g * PAGE : (g + 1) * PAGE])
+            nc.sync.dma_start(kb_col[:, g, 0:PACK], kb_got[ROW:P, g * PAGE : (g + 1) * PAGE])
 
         ks_got = sb.tile([P, N], U8, name="ks_got")
         nc.vector.tensor_copy(ks_got[:], ks_win[:].bitcast(U8).indirect(offs_sb[:]))
         vsc_win = shared.tile([P, POOL_PAGES * DV // 4], I32, name="vsc_win", offset=16384)
         nc.vector.memset(vsc_win[:], 0)
-        ks_first = sb.tile([P, N // 4], I32, name="ks_first", align_bytes=64)
+        ks_dealt = sb.tile([P, N // 4], I32, name="ks_dealt")
         nc.vector.tensor_copy(
-            ks_first[:].bitcast(U8).rearrange("p (g t m) -> p g t m", g=PAGES, t=PACK),
+            ks_dealt[:].bitcast(U8).rearrange("p (g t m) -> p g t m", g=PAGES, t=PACK),
             ks_got[:].rearrange("p (g m t) -> p g t m", g=PAGES, t=PACK),
         )
-        ks_last = sb.tile([P, N // 4], I32, name="ks_last", align_bytes=64)
-        nc.sync.dma_start(ks_last[0 : P - SHIFT, :], ks_first[SHIFT:P, :])
-        ks_planes = [ks_first[:].bitcast(U8), ks_last[:].bitcast(U8)]
+        ks_plane = sb.tile([P, PASSES * N // 4], I32, name="ks_plane", align_bytes=64)
+        for u in range(4):
+            nc.sync.dma_start(ks_plane[32 * u : 32 * u + 4, :], ks_dealt[KS_ROW + 8 * u : KS_ROW + 8 * (u + 1), :])
+        ks_planes = [ks_plane[:].bitcast(U8)[:, o * N : (o + 1) * N] for o in range(PASSES)]
 
-        nc.sync.dma_start(voffs_sb[:], voffs)
-        vw_win = sb.tile([P, POOL_PAGES * DV], I32, name="vw_win")
+        vw_win = shared.tile([P, POOL_PAGES * DV], I32, name="vw_win", offset=24576)
         nc.sync.dma_start(
             vw_win[:].rearrange("p (g e) -> p g e", g=POOL_PAGES),
             v_words.rearrange("g p e b -> p g (e b)").bitcast(I32),
         )
         vsc_rows = v_scales.rearrange("g (u r) e -> r u g e", r=4)
         for r in range(4):
-            nc.scalar.dma_start(vsc_win[r:P:32, :].rearrange("p (g e) -> p g e", g=POOL_PAGES), vsc_rows[r].bitcast(I32))
+            nc.sync.dma_start(vsc_win[r:P:32, :].rearrange("p (g e) -> p g e", g=POOL_PAGES), vsc_rows[r].bitcast(I32))
 
-        q_bf = sb.tile([P, PASSES, NQ, PACK], BF16, name="q_bf", align_bytes=64)
-        nc.vector.tensor_copy(
-            q_bf[:].rearrange("p o (c i) j -> p o c j i", i=4),
-            q_raw[:].rearrange("p o (j c i) -> p o c j i", j=PACK, i=4),
-        )
+        q_bf = shared.tile([P, PASSES, NQ, PACK], BF16, name="q_bf", align_bytes=64, offset=4032)
+        for o in range(PASSES):
+            nc.scalar.copy(
+                q_bf[:, o].rearrange("p (c i) j -> p c j i", i=4),
+                q_raws[o][:].rearrange("p j (c i) -> p c j i", i=4),
+            )
         q_codes = sb.tile([P, PASSES * NQ], U32, name="q_codes", align_bytes=64)
         q_scales = sb.tile([P, PASSES * NQ], U8, name="q_scales", align_bytes=64)
         nc.vector.quantize_mx(out=q_codes[:].bitcast(FP8X4), scales=q_scales[:], in_=q_bf[:].rearrange("p o q j -> p (o q j)"))
@@ -119,7 +123,7 @@ def tile_attend_pkv4_sigmoid_bias_kernel(tc, qT, k_words, k_scales, v_words, v_s
             kw_got = kw_pages[g]
             prob = sb.tile([P, PACK, NQ], F32, name="prob%d" % g)
             for half in range(2):
-                keys = sb.tile([P, PASSES * 2 * P * 2], U8, name="keys%d" % (2 * g + half), align_bytes=64)
+                keys = shared.tile([P, PASSES * 2 * P * 2], U8, name="keys%d" % (2 * g + half), align_bytes=64, offset=(8192, 4096)[g] + 1024 * half)
                 nc.vector.tensor_copy(
                     keys[:].bitcast(U16).rearrange("p (o u m) -> p o m u", o=PASSES, u=2),
                     kw_got[:].bitcast(U16).rearrange("p (m t o) -> p o m t", t=PACK, o=PASSES)[:, :, :, 2 * half : 2 * half + 2],
@@ -142,12 +146,10 @@ def tile_attend_pkv4_sigmoid_bias_kernel(tc, qT, k_words, k_scales, v_words, v_s
                     nc.scalar.activation(prob[:, t, :], score[:, u, :], SIGMOID, bias=kb_col[:, g, t : t + 1])
             probs.append(prob)
 
-        vs_gots = []
+        vs_got = shared.tile([P, PAGES, PAGE], F32, name="vs_got", offset=0)
         for g in range(PAGES):
-            vs_got = shared.tile([P, PAGE], F32, name="vs_got%d" % g, offset=2048 * g)
             cols = slice(g * PAGE // 16, (g + 1) * PAGE // 16)
-            nc.vector.tensor_copy(vs_got[:], vs_win[:].indirect(offs_sb[:, cols]))
-            vs_gots.append(vs_got)
+            nc.vector.tensor_copy(vs_got[:, g], vs_win[:].indirect(offs_sb[:, cols]))
 
         vw_got = sb.tile([P, PAGES * DV], U32, name="vw_got", align_bytes=64)
         vsc_got = sb.tile([P, PAGES * DV], U8, name="vsc_got", align_bytes=64)
@@ -157,14 +159,14 @@ def tile_attend_pkv4_sigmoid_bias_kernel(tc, qT, k_words, k_scales, v_words, v_s
             nc.vector.tensor_tensor(
                 w_bf[:].rearrange("p (c i) t -> p c t i", i=4),
                 probs[g][:].rearrange("p t (c i) -> p c t i", i=4),
-                vs_gots[g][:].rearrange("p (t c i) -> p c t i", t=PACK, i=4),
+                vs_got[:, g].rearrange("p (t c i) -> p c t i", t=PACK, i=4),
                 MULT,
             )
-            if g == 0:
+            if g == 1:
                 nc.vector.tensor_copy(vsc_got[:], vsc_win[:].bitcast(U8).indirect(voffs_sb[:]))
             else:
                 nc.vector.tensor_copy(vw_got[:], vw_win[:].bitcast(U32).indirect(voffs_sb[:]))
-            w_codes = sb.tile([P, NQ], U32, name="w_codes%d" % g, align_bytes=64)
+            w_codes = shared.tile([P, NQ], U32, name="w_codes%d" % g, align_bytes=64, offset=(24576, 16384)[g])
             w_scales = sb.tile([P, NQ], U8, name="w_scales%d" % g, align_bytes=64)
             nc.vector.quantize_mx(out=w_codes[:].bitcast(FP8X4), scales=w_scales[:], in_=w_bf[:].rearrange("p q t -> p (q t)"))
             weights.append((w_codes, w_scales))

@@ -43,9 +43,9 @@ def tile_attend_pkv4_sigmoid_bias_kernel(tc, qT, k_words, k_scales, v_words, v_s
         vs_pages = sb.tile([P, PAGE], F32, name="vs_pages")
         nc.scalar.dma_start(vs_pages[P - POOL_PAGES : P, :], vs[0].rearrange("(u x) -> u x", u=POOL_PAGES))
         kb_win = sb.tile([P, T], F32, name="kb_win")
-        nc.sync.dma_start(kb_win[ROW:P, :], kb[0:1, :])
-        ks_win = shared.tile([P, T // 4], I32, name="ks_win", offset=16384)
+        ks_win = sb.tile([P, T // 4], I32, name="ks_win")
         nc.sync.dma_start(ks_win[KS_ROW:P, :], k_scales.rearrange("o f t -> f o t").bitcast(I32))
+        nc.sync.dma_start(kb_win[ROW:P, :], kb[0:1, :])
         nc.sync.dma_start(voffs_sb[:], voffs)
         kw_win = sb.tile([P, T], I32, name="kw_win")
         nc.sync.dma_start(kw_win[:], k_words[0].rearrange("p t b -> p (t b)").bitcast(I32))
@@ -58,10 +58,11 @@ def tile_attend_pkv4_sigmoid_bias_kernel(tc, qT, k_words, k_scales, v_words, v_s
 
         nc.vector.memset(vs_pages[0 : P - POOL_PAGES, :].bitcast(I32), 0)
         nc.vector.memset(ks_win[0:KS_ROW, :], 0)
-        nc.vector.memset(kb_win[0:ROW, :].bitcast(I32), 0)
+        nc.vector.memset(kb_win[0:ROW, 0 : T // 2 + 8].bitcast(I32), 0)
 
         ident = sb.tile([P, P], F32, name="ident")
         make_identity(nc, ident[:])
+        nc.gpsimd.memset(kb_win[0:ROW, T // 2 : T].bitcast(I32), 0)
         warm = sb.tile([32, 8], F32, name="warm")
         nc.scalar.activation(warm[:], vs_pages[0:32, 0:8], SIGMOID)
         vs_win = sb.tile([P, T], F32, name="vs_win")
@@ -73,16 +74,8 @@ def tile_attend_pkv4_sigmoid_bias_kernel(tc, qT, k_words, k_scales, v_words, v_s
                 turned[:, P - POOL_PAGES : P].unsqueeze(2).to_broadcast([P, POOL_PAGES, NQ]),
             )
 
-        kb_got = sb.tile([P, N], F32, name="kb_got")
-        nc.vector.tensor_copy(kb_got[:], kb_win[:].indirect(offs_sb[:]))
-        kb_col = sb.tile([P, PAGES, 8], F32, name="kb_col")
-        for g in range(PAGES):
-            nc.sync.dma_start(kb_col[:, g, 0:PACK], kb_got[ROW:P, g * PAGE : (g + 1) * PAGE])
-
-        ks_got = sb.tile([P, N], U8, name="ks_got")
+        ks_got = shared.tile([P, N], U8, name="ks_got", offset=16384)
         nc.vector.tensor_copy(ks_got[:], ks_win[:].bitcast(U8).indirect(offs_sb[:]))
-        vsc_win = shared.tile([P, POOL_PAGES * DV // 4], I32, name="vsc_win", offset=16384)
-        nc.vector.memset(vsc_win[:], 0)
         ks_dealt = sb.tile([P, N // 4], I32, name="ks_dealt")
         nc.vector.tensor_copy(
             ks_dealt[:].bitcast(U8).rearrange("p (g t m) -> p g t m", g=PAGES, t=PACK),
@@ -93,7 +86,15 @@ def tile_attend_pkv4_sigmoid_bias_kernel(tc, qT, k_words, k_scales, v_words, v_s
             nc.sync.dma_start(ks_plane[32 * u : 32 * u + 4, :], ks_dealt[KS_ROW + 8 * u : KS_ROW + 8 * (u + 1), :])
         ks_planes = [ks_plane[:].bitcast(U8)[:, o * N : (o + 1) * N] for o in range(PASSES)]
 
-        vw_win = shared.tile([P, POOL_PAGES * DV], I32, name="vw_win", offset=24576)
+        kb_got = sb.tile([P, N], F32, name="kb_got")
+        nc.vector.tensor_copy(kb_got[:], kb_win[:].indirect(offs_sb[:]))
+        kb_col = sb.tile([P, PAGES, 8], F32, name="kb_col")
+        for g in range(PAGES):
+            nc.sync.dma_start(kb_col[:, g, 0:PACK], kb_got[ROW:P, g * PAGE : (g + 1) * PAGE])
+
+        vsc_win = shared.tile([P, POOL_PAGES * DV // 4], I32, name="vsc_win", offset=16384)
+        nc.gpsimd.memset(vsc_win[:], 0)
+        vw_win = sb.tile([P, POOL_PAGES * DV], I32, name="vw_win")
         nc.sync.dma_start(
             vw_win[:].rearrange("p (g e) -> p g e", g=POOL_PAGES),
             v_words.rearrange("g p e b -> p g (e b)").bitcast(I32),
@@ -153,7 +154,7 @@ def tile_attend_pkv4_sigmoid_bias_kernel(tc, qT, k_words, k_scales, v_words, v_s
 
         vw_got = sb.tile([P, PAGES * DV], U32, name="vw_got", align_bytes=64)
         vsc_got = sb.tile([P, PAGES * DV], U8, name="vsc_got", align_bytes=64)
-        weights = []
+        w_bfs = []
         for g in range(PAGES):
             w_bf = sb.tile([P, NQ, PACK], BF16, name="w_bf%d" % g, align_bytes=64)
             nc.vector.tensor_tensor(
@@ -162,13 +163,16 @@ def tile_attend_pkv4_sigmoid_bias_kernel(tc, qT, k_words, k_scales, v_words, v_s
                 vs_got[:, g].rearrange("p (t c i) -> p c t i", t=PACK, i=4),
                 MULT,
             )
-            if g == 1:
-                nc.vector.tensor_copy(vsc_got[:], vsc_win[:].bitcast(U8).indirect(voffs_sb[:]))
-            else:
+            w_bfs.append(w_bf)
+            if g == 0:
                 nc.vector.tensor_copy(vw_got[:], vw_win[:].bitcast(U32).indirect(voffs_sb[:]))
-            w_codes = shared.tile([P, NQ], U32, name="w_codes%d" % g, align_bytes=64, offset=(24576, 16384)[g])
+            else:
+                nc.vector.tensor_copy(vsc_got[:], vsc_win[:].bitcast(U8).indirect(voffs_sb[:]))
+        weights = []
+        for g in range(PAGES):
+            w_codes = shared.tile([P, NQ], U32, name="w_codes%d" % g, align_bytes=64, offset=16384 + 512 * g)
             w_scales = sb.tile([P, NQ], U8, name="w_scales%d" % g, align_bytes=64)
-            nc.vector.quantize_mx(out=w_codes[:].bitcast(FP8X4), scales=w_scales[:], in_=w_bf[:].rearrange("p q t -> p (q t)"))
+            nc.vector.quantize_mx(out=w_codes[:].bitcast(FP8X4), scales=w_scales[:], in_=w_bfs[g][:].rearrange("p q t -> p (q t)"))
             weights.append((w_codes, w_scales))
 
         y = ps.tile([P, DV], F32, name="y")

@@ -24,6 +24,8 @@ POOL_PAGES = T // PAGE
 PASSES = D // (P * PACK)
 ROW = P - 1
 KS_ROW = P - 16 * PASSES
+VSC_ROW = P - 16
+KB_SPLIT = 2176
 
 FLOPS = 2 * NQ * N * D + 2 * NQ * N * DV
 BYTES = 4 * D * NQ + 4 * P * T + 32 * T + 4 * P * POOL_PAGES * DV + 16 * POOL_PAGES * DV + 8 * T + 2 * P * (N + PAGES * DV) // 16 + 4 * NQ * DV
@@ -44,9 +46,14 @@ def tile_attend_pkv4_sigmoid_bias_kernel(tc, qT, k_words, k_scales, v_words, v_s
         nc.scalar.dma_start(vs_pages[P - POOL_PAGES : P, :], vs[0].rearrange("(u x) -> u x", u=POOL_PAGES))
         kb_win = sb.tile([P, T], F32, name="kb_win")
         ks_win = sb.tile([P, T // 4], I32, name="ks_win")
+        nc.sync.dma_start(voffs_sb[:], voffs)
+        vsc_win = sb.tile([P, POOL_PAGES * DV // 4], I32, name="vsc_win")
+        nc.sync.dma_start(
+            vsc_win[VSC_ROW:P, :].rearrange("p (g e) -> p g e", g=POOL_PAGES),
+            v_scales.rearrange("g f e -> f g e").bitcast(I32),
+        )
         nc.sync.dma_start(ks_win[KS_ROW:P, :], k_scales.rearrange("o f t -> f o t").bitcast(I32))
         nc.sync.dma_start(kb_win[ROW:P, :], kb[0:1, :])
-        nc.sync.dma_start(voffs_sb[:], voffs)
         kw_win = sb.tile([P, T], I32, name="kw_win")
         nc.sync.dma_start(kw_win[:], k_words[0].rearrange("p t b -> p (t b)").bitcast(I32))
         q_rows = qT[0].rearrange("(o p j) q -> o p j q", o=PASSES, j=PACK)
@@ -57,12 +64,13 @@ def tile_attend_pkv4_sigmoid_bias_kernel(tc, qT, k_words, k_scales, v_words, v_s
             q_raws.append(q_raw)
 
         nc.vector.memset(vs_pages[0 : P - POOL_PAGES, :].bitcast(I32), 0)
+        nc.vector.memset(vsc_win[0:VSC_ROW, :], 0)
         nc.vector.memset(ks_win[0:KS_ROW, :], 0)
-        nc.vector.memset(kb_win[0:ROW, 0 : T // 2 + 8].bitcast(I32), 0)
+        nc.vector.memset(kb_win[0:ROW, 0 : KB_SPLIT + 8].bitcast(I32), 0)
 
         ident = sb.tile([P, P], F32, name="ident")
         make_identity(nc, ident[:])
-        nc.gpsimd.memset(kb_win[0:ROW, T // 2 : T].bitcast(I32), 0)
+        nc.gpsimd.memset(kb_win[0:ROW, KB_SPLIT:T].bitcast(I32), 0)
         warm = sb.tile([32, 8], F32, name="warm")
         nc.scalar.activation(warm[:], vs_pages[0:32, 0:8], SIGMOID)
         vs_win = sb.tile([P, T], F32, name="vs_win")
@@ -74,7 +82,10 @@ def tile_attend_pkv4_sigmoid_bias_kernel(tc, qT, k_words, k_scales, v_words, v_s
                 turned[:, P - POOL_PAGES : P].unsqueeze(2).to_broadcast([P, POOL_PAGES, NQ]),
             )
 
-        ks_got = shared.tile([P, N], U8, name="ks_got", offset=16384)
+        vsc_got = sb.tile([P, PAGES * DV // 4], I32, name="vsc_got")
+        nc.vector.tensor_copy(vsc_got[:].bitcast(U8), vsc_win[:].bitcast(U8).indirect(voffs_sb[:]))
+
+        ks_got = sb.tile([P, N], U8, name="ks_got")
         nc.vector.tensor_copy(ks_got[:], ks_win[:].bitcast(U8).indirect(offs_sb[:]))
         ks_dealt = sb.tile([P, N // 4], I32, name="ks_dealt")
         nc.vector.tensor_copy(
@@ -92,16 +103,14 @@ def tile_attend_pkv4_sigmoid_bias_kernel(tc, qT, k_words, k_scales, v_words, v_s
         for g in range(PAGES):
             nc.sync.dma_start(kb_col[:, g, 0:PACK], kb_got[ROW:P, g * PAGE : (g + 1) * PAGE])
 
-        vsc_win = shared.tile([P, POOL_PAGES * DV // 4], I32, name="vsc_win", offset=16384)
-        nc.gpsimd.memset(vsc_win[:], 0)
-        vw_win = sb.tile([P, POOL_PAGES * DV], I32, name="vw_win")
+        vw_win = shared.tile([P, POOL_PAGES * DV], I32, name="vw_win", offset=16384)
         nc.sync.dma_start(
             vw_win[:].rearrange("p (g e) -> p g e", g=POOL_PAGES),
             v_words.rearrange("g p e b -> p g (e b)").bitcast(I32),
         )
-        vsc_rows = v_scales.rearrange("g (u r) e -> r u g e", r=4)
-        for r in range(4):
-            nc.sync.dma_start(vsc_win[r:P:32, :].rearrange("p (g e) -> p g e", g=POOL_PAGES), vsc_rows[r].bitcast(I32))
+        vsc_plane = sb.tile([P, PAGES * DV // 4], I32, name="vsc_plane", align_bytes=64)
+        for u in range(4):
+            nc.sync.dma_start(vsc_plane[32 * u : 32 * u + 4, :], vsc_got[VSC_ROW + 4 * u : VSC_ROW + 4 * (u + 1), :])
 
         q_bf = shared.tile([P, PASSES, NQ, PACK], BF16, name="q_bf", align_bytes=64, offset=4032)
         for o in range(PASSES):
@@ -153,7 +162,6 @@ def tile_attend_pkv4_sigmoid_bias_kernel(tc, qT, k_words, k_scales, v_words, v_s
             nc.vector.tensor_copy(vs_got[:, g], vs_win[:].indirect(offs_sb[:, cols]))
 
         vw_got = sb.tile([P, PAGES * DV], U32, name="vw_got", align_bytes=64)
-        vsc_got = sb.tile([P, PAGES * DV], U8, name="vsc_got", align_bytes=64)
         w_bfs = []
         for g in range(PAGES):
             w_bf = sb.tile([P, NQ, PACK], BF16, name="w_bf%d" % g, align_bytes=64)
@@ -164,10 +172,7 @@ def tile_attend_pkv4_sigmoid_bias_kernel(tc, qT, k_words, k_scales, v_words, v_s
                 MULT,
             )
             w_bfs.append(w_bf)
-            if g == 0:
-                nc.vector.tensor_copy(vw_got[:], vw_win[:].bitcast(U32).indirect(voffs_sb[:]))
-            else:
-                nc.vector.tensor_copy(vsc_got[:], vsc_win[:].bitcast(U8).indirect(voffs_sb[:]))
+        nc.vector.tensor_copy(vw_got[:], vw_win[:].bitcast(U32).indirect(voffs_sb[:]))
         weights = []
         for g in range(PAGES):
             w_codes = shared.tile([P, NQ], U32, name="w_codes%d" % g, align_bytes=64, offset=16384 + 512 * g)
@@ -183,7 +188,7 @@ def tile_attend_pkv4_sigmoid_bias_kernel(tc, qT, k_words, k_scales, v_words, v_s
                 lhsT=w_codes[:].bitcast(FP8X4),
                 lhsT_scale=w_scales[:],
                 rhs=vw_got[:, g * DV : (g + 1) * DV].bitcast(FP8X4),
-                rhs_scale=vsc_got[:, g * DV : (g + 1) * DV],
+                rhs_scale=vsc_plane[:].bitcast(U8)[:, g * DV : (g + 1) * DV],
                 start=(g == 0),
                 stop=(g == PAGES - 1),
             )

@@ -59,7 +59,7 @@ def tile_attend_pkv4_sigmoid_bias_kernel(tc, qT, k_words, k_scales, v_words, v_s
         q_rows = qT[0].rearrange("(o p j) q -> o p j q", o=PASSES, j=PACK)
         q_raws = []
         for o in range(PASSES):
-            q_raw = sb.tile([P, PACK, NQ], F32, name="q_raw%d" % o)
+            q_raw = shared.tile([P, PACK, NQ], F32, name="q_raw%d" % o, offset=4096 * o)
             nc.sync.dma_start(q_raw[:], q_rows[o])
             q_raws.append(q_raw)
 
@@ -74,15 +74,16 @@ def tile_attend_pkv4_sigmoid_bias_kernel(tc, qT, k_words, k_scales, v_words, v_s
         warm = sb.tile([32, 8], F32, name="warm")
         nc.scalar.activation(warm[:], vs_pages[0:32, 0:8], SIGMOID)
         vs_win = sb.tile([P, T], F32, name="vs_win")
+        vs_places = vs_win[:].rearrange("p (u t q) -> p t u q", u=POOL_PAGES, t=PACK)
+        turned = []
         for t in range(PACK):
-            turned = ps.tile([P, P], F32, name="turned%d" % t, tag="bank%d" % t)
-            nc.tensor.transpose(turned[:], vs_pages[:, t:PAGE:PACK], ident[:])
-            nc.scalar.copy(
-                vs_win[:].rearrange("p (u t q) -> p t u q", u=POOL_PAGES, t=PACK)[:, t],
-                turned[:, P - POOL_PAGES : P].unsqueeze(2).to_broadcast([P, POOL_PAGES, NQ]),
-            )
+            bank = ps.tile([P, P], F32, name="turned%d" % t, tag="bank%d" % t)
+            nc.tensor.transpose(bank[:], vs_pages[:, t:PAGE:PACK], ident[:])
+            turned.append(bank[:, P - POOL_PAGES : P])
+        for t in range(PACK - 1):
+            nc.scalar.copy(vs_places[:, t], turned[t].unsqueeze(2).to_broadcast([P, POOL_PAGES, NQ]))
 
-        vsc_got = sb.tile([P, PAGES * DV // 4], I32, name="vsc_got")
+        vsc_got = shared.tile([P, PAGES * DV // 4], I32, name="vsc_got", offset=16640)
         nc.vector.tensor_copy(vsc_got[:].bitcast(U8), vsc_win[:].bitcast(U8).indirect(voffs_sb[:]))
 
         ks_got = sb.tile([P, N], U8, name="ks_got")
@@ -103,7 +104,7 @@ def tile_attend_pkv4_sigmoid_bias_kernel(tc, qT, k_words, k_scales, v_words, v_s
         for g in range(PAGES):
             nc.sync.dma_start(kb_col[:, g, 0:PACK], kb_got[ROW:P, g * PAGE : (g + 1) * PAGE])
 
-        vw_win = shared.tile([P, POOL_PAGES * DV], I32, name="vw_win", offset=16384)
+        vw_win = sb.tile([P, POOL_PAGES * DV], I32, name="vw_win")
         nc.sync.dma_start(
             vw_win[:].rearrange("p (g e) -> p g e", g=POOL_PAGES),
             v_words.rearrange("g p e b -> p g (e b)").bitcast(I32),
@@ -112,12 +113,15 @@ def tile_attend_pkv4_sigmoid_bias_kernel(tc, qT, k_words, k_scales, v_words, v_s
         for u in range(4):
             nc.sync.dma_start(vsc_plane[32 * u : 32 * u + 4, :], vsc_got[VSC_ROW + 4 * u : VSC_ROW + 4 * (u + 1), :])
 
-        q_bf = shared.tile([P, PASSES, NQ, PACK], BF16, name="q_bf", align_bytes=64, offset=4032)
+        q_bf = sb.tile([P, PASSES, NQ, PACK], BF16, name="q_bf", align_bytes=64)
         for o in range(PASSES):
             nc.scalar.copy(
                 q_bf[:, o].rearrange("p (c i) j -> p c j i", i=4),
                 q_raws[o][:].rearrange("p j (c i) -> p c j i", i=4),
             )
+        vs_last = shared.tile([P, POOL_PAGES], F32, name="vs_last", offset=4096)
+        nc.scalar.copy(vs_last[:], turned[PACK - 1])
+        nc.scalar.copy(vs_places[:, PACK - 1], vs_last[:].unsqueeze(2).to_broadcast([P, POOL_PAGES, NQ]))
         q_codes = sb.tile([P, PASSES * NQ], U32, name="q_codes", align_bytes=64)
         q_scales = sb.tile([P, PASSES * NQ], U8, name="q_scales", align_bytes=64)
         nc.vector.quantize_mx(out=q_codes[:].bitcast(FP8X4), scales=q_scales[:], in_=q_bf[:].rearrange("p o q j -> p (o q j)"))
@@ -133,7 +137,7 @@ def tile_attend_pkv4_sigmoid_bias_kernel(tc, qT, k_words, k_scales, v_words, v_s
             kw_got = kw_pages[g]
             prob = sb.tile([P, PACK, NQ], F32, name="prob%d" % g)
             for half in range(2):
-                keys = shared.tile([P, PASSES * 2 * P * 2], U8, name="keys%d" % (2 * g + half), align_bytes=64, offset=(8192, 4096)[g] + 1024 * half)
+                keys = shared.tile([P, PASSES * 2 * P * 2], U8, name="keys%d" % (2 * g + half), align_bytes=64, offset=(8192, 4160)[g] + 1024 * half)
                 nc.vector.tensor_copy(
                     keys[:].bitcast(U16).rearrange("p (o u m) -> p o m u", o=PASSES, u=2),
                     kw_got[:].bitcast(U16).rearrange("p (m t o) -> p o m t", t=PACK, o=PASSES)[:, :, :, 2 * half : 2 * half + 2],
@@ -156,7 +160,7 @@ def tile_attend_pkv4_sigmoid_bias_kernel(tc, qT, k_words, k_scales, v_words, v_s
                     nc.scalar.activation(prob[:, t, :], score[:, u, :], SIGMOID, bias=kb_col[:, g, t : t + 1])
             probs.append(prob)
 
-        vs_got = shared.tile([P, PAGES, PAGE], F32, name="vs_got", offset=0)
+        vs_got = sb.tile([P, PAGES, PAGE], F32, name="vs_got")
         for g in range(PAGES):
             cols = slice(g * PAGE // 16, (g + 1) * PAGE // 16)
             nc.vector.tensor_copy(vs_got[:, g], vs_win[:].indirect(offs_sb[:, cols]))

@@ -166,20 +166,20 @@ def tile_attend_pkv4_sigmoid_bias_kernel(tc, qT, k_words, k_scales, v_words, v_s
             nc.vector.tensor_copy(vs_got[:, g], vs_win[:].indirect(offs_sb[:, cols]))
 
         vw_got = sb.tile([P, PAGES * DV], U32, name="vw_got", align_bytes=64)
+        nc.vector.tensor_copy(vw_got[:], vw_win[:].bitcast(U32).indirect(voffs_sb[:]))
         w_bfs = []
         for g in range(PAGES):
-            w_bf = sb.tile([P, NQ, PACK], BF16, name="w_bf%d" % g, align_bytes=64)
-            nc.vector.tensor_tensor(
+            w_bf = shared.tile([P, NQ, PACK], BF16, name="w_bf%d" % g, align_bytes=64, offset=(20480, 16896)[g])
+            (nc.gpsimd, nc.vector)[g].tensor_tensor(
                 w_bf[:].rearrange("p (c i) t -> p c t i", i=4),
                 probs[g][:].rearrange("p t (c i) -> p c t i", i=4),
                 vs_got[:, g].rearrange("p (t c i) -> p c t i", t=PACK, i=4),
                 MULT,
             )
             w_bfs.append(w_bf)
-        nc.vector.tensor_copy(vw_got[:], vw_win[:].bitcast(U32).indirect(voffs_sb[:]))
         weights = []
         for g in range(PAGES):
-            w_codes = shared.tile([P, NQ], U32, name="w_codes%d" % g, align_bytes=64, offset=16384 + 512 * g)
+            w_codes = shared.tile([P, NQ], U32, name="w_codes%d" % g, align_bytes=64, offset=(16384, 22528)[g])
             w_scales = sb.tile([P, NQ], U8, name="w_scales%d" % g, align_bytes=64)
             nc.vector.quantize_mx(out=w_codes[:].bitcast(FP8X4), scales=w_scales[:], in_=w_bfs[g][:].rearrange("p q t -> p (q t)"))
             weights.append((w_codes, w_scales))

@@ -22,10 +22,10 @@ PAGE = 512
 PAGES = N // PAGE
 POOL_PAGES = T // PAGE
 PASSES = D // (P * PACK)
-ROW = P - 1
+BLOCKS = POOL_PAGES * PACK
 KS_ROW = P - 16 * PASSES
-VSC_ROW = P - 16
-KB_SPLIT = 2176
+KB_FILL = 40
+VS_FILL = 40
 
 FLOPS = 2 * NQ * N * D + 2 * NQ * N * DV
 BYTES = 4 * D * NQ + 4 * P * T + 32 * T + 4 * P * POOL_PAGES * DV + 16 * POOL_PAGES * DV + 8 * T + 2 * P * (N + PAGES * DV) // 16 + 4 * NQ * DV
@@ -41,54 +41,58 @@ def tile_attend_pkv4_sigmoid_bias_kernel(tc, qT, k_words, k_scales, v_words, v_s
 
         offs_sb = lists.tile([P, N // 16], U16, name="offs_sb")
         voffs_sb = lists.tile([P, PAGES * DV // 16], U16, name="voffs_sb")
-        nc.sync.dma_start(offs_sb[:], offs)
-        vs_pages = sb.tile([P, PAGE], F32, name="vs_pages")
-        nc.scalar.dma_start(vs_pages[P - POOL_PAGES : P, :], vs[0].rearrange("(u x) -> u x", u=POOL_PAGES))
-        kb_win = sb.tile([P, T], F32, name="kb_win")
-        ks_win = sb.tile([P, T // 4], I32, name="ks_win")
-        nc.sync.dma_start(voffs_sb[:], voffs)
+        kb_rows = sb.tile([P, PAGE], F32, name="kb_rows")
+        vs_rows = shared.tile([P, PAGE], F32, name="vs_rows", offset=34816)
         vsc_win = sb.tile([P, POOL_PAGES * DV // 4], I32, name="vsc_win")
+        ks_win = sb.tile([P, T // 4], I32, name="ks_win")
+        kb_win = shared.tile([P, T], F32, name="kb_win", offset=0)
+        vs_win = sb.tile([P, T], F32, name="vs_win")
+        kb_blocks = kb_win[:].rearrange("p (b x) -> p b x", b=BLOCKS)
+        vs_blocks = vs_win[:].rearrange("p (b x) -> p b x", b=BLOCKS)
+
+        nc.vector.memset(kb_rows[:], 0.0)
+        nc.vector.memset(vs_rows[:], 0.0)
+        nc.vector.memset(vsc_win[:], 0)
+        nc.vector.memset(ks_win[0:KS_ROW, :], 0)
+        nc.vector.memset(kb_blocks[:, :, KB_FILL:P], 0.0)
+        nc.vector.memset(vs_blocks[:, 0:2, VS_FILL:P], 0.0)
+
+        nc.sync.dma_start(offs_sb[:], offs)
+        nc.sync.dma_start(ks_win[KS_ROW:P, :], k_scales.rearrange("o f t -> f o t").bitcast(I32))
+        for rows, table in ((kb_rows, kb), (vs_rows, vs)):
+            shifted = table.rearrange("r x -> (r x)")[0 : PACK * (T + 1)].rearrange("(t y) -> t y", t=PACK)[:, 0:T]
+            nc.sync.dma_start(rows[0:P:4, :], shifted.rearrange("t (u x) -> u t x", u=POOL_PAGES))
+        nc.sync.dma_start(voffs_sb[:], voffs)
         nc.sync.dma_start(
-            vsc_win[VSC_ROW:P, :].rearrange("p (g e) -> p g e", g=POOL_PAGES),
+            vsc_win[0:64:4, :].rearrange("p (g e) -> p g e", g=POOL_PAGES),
             v_scales.rearrange("g f e -> f g e").bitcast(I32),
         )
-        nc.sync.dma_start(ks_win[KS_ROW:P, :], k_scales.rearrange("o f t -> f o t").bitcast(I32))
-        nc.sync.dma_start(kb_win[ROW:P, :], kb[0:1, :])
+        q_raw = sb.tile([P, PASSES, PACK * NQ], F32, name="q_raw")
+        nc.sync.dma_start(q_raw[:], qT[0].rearrange("(o p j) q -> p o (j q)", o=PASSES, j=PACK))
         kw_win = sb.tile([P, T], I32, name="kw_win")
         nc.sync.dma_start(kw_win[:], k_words[0].rearrange("p t b -> p (t b)").bitcast(I32))
-        q_rows = qT[0].rearrange("(o p j) q -> o p j q", o=PASSES, j=PACK)
-        q_raws = []
-        for o in range(PASSES):
-            q_raw = shared.tile([P, PACK, NQ], F32, name="q_raw%d" % o, offset=4096 * o)
-            nc.sync.dma_start(q_raw[:], q_rows[o])
-            q_raws.append(q_raw)
-
-        nc.vector.memset(vs_pages[0 : P - POOL_PAGES, :].bitcast(I32), 0)
-        nc.vector.memset(vsc_win[0:VSC_ROW, :], 0)
-        nc.vector.memset(ks_win[0:KS_ROW, :], 0)
-        nc.vector.memset(kb_win[0:ROW, 0 : KB_SPLIT + 8].bitcast(I32), 0)
 
         ident = sb.tile([P, P], F32, name="ident")
         make_identity(nc, ident[:])
-        nc.gpsimd.memset(kb_win[0:ROW, KB_SPLIT:T].bitcast(I32), 0)
-        warm = sb.tile([32, 8], F32, name="warm")
-        nc.scalar.activation(warm[:], vs_pages[0:32, 0:8], SIGMOID)
-        vs_win = sb.tile([P, T], F32, name="vs_win")
-        vs_places = vs_win[:].rearrange("p (u t q) -> p t u q", u=POOL_PAGES, t=PACK)
-        turned = []
-        for t in range(PACK):
-            bank = ps.tile([P, P], F32, name="turned%d" % t, tag="bank%d" % t)
-            nc.tensor.transpose(bank[:], vs_pages[:, t:PAGE:PACK], ident[:])
-            turned.append(bank[:, P - POOL_PAGES : P])
-        for t in range(PACK - 1):
-            nc.scalar.copy(vs_places[:, t], turned[t].unsqueeze(2).to_broadcast([P, POOL_PAGES, NQ]))
+        nc.gpsimd.memset(vs_blocks[:, 1:BLOCKS, VS_FILL:P], 0.0)
+        warm = sb.tile([96, 8], F32, name="warm")
+        nc.scalar.activation(warm[64:96, :], ident[64:96, 0:8], SIGMOID)
 
+        for rows, blocks, fill, tag in ((kb_rows, kb_blocks, KB_FILL, "bank6"), (vs_rows, vs_blocks, VS_FILL, "bank7")):
+            turned = ps.tile([P, P], F32, name="turned", tag=tag)
+            nc.tensor.transpose(turned[:], rows[:, 0:PAGE:PACK], ident[:])
+            nc.scalar.copy(
+                blocks[:, :, 0:fill],
+                turned[:].rearrange("p (b r) -> p b r", r=4)[:, :, 0:1].to_broadcast([P, BLOCKS, fill]),
+            )
+
+        ks_got = shared.tile([P, N], U8, name="ks_got", offset=24576)
+        nc.vector.tensor_copy(ks_got[:], ks_win[:].bitcast(U8).indirect(offs_sb[:]))
+        kb_got = sb.tile([P, N], F32, name="kb_got")
+        nc.vector.tensor_copy(kb_got[:], kb_win[:].indirect(offs_sb[:]))
         vsc_got = shared.tile([P, PAGES * DV // 4], I32, name="vsc_got", offset=16640)
         nc.vector.tensor_copy(vsc_got[:].bitcast(U8), vsc_win[:].bitcast(U8).indirect(voffs_sb[:]))
-
-        ks_got = sb.tile([P, N], U8, name="ks_got")
-        nc.vector.tensor_copy(ks_got[:], ks_win[:].bitcast(U8).indirect(offs_sb[:]))
-        ks_dealt = sb.tile([P, N // 4], I32, name="ks_dealt")
+        ks_dealt = shared.tile([P, N // 4], I32, name="ks_dealt", offset=0)
         nc.vector.tensor_copy(
             ks_dealt[:].bitcast(U8).rearrange("p (g t m) -> p g t m", g=PAGES, t=PACK),
             ks_got[:].rearrange("p (g m t) -> p g t m", g=PAGES, t=PACK),
@@ -98,30 +102,24 @@ def tile_attend_pkv4_sigmoid_bias_kernel(tc, qT, k_words, k_scales, v_words, v_s
             nc.sync.dma_start(ks_plane[32 * u : 32 * u + 4, :], ks_dealt[KS_ROW + 8 * u : KS_ROW + 8 * (u + 1), :])
         ks_planes = [ks_plane[:].bitcast(U8)[:, o * N : (o + 1) * N] for o in range(PASSES)]
 
-        kb_got = sb.tile([P, N], F32, name="kb_got")
-        nc.vector.tensor_copy(kb_got[:], kb_win[:].indirect(offs_sb[:]))
-        kb_col = sb.tile([P, PAGES, 8], F32, name="kb_col")
-        for g in range(PAGES):
-            nc.sync.dma_start(kb_col[:, g, 0:PACK], kb_got[ROW:P, g * PAGE : (g + 1) * PAGE])
-
-        vw_win = sb.tile([P, POOL_PAGES * DV], I32, name="vw_win")
+        vw_win = shared.tile([P, POOL_PAGES * DV], I32, name="vw_win", offset=25088)
         nc.sync.dma_start(
             vw_win[:].rearrange("p (g e) -> p g e", g=POOL_PAGES),
             v_words.rearrange("g p e b -> p g (e b)").bitcast(I32),
         )
-        vsc_plane = sb.tile([P, PAGES * DV // 4], I32, name="vsc_plane", align_bytes=64)
+        vsc_plane = shared.tile([P, PAGES * DV // 4], I32, name="vsc_plane", align_bytes=64, offset=24576)
         for u in range(4):
-            nc.sync.dma_start(vsc_plane[32 * u : 32 * u + 4, :], vsc_got[VSC_ROW + 4 * u : VSC_ROW + 4 * (u + 1), :])
+            nc.sync.dma_start(vsc_plane[32 * u : 32 * u + 4, :], vsc_got[16 * u : 16 * (u + 1) : 4, :])
 
-        q_bf = sb.tile([P, PASSES, NQ, PACK], BF16, name="q_bf", align_bytes=64)
+        vs_got = sb.tile([P, N], F32, name="vs_got")
+        nc.vector.tensor_copy(vs_got[:], vs_win[:].indirect(offs_sb[:]))
+
+        q_bf = shared.tile([P, PASSES, NQ, PACK], BF16, name="q_bf", align_bytes=64, offset=34816)
         for o in range(PASSES):
             nc.scalar.copy(
                 q_bf[:, o].rearrange("p (c i) j -> p c j i", i=4),
-                q_raws[o][:].rearrange("p j (c i) -> p c j i", i=4),
+                q_raw[:, o].rearrange("p (j c i) -> p c j i", j=PACK, i=4),
             )
-        vs_last = shared.tile([P, POOL_PAGES], F32, name="vs_last", offset=4096)
-        nc.scalar.copy(vs_last[:], turned[PACK - 1])
-        nc.scalar.copy(vs_places[:, PACK - 1], vs_last[:].unsqueeze(2).to_broadcast([P, POOL_PAGES, NQ]))
         q_codes = sb.tile([P, PASSES * NQ], U32, name="q_codes", align_bytes=64)
         q_scales = sb.tile([P, PASSES * NQ], U8, name="q_scales", align_bytes=64)
         nc.vector.quantize_mx(out=q_codes[:].bitcast(FP8X4), scales=q_scales[:], in_=q_bf[:].rearrange("p o q j -> p (o q j)"))
@@ -137,17 +135,17 @@ def tile_attend_pkv4_sigmoid_bias_kernel(tc, qT, k_words, k_scales, v_words, v_s
             kw_got = kw_pages[g]
             prob = sb.tile([P, PACK, NQ], F32, name="prob%d" % g)
             for half in range(2):
-                keys = shared.tile([P, PASSES * 2 * P * 2], U8, name="keys%d" % (2 * g + half), align_bytes=64, offset=(8192, 4160)[g] + 1024 * half)
+                keys = sb.tile([P, PASSES * 2 * P * 2], U8, name="keys%d" % (2 * g + half), align_bytes=64)
                 nc.vector.tensor_copy(
                     keys[:].bitcast(U16).rearrange("p (o u m) -> p o m u", o=PASSES, u=2),
                     kw_got[:].bitcast(U16).rearrange("p (m t o) -> p o m t", t=PACK, o=PASSES)[:, :, :, 2 * half : 2 * half + 2],
                 )
-                score = ps.tile([P, 2, NQ], F32, name="score%d" % (2 * g + half), tag="bank%d" % (2 * g + half))
                 for u in range(2):
                     t = 2 * half + u
+                    score = ps.tile([P, NQ], F32, name="score%d" % (PACK * g + t), tag="bank%d" % (PACK * g + t))
                     for o in range(PASSES):
                         nc.tensor.matmul_mx(
-                            out=score[:, u, :],
+                            out=score[:],
                             lhsT=keys[:, (o * 2 + u) * 2 * P : (o * 2 + u + 1) * 2 * P].bitcast(FP4X4),
                             lhsT_scale=ks_planes[o][:, g * PAGE + t * P : g * PAGE + (t + 1) * P],
                             rhs=q_codes[:, o * NQ : (o + 1) * NQ].bitcast(FP8X4),
@@ -155,28 +153,25 @@ def tile_attend_pkv4_sigmoid_bias_kernel(tc, qT, k_words, k_scales, v_words, v_s
                             start=(o == 0),
                             stop=(o == PASSES - 1),
                         )
-                for u in range(2):
-                    t = 2 * half + u
-                    nc.scalar.activation(prob[:, t, :], score[:, u, :], SIGMOID, bias=kb_col[:, g, t : t + 1])
+                    first = g * PAGE + t * P
+                    nc.scalar.activation(prob[:, t, :], score[:], SIGMOID, bias=kb_got[:, first : first + 1])
             probs.append(prob)
 
-        vs_got = sb.tile([P, PAGES, PAGE], F32, name="vs_got")
-        for g in range(PAGES):
-            cols = slice(g * PAGE // 16, (g + 1) * PAGE // 16)
-            nc.vector.tensor_copy(vs_got[:, g], vs_win[:].indirect(offs_sb[:, cols]))
-
-        vw_got = sb.tile([P, PAGES * DV], U32, name="vw_got", align_bytes=64)
-        nc.vector.tensor_copy(vw_got[:], vw_win[:].bitcast(U32).indirect(voffs_sb[:]))
-        w_bfs = []
-        for g in range(PAGES):
-            w_bf = shared.tile([P, NQ, PACK], BF16, name="w_bf%d" % g, align_bytes=64, offset=(20480, 16896)[g])
-            (nc.gpsimd, nc.vector)[g].tensor_tensor(
+        def weigh(g, offset):
+            w_bf = shared.tile([P, NQ, PACK], BF16, name="w_bf%d" % g, align_bytes=64, offset=offset)
+            scale = vs_got[:, g * PAGE : (g + 1) * PAGE].rearrange("p (t x) -> p t x", t=PACK)[:, :, 0:4]
+            nc.vector.tensor_tensor(
                 w_bf[:].rearrange("p (c i) t -> p c t i", i=4),
                 probs[g][:].rearrange("p t (c i) -> p c t i", i=4),
-                vs_got[:, g].rearrange("p (t c i) -> p c t i", t=PACK, i=4),
+                scale.unsqueeze(1).to_broadcast([P, NQ // 4, PACK, 4]),
                 MULT,
             )
-            w_bfs.append(w_bf)
+            return w_bf
+
+        w_bfs = [weigh(0, 20480)]
+        vw_got = sb.tile([P, PAGES * DV], U32, name="vw_got", align_bytes=64)
+        nc.vector.tensor_copy(vw_got[:], vw_win[:].bitcast(U32).indirect(voffs_sb[:]))
+        w_bfs.append(weigh(1, 16896))
         weights = []
         for g in range(PAGES):
             w_codes = shared.tile([P, NQ], U32, name="w_codes%d" % g, align_bytes=64, offset=(16384, 22528)[g])
@@ -184,7 +179,7 @@ def tile_attend_pkv4_sigmoid_bias_kernel(tc, qT, k_words, k_scales, v_words, v_s
             nc.vector.quantize_mx(out=w_codes[:].bitcast(FP8X4), scales=w_scales[:], in_=w_bfs[g][:].rearrange("p q t -> p (q t)"))
             weights.append((w_codes, w_scales))
 
-        y = ps.tile([P, DV], F32, name="y")
+        y = ps.tile([P, DV], F32, name="y", tag="bank0")
         for g in range(PAGES):
             w_codes, w_scales = weights[g]
             nc.tensor.matmul_mx(

@@ -24,8 +24,9 @@ POOL_PAGES = T // PAGE
 PASSES = D // (P * PACK)
 BLOCKS = POOL_PAGES * PACK
 KS_ROW = P - 16 * PASSES
-KB_FILL = 40
-VS_FILL = 40
+KB_FILL = 32
+KB_HEAD = 8
+VS_FILL = 88
 
 FLOPS = 2 * NQ * N * D + 2 * NQ * N * DV
 BYTES = 4 * D * NQ + 4 * P * T + 32 * T + 4 * P * POOL_PAGES * DV + 16 * POOL_PAGES * DV + 8 * T + 2 * P * (N + PAGES * DV) // 16 + 4 * NQ * DV
@@ -41,58 +42,69 @@ def tile_attend_pkv4_sigmoid_bias_kernel(tc, qT, k_words, k_scales, v_words, v_s
 
         offs_sb = lists.tile([P, N // 16], U16, name="offs_sb")
         voffs_sb = lists.tile([P, PAGES * DV // 16], U16, name="voffs_sb")
-        kb_rows = sb.tile([P, PAGE], F32, name="kb_rows")
-        vs_rows = shared.tile([P, PAGE], F32, name="vs_rows", offset=34816)
         vsc_win = sb.tile([P, POOL_PAGES * DV // 4], I32, name="vsc_win")
+        kb_rows = shared.tile([P, PAGE], F32, name="kb_rows", offset=0)
+        vs_rows = sb.tile([P, PAGE], F32, name="vs_rows")
         ks_win = sb.tile([P, T // 4], I32, name="ks_win")
-        kb_win = shared.tile([P, T], F32, name="kb_win", offset=0)
-        vs_win = sb.tile([P, T], F32, name="vs_win")
+        kb_win = sb.tile([P, T], F32, name="kb_win")
         kb_blocks = kb_win[:].rearrange("p (b x) -> p b x", b=BLOCKS)
-        vs_blocks = vs_win[:].rearrange("p (b x) -> p b x", b=BLOCKS)
 
+        nc.vector.memset(vsc_win[:], 0)
         nc.vector.memset(kb_rows[:], 0.0)
         nc.vector.memset(vs_rows[:], 0.0)
-        nc.vector.memset(vsc_win[:], 0)
         nc.vector.memset(ks_win[0:KS_ROW, :], 0)
-        nc.vector.memset(kb_blocks[:, :, KB_FILL:P], 0.0)
-        nc.vector.memset(vs_blocks[:, 0:2, VS_FILL:P], 0.0)
+        nc.vector.memset(kb_blocks[:, 0:KB_HEAD, KB_FILL:P], 0.0)
 
-        nc.sync.dma_start(offs_sb[:], offs)
-        nc.sync.dma_start(ks_win[KS_ROW:P, :], k_scales.rearrange("o f t -> f o t").bitcast(I32))
-        for rows, table in ((kb_rows, kb), (vs_rows, vs)):
-            shifted = table.rearrange("r x -> (r x)")[0 : PACK * (T + 1)].rearrange("(t y) -> t y", t=PACK)[:, 0:T]
-            nc.sync.dma_start(rows[0:P:4, :], shifted.rearrange("t (u x) -> u t x", u=POOL_PAGES))
         nc.sync.dma_start(voffs_sb[:], voffs)
+        nc.sync.dma_start(offs_sb[:], offs)
         nc.sync.dma_start(
             vsc_win[0:64:4, :].rearrange("p (g e) -> p g e", g=POOL_PAGES),
             v_scales.rearrange("g f e -> f g e").bitcast(I32),
         )
-        q_raw = sb.tile([P, PASSES, PACK * NQ], F32, name="q_raw")
-        nc.sync.dma_start(q_raw[:], qT[0].rearrange("(o p j) q -> p o (j q)", o=PASSES, j=PACK))
+
+        def load_rows(rows, table):
+            shifted = table.rearrange("r x -> (r x)")[0 : PACK * (T + 1)].rearrange("(t y) -> t y", t=PACK)[:, 0:T]
+            nc.sync.dma_start(rows[0:P:4, :], shifted.rearrange("t (u x) -> u t x", u=POOL_PAGES))
+
+        load_rows(kb_rows, kb)
+        nc.sync.dma_start(ks_win[KS_ROW:P, :], k_scales.rearrange("o f t -> f o t").bitcast(I32))
+        load_rows(vs_rows, vs)
         kw_win = sb.tile([P, T], I32, name="kw_win")
         nc.sync.dma_start(kw_win[:], k_words[0].rearrange("p t b -> p (t b)").bitcast(I32))
+        q_rows = qT[0].rearrange("(o p j) q -> o p j q", o=PASSES, j=PACK)
+        q_raws = []
+        for o in range(PASSES):
+            q_raw = shared.tile([P, PACK, NQ], F32, name="q_raw%d" % o, offset=(18432, 24576)[o])
+            nc.sync.dma_start(q_raw[:], q_rows[o])
+            q_raws.append(q_raw)
 
         ident = sb.tile([P, P], F32, name="ident")
         make_identity(nc, ident[:])
-        nc.gpsimd.memset(vs_blocks[:, 1:BLOCKS, VS_FILL:P], 0.0)
-        warm = sb.tile([96, 8], F32, name="warm")
-        nc.scalar.activation(warm[64:96, :], ident[64:96, 0:8], SIGMOID)
+        nc.gpsimd.memset(kb_blocks[:, KB_HEAD - 1 : BLOCKS, KB_FILL:P], 0.0)
+        warm = sb.tile([32, 8], F32, name="warm")
+        nc.scalar.activation(warm[:], ident[0:32, 0:8], SIGMOID)
 
-        for rows, blocks, fill, tag in ((kb_rows, kb_blocks, KB_FILL, "bank6"), (vs_rows, vs_blocks, VS_FILL, "bank7")):
-            turned = ps.tile([P, P], F32, name="turned", tag=tag)
-            nc.tensor.transpose(turned[:], rows[:, 0:PAGE:PACK], ident[:])
-            nc.scalar.copy(
-                blocks[:, :, 0:fill],
-                turned[:].rearrange("p (b r) -> p b r", r=4)[:, :, 0:1].to_broadcast([P, BLOCKS, fill]),
-            )
+        kb_turned = ps.tile([P, P], F32, name="kb_turned", tag="bank6")
+        nc.tensor.transpose(kb_turned[:], kb_rows[:, 0:PAGE:PACK], ident[:])
+        vs_turned = ps.tile([P, P], F32, name="vs_turned", tag="bank7")
+        nc.tensor.transpose(vs_turned[:], vs_rows[:, 0:PAGE:PACK], ident[:])
+        kb_cols = shared.tile([P, BLOCKS], F32, name="kb_cols", offset=32768)
+        nc.scalar.copy(kb_cols[:], kb_turned[:, 0:P:4])
+        vs_cols = sb.tile([P, BLOCKS], F32, name="vs_cols")
+        nc.scalar.copy(vs_cols[:], vs_turned[:, 0:P:4])
+        nc.scalar.copy(kb_blocks[:, :, 0:KB_FILL], kb_cols[:].unsqueeze(2).to_broadcast([P, BLOCKS, KB_FILL]))
+        vs_win = shared.tile([P, T], F32, name="vs_win", offset=0)
+        vs_blocks = vs_win[:].rearrange("p (b x) -> p b x", b=BLOCKS)
+        nc.gpsimd.memset(vs_blocks[:, :, VS_FILL:P], 0.0)
+        nc.scalar.copy(vs_blocks[:, :, 0:VS_FILL], vs_cols[:].unsqueeze(2).to_broadcast([P, BLOCKS, VS_FILL]))
 
-        ks_got = shared.tile([P, N], U8, name="ks_got", offset=24576)
+        vsc_got = shared.tile([P, PAGES * DV // 4], I32, name="vsc_got", offset=16640)
+        nc.vector.tensor_copy(vsc_got[:].bitcast(U8), vsc_win[:].bitcast(U8).indirect(voffs_sb[:]))
+        ks_got = shared.tile([P, N], U8, name="ks_got", offset=38912)
         nc.vector.tensor_copy(ks_got[:], ks_win[:].bitcast(U8).indirect(offs_sb[:]))
         kb_got = sb.tile([P, N], F32, name="kb_got")
         nc.vector.tensor_copy(kb_got[:], kb_win[:].indirect(offs_sb[:]))
-        vsc_got = shared.tile([P, PAGES * DV // 4], I32, name="vsc_got", offset=16640)
-        nc.vector.tensor_copy(vsc_got[:].bitcast(U8), vsc_win[:].bitcast(U8).indirect(voffs_sb[:]))
-        ks_dealt = shared.tile([P, N // 4], I32, name="ks_dealt", offset=0)
+        ks_dealt = shared.tile([P, N // 4], I32, name="ks_dealt", offset=31808)
         nc.vector.tensor_copy(
             ks_dealt[:].bitcast(U8).rearrange("p (g t m) -> p g t m", g=PAGES, t=PACK),
             ks_got[:].rearrange("p (g m t) -> p g t m", g=PAGES, t=PACK),
@@ -102,43 +114,38 @@ def tile_attend_pkv4_sigmoid_bias_kernel(tc, qT, k_words, k_scales, v_words, v_s
             nc.sync.dma_start(ks_plane[32 * u : 32 * u + 4, :], ks_dealt[KS_ROW + 8 * u : KS_ROW + 8 * (u + 1), :])
         ks_planes = [ks_plane[:].bitcast(U8)[:, o * N : (o + 1) * N] for o in range(PASSES)]
 
-        vw_win = shared.tile([P, POOL_PAGES * DV], I32, name="vw_win", offset=25088)
+        vw_win = shared.tile([P, POOL_PAGES * DV], I32, name="vw_win", offset=39424)
         nc.sync.dma_start(
             vw_win[:].rearrange("p (g e) -> p g e", g=POOL_PAGES),
             v_words.rearrange("g p e b -> p g (e b)").bitcast(I32),
         )
-        vsc_plane = shared.tile([P, PAGES * DV // 4], I32, name="vsc_plane", align_bytes=64, offset=24576)
+        vsc_plane = shared.tile([P, PAGES * DV // 4], I32, name="vsc_plane", align_bytes=64, offset=38912)
         for u in range(4):
             nc.sync.dma_start(vsc_plane[32 * u : 32 * u + 4, :], vsc_got[16 * u : 16 * (u + 1) : 4, :])
 
-        vs_got = sb.tile([P, N], F32, name="vs_got")
-        nc.vector.tensor_copy(vs_got[:], vs_win[:].indirect(offs_sb[:]))
+        kw_got = shared.tile([P, N], U32, name="kw_got", offset=32832)
+        nc.vector.tensor_copy(kw_got[:], kw_win[:].bitcast(U32).indirect(offs_sb[:]))
 
-        q_bf = shared.tile([P, PASSES, NQ, PACK], BF16, name="q_bf", align_bytes=64, offset=34816)
+        q_bf = sb.tile([P, PASSES, NQ, PACK], BF16, name="q_bf", align_bytes=64)
         for o in range(PASSES):
             nc.scalar.copy(
                 q_bf[:, o].rearrange("p (c i) j -> p c j i", i=4),
-                q_raw[:, o].rearrange("p (j c i) -> p c j i", j=PACK, i=4),
+                q_raws[o][:].rearrange("p j (c i) -> p c j i", i=4),
             )
         q_codes = sb.tile([P, PASSES * NQ], U32, name="q_codes", align_bytes=64)
         q_scales = sb.tile([P, PASSES * NQ], U8, name="q_scales", align_bytes=64)
         nc.vector.quantize_mx(out=q_codes[:].bitcast(FP8X4), scales=q_scales[:], in_=q_bf[:].rearrange("p o q j -> p (o q j)"))
 
-        kw_pages = []
-        for g in range(PAGES):
-            kw_got = sb.tile([P, PAGE], U32, name="kw_got%d" % g)
-            cols = slice(g * PAGE // 16, (g + 1) * PAGE // 16)
-            nc.vector.tensor_copy(kw_got[:], kw_win[:].bitcast(U32).indirect(offs_sb[:, cols]))
-            kw_pages.append(kw_got)
+        all_keys = shared.tile([P, 4 * PASSES * 2 * P * 2], U8, name="all_keys", align_bytes=64, offset=20544)
         probs = []
         for g in range(PAGES):
-            kw_got = kw_pages[g]
+            kw_page = kw_got[:, g * PAGE : (g + 1) * PAGE]
             prob = sb.tile([P, PACK, NQ], F32, name="prob%d" % g)
             for half in range(2):
-                keys = sb.tile([P, PASSES * 2 * P * 2], U8, name="keys%d" % (2 * g + half), align_bytes=64)
+                keys = all_keys[:, (2 * g + half) * 1024 : (2 * g + half + 1) * 1024]
                 nc.vector.tensor_copy(
-                    keys[:].bitcast(U16).rearrange("p (o u m) -> p o m u", o=PASSES, u=2),
-                    kw_got[:].bitcast(U16).rearrange("p (m t o) -> p o m t", t=PACK, o=PASSES)[:, :, :, 2 * half : 2 * half + 2],
+                    keys.bitcast(U16).rearrange("p (o u m) -> p o m u", o=PASSES, u=2),
+                    kw_page.bitcast(U16).rearrange("p (m t o) -> p o m t", t=PACK, o=PASSES)[:, :, :, 2 * half : 2 * half + 2],
                 )
                 for u in range(2):
                     t = 2 * half + u
@@ -157,24 +164,30 @@ def tile_attend_pkv4_sigmoid_bias_kernel(tc, qT, k_words, k_scales, v_words, v_s
                     nc.scalar.activation(prob[:, t, :], score[:], SIGMOID, bias=kb_got[:, first : first + 1])
             probs.append(prob)
 
-        def weigh(g, offset):
-            w_bf = shared.tile([P, NQ, PACK], BF16, name="w_bf%d" % g, align_bytes=64, offset=offset)
-            scale = vs_got[:, g * PAGE : (g + 1) * PAGE].rearrange("p (t x) -> p t x", t=PACK)[:, :, 0:4]
-            nc.vector.tensor_tensor(
-                w_bf[:].rearrange("p (c i) t -> p c t i", i=4),
-                probs[g][:].rearrange("p t (c i) -> p c t i", i=4),
-                scale.unsqueeze(1).to_broadcast([P, NQ // 4, PACK, 4]),
-                MULT,
-            )
-            return w_bf
-
-        w_bfs = [weigh(0, 20480)]
+        vs_got = shared.tile([P, PAGES, PAGE], F32, name="vs_got", offset=24640)
+        for g in range(PAGES):
+            cols = slice(g * PAGE // 16, (g + 1) * PAGE // 16)
+            nc.vector.tensor_copy(vs_got[:, g], vs_win[:].indirect(offs_sb[:, cols]))
         vw_got = sb.tile([P, PAGES * DV], U32, name="vw_got", align_bytes=64)
         nc.vector.tensor_copy(vw_got[:], vw_win[:].bitcast(U32).indirect(voffs_sb[:]))
-        w_bfs.append(weigh(1, 16896))
+
+        w_bfs = [sb.tile([P, NQ, PACK], BF16, name="w_bf%d" % g, align_bytes=64) for g in range(PAGES)]
+        nc.gpsimd.tensor_tensor(
+            w_bfs[0][:].rearrange("p (c i) t -> p c t i", i=4),
+            probs[0][:].rearrange("p t (c i) -> p c t i", i=4),
+            vs_got[:, 0].rearrange("p (t x) -> p t x", t=PACK)[:, :, 0:4].unsqueeze(1).to_broadcast([P, NQ // 4, PACK, 4]),
+            MULT,
+        )
+        w_rows = sb.tile([P, PACK, NQ], BF16, name="w_rows")
+        for t in range(PACK):
+            nc.scalar.activation(w_rows[:, t, :], probs[1][:, t, :], COPY, scale=vs_got[:, 1, t * P : t * P + 1])
+        nc.scalar.copy(
+            w_bfs[1][:].rearrange("p (c i) t -> p c t i", i=4),
+            w_rows[:].rearrange("p t (c i) -> p c t i", i=4),
+        )
         weights = []
         for g in range(PAGES):
-            w_codes = shared.tile([P, NQ], U32, name="w_codes%d" % g, align_bytes=64, offset=(16384, 22528)[g])
+            w_codes = shared.tile([P, NQ], U32, name="w_codes%d" % g, align_bytes=64, offset=(16384, 16896)[g])
             w_scales = sb.tile([P, NQ], U8, name="w_scales%d" % g, align_bytes=64)
             nc.vector.quantize_mx(out=w_codes[:].bitcast(FP8X4), scales=w_scales[:], in_=w_bfs[g][:].rearrange("p q t -> p (q t)"))
             weights.append((w_codes, w_scales))

@@ -24,9 +24,9 @@ POOL_PAGES = T // PAGE
 PASSES = D // (P * PACK)
 BLOCKS = POOL_PAGES * PACK
 KS_ROW = P - 16 * PASSES
-KB_FILL = 32
-KB_HEAD = 8
-VS_FILL = 88
+KB_FILL = 48
+KB_HEAD = 16
+VS_FILL = 72
 
 FLOPS = 2 * NQ * N * D + 2 * NQ * N * DV
 BYTES = 4 * D * NQ + 4 * P * T + 32 * T + 4 * P * POOL_PAGES * DV + 16 * POOL_PAGES * DV + 8 * T + 2 * P * (N + PAGES * DV) // 16 + 4 * NQ * DV
@@ -43,38 +43,37 @@ def tile_attend_pkv4_sigmoid_bias_kernel(tc, qT, k_words, k_scales, v_words, v_s
         offs_sb = lists.tile([P, N // 16], U16, name="offs_sb")
         voffs_sb = lists.tile([P, PAGES * DV // 16], U16, name="voffs_sb")
         vsc_win = sb.tile([P, POOL_PAGES * DV // 4], I32, name="vsc_win")
-        kb_rows = shared.tile([P, PAGE], F32, name="kb_rows", offset=0)
+        kb_rows = sb.tile([P, PAGE], F32, name="kb_rows")
         vs_rows = sb.tile([P, PAGE], F32, name="vs_rows")
         ks_win = sb.tile([P, T // 4], I32, name="ks_win")
         kb_win = sb.tile([P, T], F32, name="kb_win")
         kb_blocks = kb_win[:].rearrange("p (b x) -> p b x", b=BLOCKS)
 
         nc.vector.memset(vsc_win[:], 0)
-        nc.vector.memset(kb_rows[:], 0.0)
         nc.vector.memset(vs_rows[:], 0.0)
+        nc.vector.memset(kb_rows[0:KS_ROW, :], 0.0)
         nc.vector.memset(ks_win[0:KS_ROW, :], 0)
         nc.vector.memset(kb_blocks[:, 0:KB_HEAD, KB_FILL:P], 0.0)
 
-        nc.sync.dma_start(voffs_sb[:], voffs)
+        def shifted_rows(table):
+            shifted = table.rearrange("r x -> (r x)")[0 : PACK * (T + 1)].rearrange("(t y) -> t y", t=PACK)[:, 0:T]
+            return shifted.rearrange("t (u x) -> u t x", u=POOL_PAGES)
+
+        nc.scalar.dma_start(ks_win[KS_ROW:P, :], k_scales.rearrange("o f t -> f o t").bitcast(I32))
+        nc.scalar.dma_start(kb_rows[KS_ROW:P, :], shifted_rows(kb))
         nc.sync.dma_start(offs_sb[:], offs)
+        nc.sync.dma_start(voffs_sb[:], voffs)
         nc.sync.dma_start(
             vsc_win[0:64:4, :].rearrange("p (g e) -> p g e", g=POOL_PAGES),
             v_scales.rearrange("g f e -> f g e").bitcast(I32),
         )
-
-        def load_rows(rows, table):
-            shifted = table.rearrange("r x -> (r x)")[0 : PACK * (T + 1)].rearrange("(t y) -> t y", t=PACK)[:, 0:T]
-            nc.sync.dma_start(rows[0:P:4, :], shifted.rearrange("t (u x) -> u t x", u=POOL_PAGES))
-
-        load_rows(kb_rows, kb)
-        nc.sync.dma_start(ks_win[KS_ROW:P, :], k_scales.rearrange("o f t -> f o t").bitcast(I32))
-        load_rows(vs_rows, vs)
-        kw_win = sb.tile([P, T], I32, name="kw_win")
+        nc.sync.dma_start(vs_rows[0:64:2, :], shifted_rows(vs))
+        kw_win = shared.tile([P, T], I32, name="kw_win", offset=66560)
         nc.sync.dma_start(kw_win[:], k_words[0].rearrange("p t b -> p (t b)").bitcast(I32))
         q_rows = qT[0].rearrange("(o p j) q -> o p j q", o=PASSES, j=PACK)
         q_raws = []
         for o in range(PASSES):
-            q_raw = shared.tile([P, PACK, NQ], F32, name="q_raw%d" % o, offset=(18432, 24576)[o])
+            q_raw = shared.tile([P, PACK, NQ], F32, name="q_raw%d" % o, offset=(18432, 83968)[o])
             nc.sync.dma_start(q_raw[:], q_rows[o])
             q_raws.append(q_raw)
 
@@ -89,105 +88,105 @@ def tile_attend_pkv4_sigmoid_bias_kernel(tc, qT, k_words, k_scales, v_words, v_s
         vs_turned = ps.tile([P, P], F32, name="vs_turned", tag="bank7")
         nc.tensor.transpose(vs_turned[:], vs_rows[:, 0:PAGE:PACK], ident[:])
         kb_cols = shared.tile([P, BLOCKS], F32, name="kb_cols", offset=32768)
-        nc.scalar.copy(kb_cols[:], kb_turned[:, 0:P:4])
-        vs_cols = sb.tile([P, BLOCKS], F32, name="vs_cols")
-        nc.scalar.copy(vs_cols[:], vs_turned[:, 0:P:4])
+        nc.scalar.copy(kb_cols[:], kb_turned[:, KS_ROW:P])
+        vs_cols = shared.tile([P, BLOCKS], F32, name="vs_cols", offset=20480)
+        nc.scalar.copy(vs_cols[:], vs_turned[:, 0:64:2])
         nc.scalar.copy(kb_blocks[:, :, 0:KB_FILL], kb_cols[:].unsqueeze(2).to_broadcast([P, BLOCKS, KB_FILL]))
-        vs_win = shared.tile([P, T], F32, name="vs_win", offset=0)
-        vs_blocks = vs_win[:].rearrange("p (b x) -> p b x", b=BLOCKS)
-        nc.gpsimd.memset(vs_blocks[:, :, VS_FILL:P], 0.0)
-        nc.scalar.copy(vs_blocks[:, :, 0:VS_FILL], vs_cols[:].unsqueeze(2).to_broadcast([P, BLOCKS, VS_FILL]))
 
+        ks_got = shared.tile([P, N], U8, name="ks_got", offset=57344)
+        nc.vector.tensor_copy(ks_got[:], ks_win[:].bitcast(U8).indirect(offs_sb[:]))
         vsc_got = shared.tile([P, PAGES * DV // 4], I32, name="vsc_got", offset=16640)
         nc.vector.tensor_copy(vsc_got[:].bitcast(U8), vsc_win[:].bitcast(U8).indirect(voffs_sb[:]))
-        ks_got = shared.tile([P, N], U8, name="ks_got", offset=38912)
-        nc.vector.tensor_copy(ks_got[:], ks_win[:].bitcast(U8).indirect(offs_sb[:]))
-        kb_got = sb.tile([P, N], F32, name="kb_got")
-        nc.vector.tensor_copy(kb_got[:], kb_win[:].indirect(offs_sb[:]))
-        ks_dealt = shared.tile([P, N // 4], I32, name="ks_dealt", offset=31808)
+        ks_dealt = sb.tile([P, N // 4], I32, name="ks_dealt")
         nc.vector.tensor_copy(
             ks_dealt[:].bitcast(U8).rearrange("p (g t m) -> p g t m", g=PAGES, t=PACK),
             ks_got[:].rearrange("p (g m t) -> p g t m", g=PAGES, t=PACK),
         )
+        kb_got = sb.tile([P, N], F32, name="kb_got")
+        nc.vector.tensor_copy(kb_got[:], kb_win[:].indirect(offs_sb[:]))
+        vs_win = shared.tile([P, T], F32, name="vs_win", offset=41024)
+        vs_blocks = vs_win[:].rearrange("p (b x) -> p b x", b=BLOCKS)
+        nc.gpsimd.memset(vs_blocks[:, :, VS_FILL:P], 0.0)
+        nc.scalar.copy(vs_blocks[:, :, 0:VS_FILL], vs_cols[:].unsqueeze(2).to_broadcast([P, BLOCKS, VS_FILL]))
         ks_plane = sb.tile([P, PASSES * N // 4], I32, name="ks_plane", align_bytes=64)
         for u in range(4):
             nc.sync.dma_start(ks_plane[32 * u : 32 * u + 4, :], ks_dealt[KS_ROW + 8 * u : KS_ROW + 8 * (u + 1), :])
         ks_planes = [ks_plane[:].bitcast(U8)[:, o * N : (o + 1) * N] for o in range(PASSES)]
 
-        vw_win = shared.tile([P, POOL_PAGES * DV], I32, name="vw_win", offset=39424)
+        vw_win = shared.tile([P, POOL_PAGES * DV], I32, name="vw_win", offset=57920)
         nc.sync.dma_start(
             vw_win[:].rearrange("p (g e) -> p g e", g=POOL_PAGES),
             v_words.rearrange("g p e b -> p g (e b)").bitcast(I32),
         )
-        vsc_plane = shared.tile([P, PAGES * DV // 4], I32, name="vsc_plane", align_bytes=64, offset=38912)
+        vsc_plane = shared.tile([P, PAGES * DV // 4], I32, name="vsc_plane", align_bytes=64, offset=57408)
         for u in range(4):
             nc.sync.dma_start(vsc_plane[32 * u : 32 * u + 4, :], vsc_got[16 * u : 16 * (u + 1) : 4, :])
 
-        kw_got = shared.tile([P, N], U32, name="kw_got", offset=32832)
-        nc.vector.tensor_copy(kw_got[:], kw_win[:].bitcast(U32).indirect(offs_sb[:]))
+        kw_pages = []
+        for g in range(PAGES):
+            kw_got = shared.tile([P, PAGE], U32, name="kw_got%d" % g, offset=(30784, 32832)[g])
+            cols = slice(g * PAGE // 16, (g + 1) * PAGE // 16)
+            nc.vector.tensor_copy(kw_got[:], kw_win[:].bitcast(U32).indirect(offs_sb[:, cols]))
+            kw_pages.append(kw_got)
 
-        q_bf = sb.tile([P, PASSES, NQ, PACK], BF16, name="q_bf", align_bytes=64)
+        q_bf = shared.tile([P, PASSES, NQ, PACK], BF16, name="q_bf", align_bytes=64, offset=20480)
         for o in range(PASSES):
             nc.scalar.copy(
                 q_bf[:, o].rearrange("p (c i) j -> p c j i", i=4),
                 q_raws[o][:].rearrange("p j (c i) -> p c j i", i=4),
             )
-        q_codes = sb.tile([P, PASSES * NQ], U32, name="q_codes", align_bytes=64)
+        q_codes = shared.tile([P, PASSES * NQ], U32, name="q_codes", align_bytes=64, offset=66560)
         q_scales = sb.tile([P, PASSES * NQ], U8, name="q_scales", align_bytes=64)
         nc.vector.quantize_mx(out=q_codes[:].bitcast(FP8X4), scales=q_scales[:], in_=q_bf[:].rearrange("p o q j -> p (o q j)"))
 
-        all_keys = shared.tile([P, 4 * PASSES * 2 * P * 2], U8, name="all_keys", align_bytes=64, offset=20544)
         probs = []
         for g in range(PAGES):
-            kw_page = kw_got[:, g * PAGE : (g + 1) * PAGE]
+            page_keys = shared.tile([P, 2048], U8, name="page_keys%d" % g, align_bytes=64, offset=(4096, 82432)[g])
+            page_words = kw_pages[g][:].bitcast(U16).rearrange("p (m t o) -> p o m t", t=PACK, o=PASSES)
             prob = sb.tile([P, PACK, NQ], F32, name="prob%d" % g)
             for half in range(2):
-                keys = all_keys[:, (2 * g + half) * 1024 : (2 * g + half + 1) * 1024]
+                keys = page_keys[:, half * 1024 : (half + 1) * 1024]
                 nc.vector.tensor_copy(
                     keys.bitcast(U16).rearrange("p (o u m) -> p o m u", o=PASSES, u=2),
-                    kw_page.bitcast(U16).rearrange("p (m t o) -> p o m t", t=PACK, o=PASSES)[:, :, :, 2 * half : 2 * half + 2],
+                    page_words[:, :, :, 2 * half : 2 * half + 2],
                 )
                 for u in range(2):
                     t = 2 * half + u
+                    first = g * PAGE + t * P
                     score = ps.tile([P, NQ], F32, name="score%d" % (PACK * g + t), tag="bank%d" % (PACK * g + t))
                     for o in range(PASSES):
                         nc.tensor.matmul_mx(
                             out=score[:],
                             lhsT=keys[:, (o * 2 + u) * 2 * P : (o * 2 + u + 1) * 2 * P].bitcast(FP4X4),
-                            lhsT_scale=ks_planes[o][:, g * PAGE + t * P : g * PAGE + (t + 1) * P],
+                            lhsT_scale=ks_planes[o][:, first : first + P],
                             rhs=q_codes[:, o * NQ : (o + 1) * NQ].bitcast(FP8X4),
                             rhs_scale=q_scales[:, o * NQ : (o + 1) * NQ],
                             start=(o == 0),
                             stop=(o == PASSES - 1),
                         )
-                    first = g * PAGE + t * P
                     nc.scalar.activation(prob[:, t, :], score[:], SIGMOID, bias=kb_got[:, first : first + 1])
             probs.append(prob)
 
-        vs_got = shared.tile([P, PAGES, PAGE], F32, name="vs_got", offset=24640)
+        vs_got = shared.tile([P, PAGES, PAGE], F32, name="vs_got", offset=22464)
         for g in range(PAGES):
             cols = slice(g * PAGE // 16, (g + 1) * PAGE // 16)
             nc.vector.tensor_copy(vs_got[:, g], vs_win[:].indirect(offs_sb[:, cols]))
-        vw_got = sb.tile([P, PAGES * DV], U32, name="vw_got", align_bytes=64)
+        vw_got = shared.tile([P, PAGES * DV], U32, name="vw_got", align_bytes=64, offset=34816)
         nc.vector.tensor_copy(vw_got[:], vw_win[:].bitcast(U32).indirect(voffs_sb[:]))
 
-        w_bfs = [sb.tile([P, NQ, PACK], BF16, name="w_bf%d" % g, align_bytes=64) for g in range(PAGES)]
-        nc.gpsimd.tensor_tensor(
-            w_bfs[0][:].rearrange("p (c i) t -> p c t i", i=4),
-            probs[0][:].rearrange("p t (c i) -> p c t i", i=4),
-            vs_got[:, 0].rearrange("p (t x) -> p t x", t=PACK)[:, :, 0:4].unsqueeze(1).to_broadcast([P, NQ // 4, PACK, 4]),
-            MULT,
-        )
-        w_rows = sb.tile([P, PACK, NQ], BF16, name="w_rows")
-        for t in range(PACK):
-            nc.scalar.activation(w_rows[:, t, :], probs[1][:, t, :], COPY, scale=vs_got[:, 1, t * P : t * P + 1])
-        nc.scalar.copy(
-            w_bfs[1][:].rearrange("p (c i) t -> p c t i", i=4),
-            w_rows[:].rearrange("p t (c i) -> p c t i", i=4),
-        )
+        w_bfs = []
+        for g in range(PAGES):
+            w_bf = shared.tile([P, NQ, PACK], BF16, name="w_bf%d" % g, align_bytes=64, offset=(0, 15680)[g])
+            (nc.gpsimd, nc.vector)[g].tensor_tensor(
+                w_bf[:].rearrange("p (c i) t -> p c t i", i=4),
+                probs[g][:].rearrange("p t (c i) -> p c t i", i=4),
+                vs_got[:, g].rearrange("p (t x) -> p t x", t=PACK)[:, :, 0:4].unsqueeze(1).to_broadcast([P, NQ // 4, PACK, 4]),
+                MULT,
+            )
+            w_bfs.append(w_bf)
         weights = []
         for g in range(PAGES):
-            w_codes = shared.tile([P, NQ], U32, name="w_codes%d" % g, align_bytes=64, offset=(16384, 16896)[g])
+            w_codes = shared.tile([P, NQ], U32, name="w_codes%d" % g, align_bytes=64, offset=(16896, 2048)[g])
             w_scales = sb.tile([P, NQ], U8, name="w_scales%d" % g, align_bytes=64)
             nc.vector.quantize_mx(out=w_codes[:].bitcast(FP8X4), scales=w_scales[:], in_=w_bfs[g][:].rearrange("p q t -> p (q t)"))
             weights.append((w_codes, w_scales))

@@ -27,6 +27,7 @@ KS_ROW = P - 16 * PASSES
 KB_FILL = 48
 KB_HEAD = 16
 VS_FILL = 72
+POOL_Q = 96
 
 FLOPS = 2 * NQ * N * D + 2 * NQ * N * DV
 BYTES = 4 * D * NQ + 4 * P * T + 32 * T + 4 * P * POOL_PAGES * DV + 16 * POOL_PAGES * DV + 8 * T + 2 * P * (N + PAGES * DV) // 16 + 4 * NQ * DV
@@ -73,7 +74,7 @@ def tile_attend_pkv4_sigmoid_bias_kernel(tc, qT, k_words, k_scales, v_words, v_s
         q_rows = qT[0].rearrange("(o p j) q -> o p j q", o=PASSES, j=PACK)
         q_raws = []
         for o in range(PASSES):
-            q_raw = shared.tile([P, PACK, NQ], F32, name="q_raw%d" % o, offset=(18432, 83968)[o])
+            q_raw = shared.tile([P, PACK, NQ], F32, name="q_raw%d" % o, offset=(8192, 82944)[o])
             nc.sync.dma_start(q_raw[:], q_rows[o])
             q_raws.append(q_raw)
 
@@ -89,7 +90,7 @@ def tile_attend_pkv4_sigmoid_bias_kernel(tc, qT, k_words, k_scales, v_words, v_s
         nc.tensor.transpose(vs_turned[:], vs_rows[:, 0:PAGE:PACK], ident[:])
         kb_cols = shared.tile([P, BLOCKS], F32, name="kb_cols", offset=32768)
         nc.scalar.copy(kb_cols[:], kb_turned[:, KS_ROW:P])
-        vs_cols = shared.tile([P, BLOCKS], F32, name="vs_cols", offset=20480)
+        vs_cols = shared.tile([P, BLOCKS], F32, name="vs_cols", offset=21440)
         nc.scalar.copy(vs_cols[:], vs_turned[:, 0:64:2])
         nc.scalar.copy(kb_blocks[:, :, 0:KB_FILL], kb_cols[:].unsqueeze(2).to_broadcast([P, BLOCKS, KB_FILL]))
 
@@ -129,43 +130,59 @@ def tile_attend_pkv4_sigmoid_bias_kernel(tc, qT, k_words, k_scales, v_words, v_s
             nc.vector.tensor_copy(kw_got[:], kw_win[:].bitcast(U32).indirect(offs_sb[:, cols]))
             kw_pages.append(kw_got)
 
-        q_bf = shared.tile([P, PASSES, NQ, PACK], BF16, name="q_bf", align_bytes=64, offset=20480)
+        q_bfs, q_ops = [], []
         for o in range(PASSES):
+            q_bf = shared.tile([P, NQ, PACK], BF16, name="q_bf%d" % o, align_bytes=64, offset=(20480, 21504)[o])
             nc.scalar.copy(
-                q_bf[:, o].rearrange("p (c i) j -> p c j i", i=4),
+                q_bf[:].rearrange("p (c i) j -> p c j i", i=4),
                 q_raws[o][:].rearrange("p j (c i) -> p c j i", i=4),
             )
-        q_codes = shared.tile([P, PASSES * NQ], U32, name="q_codes", align_bytes=64, offset=66560)
-        q_scales = sb.tile([P, PASSES * NQ], U8, name="q_scales", align_bytes=64)
-        nc.vector.quantize_mx(out=q_codes[:].bitcast(FP8X4), scales=q_scales[:], in_=q_bf[:].rearrange("p o q j -> p (o q j)"))
+            q_bfs.append(q_bf)
 
-        probs = []
-        for g in range(PAGES):
-            page_keys = shared.tile([P, 2048], U8, name="page_keys%d" % g, align_bytes=64, offset=(4096, 82432)[g])
-            page_words = kw_pages[g][:].bitcast(U16).rearrange("p (m t o) -> p o m t", t=PACK, o=PASSES)
-            prob = sb.tile([P, PACK, NQ], F32, name="prob%d" % g)
-            for half in range(2):
-                keys = page_keys[:, half * 1024 : (half + 1) * 1024]
-                nc.vector.tensor_copy(
-                    keys.bitcast(U16).rearrange("p (o u m) -> p o m u", o=PASSES, u=2),
-                    page_words[:, :, :, 2 * half : 2 * half + 2],
-                )
-                for u in range(2):
-                    t = 2 * half + u
-                    first = g * PAGE + t * P
-                    score = ps.tile([P, NQ], F32, name="score%d" % (PACK * g + t), tag="bank%d" % (PACK * g + t))
-                    for o in range(PASSES):
-                        nc.tensor.matmul_mx(
-                            out=score[:],
-                            lhsT=keys[:, (o * 2 + u) * 2 * P : (o * 2 + u + 1) * 2 * P].bitcast(FP4X4),
-                            lhsT_scale=ks_planes[o][:, first : first + P],
-                            rhs=q_codes[:, o * NQ : (o + 1) * NQ].bitcast(FP8X4),
-                            rhs_scale=q_scales[:, o * NQ : (o + 1) * NQ],
-                            start=(o == 0),
-                            stop=(o == PASSES - 1),
-                        )
-                    nc.scalar.activation(prob[:, t, :], score[:], SIGMOID, bias=kb_got[:, first : first + 1])
-            probs.append(prob)
+        def quantise_queries(o):
+            q_codes = shared.tile([P, NQ], U32, name="q_codes%d" % o, align_bytes=64, offset=66560 + 512 * o)
+            q_scales = sb.tile([P, NQ], U8, name="q_scales%d" % o, align_bytes=64)
+            nc.vector.quantize_mx(out=q_codes[:].bitcast(FP8X4), scales=q_scales[:], in_=q_bfs[o][:].rearrange("p q j -> p (q j)"))
+            q_ops.append((q_codes, q_scales))
+
+        probs = [sb.tile([P, PACK, NQ], F32, name="prob%d" % g) for g in range(PAGES)]
+        scores = {}
+
+        def score_pass(g, t, o, keys):
+            if o == 0:
+                scores[g, t] = ps.tile([P, NQ], F32, name="score%d" % (PACK * g + t), tag="bank%d" % (PACK * g + t))
+            first = g * PAGE + t * P
+            nc.tensor.matmul_mx(
+                out=scores[g, t][:],
+                lhsT=keys.bitcast(FP4X4),
+                lhsT_scale=ks_planes[o][:, first : first + P],
+                rhs=q_ops[o][0][:].bitcast(FP8X4),
+                rhs_scale=q_ops[o][1][:],
+                start=(o == 0),
+                stop=(o == PASSES - 1),
+            )
+            if o == PASSES - 1:
+                nc.scalar.activation(probs[g][:, t, :], scores[g, t][:], SIGMOID, bias=kb_got[:, first : first + 1])
+
+        first_keys = sb.tile([P, 1024], U8, name="first_keys", align_bytes=64)
+        second_keys = shared.tile([P, 1024], U8, name="second_keys", align_bytes=64, offset=82432)
+        later_keys = shared.tile([P, 2 * 1024], U8, name="later_keys", align_bytes=64, offset=18496)
+        page_words = [kw_pages[g][:].bitcast(U16).rearrange("p (m t o) -> p o m t", t=PACK, o=PASSES) for g in range(PAGES)]
+        for o in range(PASSES):
+            quantise_queries(o)
+            keys = (first_keys, second_keys)[o][:]
+            nc.vector.tensor_copy(keys.bitcast(U16).rearrange("p (t m) -> p m t", t=PACK), page_words[0][:, o])
+            for t in range(PACK):
+                score_pass(0, t, o, keys[:, t * 2 * P : (t + 1) * 2 * P])
+        for half in range(2):
+            keys = later_keys[:, half * 1024 : (half + 1) * 1024]
+            nc.vector.tensor_copy(
+                keys.bitcast(U16).rearrange("p (o u m) -> p o m u", o=PASSES, u=2),
+                page_words[1][:, :, :, 2 * half : 2 * half + 2],
+            )
+            for u in range(2):
+                for o in range(PASSES):
+                    score_pass(1, 2 * half + u, o, keys[:, (o * 2 + u) * 2 * P : (o * 2 + u + 1) * 2 * P])
 
         vs_got = shared.tile([P, PAGES, PAGE], F32, name="vs_got", offset=22464)
         for g in range(PAGES):
@@ -174,16 +191,21 @@ def tile_attend_pkv4_sigmoid_bias_kernel(tc, qT, k_words, k_scales, v_words, v_s
         vw_got = shared.tile([P, PAGES * DV], U32, name="vw_got", align_bytes=64, offset=34816)
         nc.vector.tensor_copy(vw_got[:], vw_win[:].bitcast(U32).indirect(voffs_sb[:]))
 
-        w_bfs = []
-        for g in range(PAGES):
-            w_bf = shared.tile([P, NQ, PACK], BF16, name="w_bf%d" % g, align_bytes=64, offset=(0, 15680)[g])
-            (nc.gpsimd, nc.vector)[g].tensor_tensor(
-                w_bf[:].rearrange("p (c i) t -> p c t i", i=4),
-                probs[g][:].rearrange("p t (c i) -> p c t i", i=4),
-                vs_got[:, g].rearrange("p (t x) -> p t x", t=PACK)[:, :, 0:4].unsqueeze(1).to_broadcast([P, NQ // 4, PACK, 4]),
+        w_bfs = [shared.tile([P, NQ, PACK], BF16, name="w_bf%d" % g, align_bytes=64, offset=(0, 15680)[g]) for g in range(PAGES)]
+        for g, engine, queries in ((0, nc.gpsimd, POOL_Q), (1, nc.vector, NQ)):
+            engine.tensor_tensor(
+                w_bfs[g][:, 0:queries, :].rearrange("p (c i) t -> p c t i", i=4),
+                probs[g][:, :, 0:queries].rearrange("p t (c i) -> p c t i", i=4),
+                vs_got[:, g].rearrange("p (t x) -> p t x", t=PACK)[:, :, 0:4].unsqueeze(1).to_broadcast([P, queries // 4, PACK, 4]),
                 MULT,
             )
-            w_bfs.append(w_bf)
+        w_rows = sb.tile([P, PACK, NQ - POOL_Q], BF16, name="w_rows")
+        for t in range(PACK):
+            nc.scalar.activation(w_rows[:, t, :], probs[0][:, t, POOL_Q:NQ], COPY, scale=vs_got[:, 0, t * P : t * P + 1])
+        nc.scalar.copy(
+            w_bfs[0][:, POOL_Q:NQ, :].rearrange("p (c i) t -> p c t i", i=4),
+            w_rows[:].rearrange("p t (c i) -> p c t i", i=4),
+        )
         weights = []
         for g in range(PAGES):
             w_codes = shared.tile([P, NQ], U32, name="w_codes%d" % g, align_bytes=64, offset=(16896, 2048)[g])

@@ -26,8 +26,8 @@ BLOCKS = POOL_PAGES * PACK
 KS_ROW = P - 16 * PASSES
 KB_FILL = 48
 KB_HEAD = 16
-VS_FILL = 72
-POOL_Q = 96
+VS_FILL = 64
+WIDE_Q = (96, 80)
 
 FLOPS = 2 * NQ * N * D + 2 * NQ * N * DV
 BYTES = 4 * D * NQ + 4 * P * T + 32 * T + 4 * P * POOL_PAGES * DV + 16 * POOL_PAGES * DV + 8 * T + 2 * P * (N + PAGES * DV) // 16 + 4 * NQ * DV
@@ -96,21 +96,21 @@ def tile_attend_pkv4_sigmoid_bias_kernel(tc, qT, k_words, k_scales, v_words, v_s
 
         ks_got = shared.tile([P, N], U8, name="ks_got", offset=57344)
         nc.vector.tensor_copy(ks_got[:], ks_win[:].bitcast(U8).indirect(offs_sb[:]))
-        vsc_got = shared.tile([P, PAGES * DV // 4], I32, name="vsc_got", offset=16640)
+        vsc_got = sb.tile([P, PAGES * DV // 4], I32, name="vsc_got")
         nc.vector.tensor_copy(vsc_got[:].bitcast(U8), vsc_win[:].bitcast(U8).indirect(voffs_sb[:]))
         ks_dealt = sb.tile([P, N // 4], I32, name="ks_dealt")
         nc.vector.tensor_copy(
             ks_dealt[:].bitcast(U8).rearrange("p (g t m) -> p g t m", g=PAGES, t=PACK),
             ks_got[:].rearrange("p (g m t) -> p g t m", g=PAGES, t=PACK),
         )
-        kb_got = sb.tile([P, N], F32, name="kb_got")
+        kb_got = shared.tile([P, N], F32, name="kb_got", offset=12288)
         nc.vector.tensor_copy(kb_got[:], kb_win[:].indirect(offs_sb[:]))
         vs_win = shared.tile([P, T], F32, name="vs_win", offset=41024)
         vs_blocks = vs_win[:].rearrange("p (b x) -> p b x", b=BLOCKS)
         nc.gpsimd.memset(vs_blocks[:, :, VS_FILL:P], 0.0)
         nc.scalar.copy(vs_blocks[:, :, 0:VS_FILL], vs_cols[:].unsqueeze(2).to_broadcast([P, BLOCKS, VS_FILL]))
         ks_plane = sb.tile([P, PASSES * N // 4], I32, name="ks_plane", align_bytes=64)
-        for u in range(4):
+        for u in (0, 2, 1, 3):
             nc.sync.dma_start(ks_plane[32 * u : 32 * u + 4, :], ks_dealt[KS_ROW + 8 * u : KS_ROW + 8 * (u + 1), :])
         ks_planes = [ks_plane[:].bitcast(U8)[:, o * N : (o + 1) * N] for o in range(PASSES)]
 
@@ -120,7 +120,7 @@ def tile_attend_pkv4_sigmoid_bias_kernel(tc, qT, k_words, k_scales, v_words, v_s
             v_words.rearrange("g p e b -> p g (e b)").bitcast(I32),
         )
         vsc_plane = shared.tile([P, PAGES * DV // 4], I32, name="vsc_plane", align_bytes=64, offset=57408)
-        for u in range(4):
+        for u in (0, 2, 1, 3):
             nc.sync.dma_start(vsc_plane[32 * u : 32 * u + 4, :], vsc_got[16 * u : 16 * (u + 1) : 4, :])
 
         kw_pages = []
@@ -191,24 +191,25 @@ def tile_attend_pkv4_sigmoid_bias_kernel(tc, qT, k_words, k_scales, v_words, v_s
         vw_got = shared.tile([P, PAGES * DV], U32, name="vw_got", align_bytes=64, offset=34816)
         nc.vector.tensor_copy(vw_got[:], vw_win[:].bitcast(U32).indirect(voffs_sb[:]))
 
-        w_bfs = [shared.tile([P, NQ, PACK], BF16, name="w_bf%d" % g, align_bytes=64, offset=(0, 15680)[g]) for g in range(PAGES)]
-        for g, engine, queries in ((0, nc.gpsimd, POOL_Q), (1, nc.vector, NQ)):
+        w_bfs = [sb.tile([P, NQ, PACK], BF16, name="w_bf%d" % g, align_bytes=64) for g in range(PAGES)]
+        for g, engine in enumerate((nc.gpsimd, nc.vector)):
+            queries = WIDE_Q[g]
             engine.tensor_tensor(
                 w_bfs[g][:, 0:queries, :].rearrange("p (c i) t -> p c t i", i=4),
                 probs[g][:, :, 0:queries].rearrange("p t (c i) -> p c t i", i=4),
                 vs_got[:, g].rearrange("p (t x) -> p t x", t=PACK)[:, :, 0:4].unsqueeze(1).to_broadcast([P, queries // 4, PACK, 4]),
                 MULT,
             )
-        w_rows = sb.tile([P, PACK, NQ - POOL_Q], BF16, name="w_rows")
-        for t in range(PACK):
-            nc.scalar.activation(w_rows[:, t, :], probs[0][:, t, POOL_Q:NQ], COPY, scale=vs_got[:, 0, t * P : t * P + 1])
-        nc.scalar.copy(
-            w_bfs[0][:, POOL_Q:NQ, :].rearrange("p (c i) t -> p c t i", i=4),
-            w_rows[:].rearrange("p t (c i) -> p c t i", i=4),
-        )
+            w_rows = shared.tile([P, PACK, NQ - queries], BF16, name="w_rows%d" % g, offset=(0, 13312)[g])
+            for t in range(PACK):
+                nc.scalar.activation(w_rows[:, t, :], probs[g][:, t, queries:NQ], COPY, scale=vs_got[:, g, t * P : t * P + 1])
+            nc.scalar.copy(
+                w_bfs[g][:, queries:NQ, :].rearrange("p (c i) t -> p c t i", i=4),
+                w_rows[:].rearrange("p t (c i) -> p c t i", i=4),
+            )
         weights = []
         for g in range(PAGES):
-            w_codes = shared.tile([P, NQ], U32, name="w_codes%d" % g, align_bytes=64, offset=(16896, 2048)[g])
+            w_codes = shared.tile([P, NQ], U32, name="w_codes%d" % g, align_bytes=64, offset=(12288, 2048)[g])
             w_scales = sb.tile([P, NQ], U8, name="w_scales%d" % g, align_bytes=64)
             nc.vector.quantize_mx(out=w_codes[:].bitcast(FP8X4), scales=w_scales[:], in_=w_bfs[g][:].rearrange("p q t -> p (q t)"))
             weights.append((w_codes, w_scales))

@@ -26,7 +26,7 @@ BLOCKS = POOL_PAGES * PACK
 KS_ROW = P - 16 * PASSES
 KB_FILL = 48
 KB_HEAD = 16
-VS_FILL = 64
+VS_FILL = 48
 WIDE_Q = (96, 80)
 
 FLOPS = 2 * NQ * N * D + 2 * NQ * N * DV
@@ -47,7 +47,7 @@ def tile_attend_pkv4_sigmoid_bias_kernel(tc, qT, k_words, k_scales, v_words, v_s
         kb_rows = sb.tile([P, PAGE], F32, name="kb_rows")
         vs_rows = sb.tile([P, PAGE], F32, name="vs_rows")
         ks_win = sb.tile([P, T // 4], I32, name="ks_win")
-        kb_win = sb.tile([P, T], F32, name="kb_win")
+        kb_win = shared.tile([P, T], F32, name="kb_win", offset=86016)
         kb_blocks = kb_win[:].rearrange("p (b x) -> p b x", b=BLOCKS)
 
         nc.vector.memset(vsc_win[:], 0)
@@ -88,11 +88,9 @@ def tile_attend_pkv4_sigmoid_bias_kernel(tc, qT, k_words, k_scales, v_words, v_s
         nc.tensor.transpose(kb_turned[:], kb_rows[:, 0:PAGE:PACK], ident[:])
         vs_turned = ps.tile([P, P], F32, name="vs_turned", tag="bank7")
         nc.tensor.transpose(vs_turned[:], vs_rows[:, 0:PAGE:PACK], ident[:])
-        kb_cols = shared.tile([P, BLOCKS], F32, name="kb_cols", offset=32768)
-        nc.scalar.copy(kb_cols[:], kb_turned[:, KS_ROW:P])
+        nc.scalar.copy(kb_blocks[:, :, 0:KB_FILL], kb_turned[:, KS_ROW:P].unsqueeze(2).to_broadcast([P, BLOCKS, KB_FILL]))
         vs_cols = shared.tile([P, BLOCKS], F32, name="vs_cols", offset=21440)
         nc.scalar.copy(vs_cols[:], vs_turned[:, 0:64:2])
-        nc.scalar.copy(kb_blocks[:, :, 0:KB_FILL], kb_cols[:].unsqueeze(2).to_broadcast([P, BLOCKS, KB_FILL]))
 
         ks_got = shared.tile([P, N], U8, name="ks_got", offset=57344)
         nc.vector.tensor_copy(ks_got[:], ks_win[:].bitcast(U8).indirect(offs_sb[:]))
@@ -125,7 +123,7 @@ def tile_attend_pkv4_sigmoid_bias_kernel(tc, qT, k_words, k_scales, v_words, v_s
 
         kw_pages = []
         for g in range(PAGES):
-            kw_got = shared.tile([P, PAGE], U32, name="kw_got%d" % g, offset=(30784, 32832)[g])
+            kw_got = shared.tile([P, PAGE], U32, name="kw_got%d" % g, offset=(86016, 88064)[g])
             cols = slice(g * PAGE // 16, (g + 1) * PAGE // 16)
             nc.vector.tensor_copy(kw_got[:], kw_win[:].bitcast(U32).indirect(offs_sb[:, cols]))
             kw_pages.append(kw_got)
@@ -188,7 +186,7 @@ def tile_attend_pkv4_sigmoid_bias_kernel(tc, qT, k_words, k_scales, v_words, v_s
         for g in range(PAGES):
             cols = slice(g * PAGE // 16, (g + 1) * PAGE // 16)
             nc.vector.tensor_copy(vs_got[:, g], vs_win[:].indirect(offs_sb[:, cols]))
-        vw_got = shared.tile([P, PAGES * DV], U32, name="vw_got", align_bytes=64, offset=34816)
+        vw_got = shared.tile([P, PAGES * DV], U32, name="vw_got", align_bytes=64, offset=90048)
         nc.vector.tensor_copy(vw_got[:], vw_win[:].bitcast(U32).indirect(voffs_sb[:]))
 
         w_bfs = [sb.tile([P, NQ, PACK], BF16, name="w_bf%d" % g, align_bytes=64) for g in range(PAGES)]

@@ -24,6 +24,8 @@ POOL_PAGES = T // PAGE
 PASSES = D // (P * PACK)
 BLOCKS = POOL_PAGES * PACK
 KS_ROW = P - 16 * PASSES
+KB_ROW = P - 2 * POOL_PAGES
+KW_HEAD = 512
 KB_FILL = 48
 KB_HEAD = 16
 VS_FILL = 48
@@ -44,7 +46,7 @@ def tile_attend_pkv4_sigmoid_bias_kernel(tc, qT, k_words, k_scales, v_words, v_s
         offs_sb = lists.tile([P, N // 16], U16, name="offs_sb")
         voffs_sb = lists.tile([P, PAGES * DV // 16], U16, name="voffs_sb")
         vsc_win = sb.tile([P, POOL_PAGES * DV // 4], I32, name="vsc_win")
-        kb_rows = sb.tile([P, PAGE], F32, name="kb_rows")
+        kb_rows = shared.tile([P, PAGE], F32, name="kb_rows", offset=102400)
         vs_rows = sb.tile([P, PAGE], F32, name="vs_rows")
         ks_win = sb.tile([P, T // 4], I32, name="ks_win")
         kb_win = shared.tile([P, T], F32, name="kb_win", offset=86016)
@@ -52,25 +54,25 @@ def tile_attend_pkv4_sigmoid_bias_kernel(tc, qT, k_words, k_scales, v_words, v_s
 
         nc.vector.memset(vsc_win[:], 0)
         nc.vector.memset(vs_rows[:], 0.0)
-        nc.vector.memset(kb_rows[0:KS_ROW, :], 0.0)
+        nc.vector.memset(kb_rows[0:KB_ROW, :], 0.0)
         nc.vector.memset(ks_win[0:KS_ROW, :], 0)
         nc.vector.memset(kb_blocks[:, 0:KB_HEAD, KB_FILL:P], 0.0)
 
-        def shifted_rows(table):
-            shifted = table.rearrange("r x -> (r x)")[0 : PACK * (T + 1)].rearrange("(t y) -> t y", t=PACK)[:, 0:T]
-            return shifted.rearrange("t (u x) -> u t x", u=POOL_PAGES)
+        kb_shifted = kb.rearrange("r x -> (r x)")[0 : 2 * (T + 2)].rearrange("(s y) -> s y", s=2)[:, 0:T]
 
         nc.scalar.dma_start(ks_win[KS_ROW:P, :], k_scales.rearrange("o f t -> f o t").bitcast(I32))
-        nc.scalar.dma_start(kb_rows[KS_ROW:P, :], shifted_rows(kb))
+        nc.scalar.dma_start(kb_rows[KB_ROW:P, :], kb_shifted.rearrange("s (u x) -> u s x", u=POOL_PAGES))
         nc.sync.dma_start(offs_sb[:], offs)
         nc.sync.dma_start(voffs_sb[:], voffs)
+        kw_win = shared.tile([P, T], I32, name="kw_win", offset=66560)
+        kw_hbm = k_words[0].rearrange("p t b -> p (t b)").bitcast(I32)
+        nc.sync.dma_start(kw_win[:, 0:KW_HEAD], kw_hbm[:, 0:KW_HEAD])
         nc.sync.dma_start(
             vsc_win[0:64:4, :].rearrange("p (g e) -> p g e", g=POOL_PAGES),
             v_scales.rearrange("g f e -> f g e").bitcast(I32),
         )
-        nc.sync.dma_start(vs_rows[0:64:2, :], shifted_rows(vs))
-        kw_win = shared.tile([P, T], I32, name="kw_win", offset=66560)
-        nc.sync.dma_start(kw_win[:], k_words[0].rearrange("p t b -> p (t b)").bitcast(I32))
+        nc.sync.dma_start(vs_rows[0:32:4, :], vs[0].rearrange("(u x) -> u x", u=POOL_PAGES))
+        nc.sync.dma_start(kw_win[:, KW_HEAD:T], kw_hbm[:, KW_HEAD:T])
         q_rows = qT[0].rearrange("(o p j) q -> o p j q", o=PASSES, j=PACK)
         q_raws = []
         for o in range(PASSES):
@@ -84,19 +86,24 @@ def tile_attend_pkv4_sigmoid_bias_kernel(tc, qT, k_words, k_scales, v_words, v_s
         warm = sb.tile([32, 8], F32, name="warm")
         nc.scalar.activation(warm[:], ident[0:32, 0:8], SIGMOID)
 
-        kb_turned = ps.tile([P, P], F32, name="kb_turned", tag="bank6")
-        nc.tensor.transpose(kb_turned[:], kb_rows[:, 0:PAGE:PACK], ident[:])
-        vs_turned = ps.tile([P, P], F32, name="vs_turned", tag="bank7")
-        nc.tensor.transpose(vs_turned[:], vs_rows[:, 0:PAGE:PACK], ident[:])
-        nc.scalar.copy(kb_blocks[:, :, 0:KB_FILL], kb_turned[:, KS_ROW:P].unsqueeze(2).to_broadcast([P, BLOCKS, KB_FILL]))
+        kb_turned = ps.tile([P, 2, P], F32, name="kb_turned", tag="bank6")
+        for c in range(2):
+            nc.tensor.transpose(kb_turned[:, c, :], kb_rows[:, c:PAGE:PACK], ident[:])
+        vs_turned = ps.tile([P, PACK, P], F32, name="vs_turned", tag="bank7")
+        for t in range(PACK):
+            nc.tensor.transpose(vs_turned[:, t, :], vs_rows[:, t:PAGE:PACK], ident[:])
+        nc.scalar.copy(
+            kb_blocks[:, :, 0:KB_FILL].rearrange("p (r c) x -> p r c x", c=2),
+            kb_turned[:, :, KB_ROW:P].rearrange("p c r -> p r c").unsqueeze(3).to_broadcast([P, BLOCKS // 2, 2, KB_FILL]),
+        )
         vs_cols = shared.tile([P, BLOCKS], F32, name="vs_cols", offset=21440)
-        nc.scalar.copy(vs_cols[:], vs_turned[:, 0:64:2])
+        nc.scalar.copy(vs_cols[:].rearrange("p (u t) -> p u t", t=PACK), vs_turned[:, :, 0:32:4].rearrange("p t u -> p u t"))
 
         ks_got = shared.tile([P, N], U8, name="ks_got", offset=57344)
         nc.vector.tensor_copy(ks_got[:], ks_win[:].bitcast(U8).indirect(offs_sb[:]))
         vsc_got = sb.tile([P, PAGES * DV // 4], I32, name="vsc_got")
         nc.vector.tensor_copy(vsc_got[:].bitcast(U8), vsc_win[:].bitcast(U8).indirect(voffs_sb[:]))
-        ks_dealt = sb.tile([P, N // 4], I32, name="ks_dealt")
+        ks_dealt = shared.tile([P, N // 4], I32, name="ks_dealt", offset=102400)
         nc.vector.tensor_copy(
             ks_dealt[:].bitcast(U8).rearrange("p (g t m) -> p g t m", g=PAGES, t=PACK),
             ks_got[:].rearrange("p (g m t) -> p g t m", g=PAGES, t=PACK),

@@ -29,7 +29,8 @@ KW_HEAD = 512
 KB_FILL = 48
 KB_HEAD = 16
 VS_FILL = 48
-WIDE_Q = (96, 80)
+WIDE_Q = (128, 80)
+CAST_Q = (128, 80)
 
 FLOPS = 2 * NQ * N * D + 2 * NQ * N * DV
 BYTES = 4 * D * NQ + 4 * P * T + 32 * T + 4 * P * POOL_PAGES * DV + 16 * POOL_PAGES * DV + 8 * T + 2 * P * (N + PAGES * DV) // 16 + 4 * NQ * DV
@@ -139,8 +140,8 @@ def tile_attend_pkv4_sigmoid_bias_kernel(tc, qT, k_words, k_scales, v_words, v_s
         for o in range(PASSES):
             q_bf = shared.tile([P, NQ, PACK], BF16, name="q_bf%d" % o, align_bytes=64, offset=(20480, 21504)[o])
             nc.scalar.copy(
-                q_bf[:].rearrange("p (c i) j -> p c j i", i=4),
-                q_raws[o][:].rearrange("p j (c i) -> p c j i", i=4),
+                q_bf[:, 0 : CAST_Q[o], :].rearrange("p (c i) j -> p c j i", i=4),
+                q_raws[o][:, :, 0 : CAST_Q[o]].rearrange("p j (c i) -> p c j i", i=4),
             )
             q_bfs.append(q_bf)
 
@@ -170,13 +171,18 @@ def tile_attend_pkv4_sigmoid_bias_kernel(tc, qT, k_words, k_scales, v_words, v_s
                 nc.scalar.activation(probs[g][:, t, :], scores[g, t][:], SIGMOID, bias=kb_got[:, first : first + 1])
 
         first_keys = sb.tile([P, 1024], U8, name="first_keys", align_bytes=64)
-        second_keys = shared.tile([P, 1024], U8, name="second_keys", align_bytes=64, offset=82432)
-        later_keys = shared.tile([P, 2 * 1024], U8, name="later_keys", align_bytes=64, offset=18496)
+        second_keys = shared.tile([P, 1024], U8, name="second_keys", align_bytes=64, offset=8192)
+        later_keys = shared.tile([P, 2 * 1024], U8, name="later_keys", align_bytes=64, offset=82944)
         page_words = [kw_pages[g][:].bitcast(U16).rearrange("p (m t o) -> p o m t", t=PACK, o=PASSES) for g in range(PAGES)]
         for o in range(PASSES):
-            quantise_queries(o)
             keys = (first_keys, second_keys)[o][:]
             nc.vector.tensor_copy(keys.bitcast(U16).rearrange("p (t m) -> p m t", t=PACK), page_words[0][:, o])
+            if o == 0:
+                nc.vector.tensor_copy(
+                    q_bfs[1][:, CAST_Q[1] : NQ, :].rearrange("p (c i) j -> p c j i", i=4),
+                    q_raws[1][:, :, CAST_Q[1] : NQ].rearrange("p j (c i) -> p c j i", i=4),
+                )
+            quantise_queries(o)
             for t in range(PACK):
                 score_pass(0, t, o, keys[:, t * 2 * P : (t + 1) * 2 * P])
         for half in range(2):
@@ -196,7 +202,7 @@ def tile_attend_pkv4_sigmoid_bias_kernel(tc, qT, k_words, k_scales, v_words, v_s
         vw_got = shared.tile([P, PAGES * DV], U32, name="vw_got", align_bytes=64, offset=90048)
         nc.vector.tensor_copy(vw_got[:], vw_win[:].bitcast(U32).indirect(voffs_sb[:]))
 
-        w_bfs = [sb.tile([P, NQ, PACK], BF16, name="w_bf%d" % g, align_bytes=64) for g in range(PAGES)]
+        w_bfs = [shared.tile([P, NQ, PACK], BF16, name="w_bf%d" % g, align_bytes=64, offset=(0, 13312)[g]) for g in range(PAGES)]
         for g, engine in enumerate((nc.gpsimd, nc.vector)):
             queries = WIDE_Q[g]
             engine.tensor_tensor(
@@ -205,13 +211,8 @@ def tile_attend_pkv4_sigmoid_bias_kernel(tc, qT, k_words, k_scales, v_words, v_s
                 vs_got[:, g].rearrange("p (t x) -> p t x", t=PACK)[:, :, 0:4].unsqueeze(1).to_broadcast([P, queries // 4, PACK, 4]),
                 MULT,
             )
-            w_rows = shared.tile([P, PACK, NQ - queries], BF16, name="w_rows%d" % g, offset=(0, 13312)[g])
-            for t in range(PACK):
-                nc.scalar.activation(w_rows[:, t, :], probs[g][:, t, queries:NQ], COPY, scale=vs_got[:, g, t * P : t * P + 1])
-            nc.scalar.copy(
-                w_bfs[g][:, queries:NQ, :].rearrange("p (c i) t -> p c t i", i=4),
-                w_rows[:].rearrange("p t (c i) -> p c t i", i=4),
-            )
+        for t in range(PACK):
+            nc.scalar.activation(w_bfs[1][:, queries:NQ, t], probs[1][:, t, queries:NQ], COPY, scale=vs_got[:, 1, t * P : t * P + 1])
         weights = []
         for g in range(PAGES):
             w_codes = shared.tile([P, NQ], U32, name="w_codes%d" % g, align_bytes=64, offset=(12288, 2048)[g])

@@ -29,7 +29,7 @@ KW_HEAD = 512
 KB_FILL = 48
 KB_HEAD = 16
 VS_FILL = 48
-WIDE_Q = (128, 80)
+WIDE_Q = (128, 96)
 CAST_Q = (128, 80)
 
 FLOPS = 2 * NQ * N * D + 2 * NQ * N * DV

@@ -24,16 +24,24 @@ POOL_PAGES = T // PAGE
 PASSES = D // (P * PACK)
 BLOCKS = POOL_PAGES * PACK
 KS_ROW = P - 16 * PASSES
-KB_ROW = P - 2 * POOL_PAGES
 KW_HEAD = 512
-KB_FILL = 48
-KB_HEAD = 16
-VS_FILL = 48
-WIDE_Q = (128, 96)
-CAST_Q = (128, 80)
+KB_FILL = 40
+KB_HEAD = 20
+VS_FILL = 56
 
 FLOPS = 2 * NQ * N * D + 2 * NQ * N * DV
 BYTES = 4 * D * NQ + 4 * P * T + 32 * T + 4 * P * POOL_PAGES * DV + 16 * POOL_PAGES * DV + 8 * T + 2 * P * (N + PAGES * DV) // 16 + 4 * NQ * DV
+
+AT_VS_WIN = 0
+AT_KS_GOT = 16320
+AT_VW_WIN = 17280
+AT_KB_WIN = 26624
+AT_Q_RAW = (43008, 47104)
+AT_KB_GOT = 53248
+AT_KS_WIN = 57344
+AT_PROB = 61440
+AT_KS_DEALT = 65536
+AT_FIRST_KEYS = 67584
 
 
 def tile_attend_pkv4_sigmoid_bias_kernel(tc, qT, k_words, k_scales, v_words, v_scales, vs, kb, offs, voffs, out):
@@ -46,38 +54,38 @@ def tile_attend_pkv4_sigmoid_bias_kernel(tc, qT, k_words, k_scales, v_words, v_s
 
         offs_sb = lists.tile([P, N // 16], U16, name="offs_sb")
         voffs_sb = lists.tile([P, PAGES * DV // 16], U16, name="voffs_sb")
-        vsc_win = sb.tile([P, POOL_PAGES * DV // 4], I32, name="vsc_win")
-        kb_rows = shared.tile([P, PAGE], F32, name="kb_rows", offset=102400)
+        kb_rows = sb.tile([P, PAGE], F32, name="kb_rows")
         vs_rows = sb.tile([P, PAGE], F32, name="vs_rows")
-        ks_win = sb.tile([P, T // 4], I32, name="ks_win")
-        kb_win = shared.tile([P, T], F32, name="kb_win", offset=86016)
+        vsc_win = sb.tile([P, POOL_PAGES * DV // 4], I32, name="vsc_win")
+        ks_win = shared.tile([P, T // 4], I32, name="ks_win", offset=AT_KS_WIN)
+        kb_win = shared.tile([P, T], F32, name="kb_win", offset=AT_KB_WIN)
         kb_blocks = kb_win[:].rearrange("p (b x) -> p b x", b=BLOCKS)
 
-        nc.vector.memset(vsc_win[:], 0)
+        nc.vector.memset(kb_rows[:], 0.0)
         nc.vector.memset(vs_rows[:], 0.0)
-        nc.vector.memset(kb_rows[0:KB_ROW, :], 0.0)
+        nc.vector.memset(vsc_win[:], 0)
         nc.vector.memset(ks_win[0:KS_ROW, :], 0)
         nc.vector.memset(kb_blocks[:, 0:KB_HEAD, KB_FILL:P], 0.0)
 
         kb_shifted = kb.rearrange("r x -> (r x)")[0 : 2 * (T + 2)].rearrange("(s y) -> s y", s=2)[:, 0:T]
 
         nc.scalar.dma_start(ks_win[KS_ROW:P, :], k_scales.rearrange("o f t -> f o t").bitcast(I32))
-        nc.scalar.dma_start(kb_rows[KB_ROW:P, :], kb_shifted.rearrange("s (u x) -> u s x", u=POOL_PAGES))
         nc.sync.dma_start(offs_sb[:], offs)
         nc.sync.dma_start(voffs_sb[:], voffs)
-        kw_win = shared.tile([P, T], I32, name="kw_win", offset=66560)
+        kw_win = sb.tile([P, T], I32, name="kw_win")
         kw_hbm = k_words[0].rearrange("p t b -> p (t b)").bitcast(I32)
         nc.sync.dma_start(kw_win[:, 0:KW_HEAD], kw_hbm[:, 0:KW_HEAD])
+        nc.sync.dma_start(kb_rows[0:64:4, :], kb_shifted.rearrange("s (u x) -> u s x", u=POOL_PAGES))
+        nc.sync.dma_start(vs_rows[0:32:4, :], vs[0].rearrange("(u x) -> u x", u=POOL_PAGES))
         nc.sync.dma_start(
             vsc_win[0:64:4, :].rearrange("p (g e) -> p g e", g=POOL_PAGES),
             v_scales.rearrange("g f e -> f g e").bitcast(I32),
         )
-        nc.sync.dma_start(vs_rows[0:32:4, :], vs[0].rearrange("(u x) -> u x", u=POOL_PAGES))
         nc.sync.dma_start(kw_win[:, KW_HEAD:T], kw_hbm[:, KW_HEAD:T])
         q_rows = qT[0].rearrange("(o p j) q -> o p j q", o=PASSES, j=PACK)
         q_raws = []
         for o in range(PASSES):
-            q_raw = shared.tile([P, PACK, NQ], F32, name="q_raw%d" % o, offset=(8192, 82944)[o])
+            q_raw = shared.tile([P, PACK, NQ], F32, name="q_raw%d" % o, offset=AT_Q_RAW[o])
             nc.sync.dma_start(q_raw[:], q_rows[o])
             q_raws.append(q_raw)
 
@@ -95,63 +103,64 @@ def tile_attend_pkv4_sigmoid_bias_kernel(tc, qT, k_words, k_scales, v_words, v_s
             nc.tensor.transpose(vs_turned[:, t, :], vs_rows[:, t:PAGE:PACK], ident[:])
         nc.scalar.copy(
             kb_blocks[:, :, 0:KB_FILL].rearrange("p (r c) x -> p r c x", c=2),
-            kb_turned[:, :, KB_ROW:P].rearrange("p c r -> p r c").unsqueeze(3).to_broadcast([P, BLOCKS // 2, 2, KB_FILL]),
+            kb_turned[:, :, 0:64:4].rearrange("p c r -> p r c").unsqueeze(3).to_broadcast([P, BLOCKS // 2, 2, KB_FILL]),
         )
-        vs_cols = shared.tile([P, BLOCKS], F32, name="vs_cols", offset=21440)
-        nc.scalar.copy(vs_cols[:].rearrange("p (u t) -> p u t", t=PACK), vs_turned[:, :, 0:32:4].rearrange("p t u -> p u t"))
 
-        ks_got = shared.tile([P, N], U8, name="ks_got", offset=57344)
+        ks_got = shared.tile([P, N], U8, name="ks_got", offset=AT_KS_GOT)
         nc.vector.tensor_copy(ks_got[:], ks_win[:].bitcast(U8).indirect(offs_sb[:]))
-        vsc_got = sb.tile([P, PAGES * DV // 4], I32, name="vsc_got")
-        nc.vector.tensor_copy(vsc_got[:].bitcast(U8), vsc_win[:].bitcast(U8).indirect(voffs_sb[:]))
-        ks_dealt = shared.tile([P, N // 4], I32, name="ks_dealt", offset=102400)
+        ks_dealt = shared.tile([P, N // 4], I32, name="ks_dealt", offset=AT_KS_DEALT)
         nc.vector.tensor_copy(
             ks_dealt[:].bitcast(U8).rearrange("p (g t m) -> p g t m", g=PAGES, t=PACK),
             ks_got[:].rearrange("p (g m t) -> p g t m", g=PAGES, t=PACK),
         )
-        kb_got = shared.tile([P, N], F32, name="kb_got", offset=12288)
+        vsc_got = shared.tile([P, PAGES * DV // 4], I32, name="vsc_got", offset=AT_KS_WIN)
+        nc.vector.tensor_copy(vsc_got[:].bitcast(U8), vsc_win[:].bitcast(U8).indirect(voffs_sb[:]))
+        kb_got = shared.tile([P, N], F32, name="kb_got", offset=AT_KB_GOT)
         nc.vector.tensor_copy(kb_got[:], kb_win[:].indirect(offs_sb[:]))
-        vs_win = shared.tile([P, T], F32, name="vs_win", offset=41024)
+        vs_win = shared.tile([P, T], F32, name="vs_win", offset=AT_VS_WIN)
         vs_blocks = vs_win[:].rearrange("p (b x) -> p b x", b=BLOCKS)
         nc.gpsimd.memset(vs_blocks[:, :, VS_FILL:P], 0.0)
-        nc.scalar.copy(vs_blocks[:, :, 0:VS_FILL], vs_cols[:].unsqueeze(2).to_broadcast([P, BLOCKS, VS_FILL]))
+        nc.scalar.copy(
+            vs_blocks[:, :, 0:VS_FILL].rearrange("p (u t) x -> p u t x", t=PACK),
+            vs_turned[:, :, 0:32:4].rearrange("p t u -> p u t").unsqueeze(3).to_broadcast([P, POOL_PAGES, PACK, VS_FILL]),
+        )
         ks_plane = sb.tile([P, PASSES * N // 4], I32, name="ks_plane", align_bytes=64)
         for u in (0, 2, 1, 3):
             nc.sync.dma_start(ks_plane[32 * u : 32 * u + 4, :], ks_dealt[KS_ROW + 8 * u : KS_ROW + 8 * (u + 1), :])
         ks_planes = [ks_plane[:].bitcast(U8)[:, o * N : (o + 1) * N] for o in range(PASSES)]
 
-        vw_win = shared.tile([P, POOL_PAGES * DV], I32, name="vw_win", offset=57920)
+        vw_win = shared.tile([P, POOL_PAGES * DV], I32, name="vw_win", offset=AT_VW_WIN)
         nc.sync.dma_start(
             vw_win[:].rearrange("p (g e) -> p g e", g=POOL_PAGES),
             v_words.rearrange("g p e b -> p g (e b)").bitcast(I32),
         )
-        vsc_plane = shared.tile([P, PAGES * DV // 4], I32, name="vsc_plane", align_bytes=64, offset=57408)
+        vsc_plane = shared.tile([P, PAGES * DV // 4], I32, name="vsc_plane", align_bytes=64, offset=AT_KB_WIN + 2048)
         for u in (0, 2, 1, 3):
             nc.sync.dma_start(vsc_plane[32 * u : 32 * u + 4, :], vsc_got[16 * u : 16 * (u + 1) : 4, :])
 
-        kw_pages = []
-        for g in range(PAGES):
-            kw_got = shared.tile([P, PAGE], U32, name="kw_got%d" % g, offset=(86016, 88064)[g])
-            cols = slice(g * PAGE // 16, (g + 1) * PAGE // 16)
-            nc.vector.tensor_copy(kw_got[:], kw_win[:].bitcast(U32).indirect(offs_sb[:, cols]))
-            kw_pages.append(kw_got)
-
         q_bfs, q_ops = [], []
         for o in range(PASSES):
-            q_bf = shared.tile([P, NQ, PACK], BF16, name="q_bf%d" % o, align_bytes=64, offset=(20480, 21504)[o])
+            q_bf = shared.tile([P, NQ, PACK], BF16, name="q_bf%d" % o, align_bytes=64, offset=AT_KB_WIN + 1024 * o)
             nc.scalar.copy(
-                q_bf[:, 0 : CAST_Q[o], :].rearrange("p (c i) j -> p c j i", i=4),
-                q_raws[o][:, :, 0 : CAST_Q[o]].rearrange("p j (c i) -> p c j i", i=4),
+                q_bf[:].rearrange("p (c i) j -> p c j i", i=4),
+                q_raws[o][:].rearrange("p j (c i) -> p c j i", i=4),
             )
             q_bfs.append(q_bf)
 
+        def gather_keys(kw_got, g):
+            cols = slice(g * PAGE // 16, (g + 1) * PAGE // 16)
+            nc.vector.tensor_copy(kw_got[:], kw_win[:].bitcast(U32).indirect(offs_sb[:, cols]))
+            return kw_got[:].bitcast(U16).rearrange("p (m t o) -> p o m t", t=PACK, o=PASSES)
+
         def quantise_queries(o):
-            q_codes = shared.tile([P, NQ], U32, name="q_codes%d" % o, align_bytes=64, offset=66560 + 512 * o)
+            q_codes = sb.tile([P, NQ], U32, name="q_codes%d" % o, align_bytes=64)
             q_scales = sb.tile([P, NQ], U8, name="q_scales%d" % o, align_bytes=64)
             nc.vector.quantize_mx(out=q_codes[:].bitcast(FP8X4), scales=q_scales[:], in_=q_bfs[o][:].rearrange("p q j -> p (q j)"))
             q_ops.append((q_codes, q_scales))
 
-        probs = [sb.tile([P, PACK, NQ], F32, name="prob%d" % g) for g in range(PAGES)]
+        last = PACK - 1
+        probs = [shared.tile([P, PACK - g, NQ], F32, name="prob%d" % g, offset=AT_PROB + 2048 * g) for g in range(PAGES)]
+        last_prob = sb.tile([P, NQ], F32, name="last_prob")
         scores = {}
 
         def score_pass(g, t, o, keys):
@@ -168,70 +177,76 @@ def tile_attend_pkv4_sigmoid_bias_kernel(tc, qT, k_words, k_scales, v_words, v_s
                 stop=(o == PASSES - 1),
             )
             if o == PASSES - 1:
-                nc.scalar.activation(probs[g][:, t, :], scores[g, t][:], SIGMOID, bias=kb_got[:, first : first + 1])
+                nc.scalar.activation(last_prob[:] if (g, t) == (1, last) else probs[g][:, t, :], scores[g, t][:], SIGMOID, bias=kb_got[:, first : first + 1])
 
-        first_keys = sb.tile([P, 1024], U8, name="first_keys", align_bytes=64)
-        second_keys = shared.tile([P, 1024], U8, name="second_keys", align_bytes=64, offset=8192)
-        later_keys = shared.tile([P, 2 * 1024], U8, name="later_keys", align_bytes=64, offset=82944)
-        page_words = [kw_pages[g][:].bitcast(U16).rearrange("p (m t o) -> p o m t", t=PACK, o=PASSES) for g in range(PAGES)]
+        kw_got0 = shared.tile([P, PAGE], U32, name="kw_got0", offset=AT_KB_WIN + 4096)
+        words0 = gather_keys(kw_got0, 0)
+        first_keys = []
         for o in range(PASSES):
-            keys = (first_keys, second_keys)[o][:]
-            nc.vector.tensor_copy(keys.bitcast(U16).rearrange("p (t m) -> p m t", t=PACK), page_words[0][:, o])
-            if o == 0:
-                nc.vector.tensor_copy(
-                    q_bfs[1][:, CAST_Q[1] : NQ, :].rearrange("p (c i) j -> p c j i", i=4),
-                    q_raws[1][:, :, CAST_Q[1] : NQ].rearrange("p j (c i) -> p c j i", i=4),
-                )
-            quantise_queries(o)
-            for t in range(PACK):
-                score_pass(0, t, o, keys[:, t * 2 * P : (t + 1) * 2 * P])
-        for half in range(2):
-            keys = later_keys[:, half * 1024 : (half + 1) * 1024]
+            keys = shared.tile([P, 1024], U8, name="first_keys%d" % o, align_bytes=64, offset=AT_FIRST_KEYS + 8192 * o)
+            nc.vector.tensor_copy(keys[:].bitcast(U16).rearrange("p (t m) -> p m t", t=PACK), words0[:, o])
+            first_keys.append(keys)
+        quantise_queries(0)
+        for t in range(PACK):
+            score_pass(0, t, 0, first_keys[0][:, t * 2 * P : (t + 1) * 2 * P])
+        kw_got1 = shared.tile([P, PAGE], U32, name="kw_got1", offset=AT_KS_DEALT)
+        words1 = gather_keys(kw_got1, 1)
+        quantise_queries(1)
+        for t in range(PACK):
+            score_pass(0, t, 1, first_keys[1][:, t * 2 * P : (t + 1) * 2 * P])
+        later_keys = sb.tile([P, 2 * 1024], U8, name="later_keys", align_bytes=64)
+        for pair in range(2):
+            keys = later_keys[:, pair * 1024 : (pair + 1) * 1024]
             nc.vector.tensor_copy(
                 keys.bitcast(U16).rearrange("p (o u m) -> p o m u", o=PASSES, u=2),
-                page_words[1][:, :, :, 2 * half : 2 * half + 2],
+                words1[:, :, :, 2 * pair : 2 * pair + 2],
             )
             for u in range(2):
                 for o in range(PASSES):
-                    score_pass(1, 2 * half + u, o, keys[:, (o * 2 + u) * 2 * P : (o * 2 + u + 1) * 2 * P])
+                    score_pass(1, 2 * pair + u, o, keys[:, (o * 2 + u) * 2 * P : (o * 2 + u + 1) * 2 * P])
 
-        vs_got = shared.tile([P, PAGES, PAGE], F32, name="vs_got", offset=22464)
+        vs_got = shared.tile([P, PAGES, PAGE], F32, name="vs_got", offset=AT_FIRST_KEYS)
         for g in range(PAGES):
             cols = slice(g * PAGE // 16, (g + 1) * PAGE // 16)
             nc.vector.tensor_copy(vs_got[:, g], vs_win[:].indirect(offs_sb[:, cols]))
-        vw_got = shared.tile([P, PAGES * DV], U32, name="vw_got", align_bytes=64, offset=90048)
+        vw_got = sb.tile([P, PAGES * DV], U32, name="vw_got", align_bytes=64)
         nc.vector.tensor_copy(vw_got[:], vw_win[:].bitcast(U32).indirect(voffs_sb[:]))
 
-        w_bfs = [shared.tile([P, NQ, PACK], BF16, name="w_bf%d" % g, align_bytes=64, offset=(0, 13312)[g]) for g in range(PAGES)]
-        for g, engine in enumerate((nc.gpsimd, nc.vector)):
-            queries = WIDE_Q[g]
+        w_bfs = [
+            sb.tile([P, NQ, PACK], BF16, name="w_bf0", align_bytes=64),
+            shared.tile([P, NQ, PACK], BF16, name="w_bf1", align_bytes=64, offset=AT_VW_WIN + 1024),
+        ]
+        for g, engine, places in ((0, nc.gpsimd, PACK), (1, nc.vector, PACK - 1)):
             engine.tensor_tensor(
-                w_bfs[g][:, 0:queries, :].rearrange("p (c i) t -> p c t i", i=4),
-                probs[g][:, :, 0:queries].rearrange("p t (c i) -> p c t i", i=4),
-                vs_got[:, g].rearrange("p (t x) -> p t x", t=PACK)[:, :, 0:4].unsqueeze(1).to_broadcast([P, queries // 4, PACK, 4]),
+                w_bfs[g][:, :, 0:places].rearrange("p (c i) t -> p c t i", i=4),
+                probs[g][:, 0:places, :].rearrange("p t (c i) -> p c t i", i=4),
+                vs_got[:, g].rearrange("p (t x) -> p t x", t=PACK)[:, 0:places, 0:4].unsqueeze(1).to_broadcast([P, NQ // 4, places, 4]),
                 MULT,
             )
-        for t in range(PACK):
-            nc.scalar.activation(w_bfs[1][:, queries:NQ, t], probs[1][:, t, queries:NQ], COPY, scale=vs_got[:, 1, t * P : t * P + 1])
+        nc.vector.tensor_scalar(w_bfs[1][:, :, last], last_prob[:], vs_got[:, 1, last * P : last * P + 1], None, MULT)
         weights = []
         for g in range(PAGES):
-            w_codes = shared.tile([P, NQ], U32, name="w_codes%d" % g, align_bytes=64, offset=(12288, 2048)[g])
+            w_codes = shared.tile([P, NQ], U32, name="w_codes%d" % g, align_bytes=64, offset=AT_PROB + 2048 + 512 * g)
             w_scales = sb.tile([P, NQ], U8, name="w_scales%d" % g, align_bytes=64)
             nc.vector.quantize_mx(out=w_codes[:].bitcast(FP8X4), scales=w_scales[:], in_=w_bfs[g][:].rearrange("p q t -> p (q t)"))
             weights.append((w_codes, w_scales))
 
-        y = ps.tile([P, DV], F32, name="y", tag="bank0")
+        half = DV // 2
+        ys = [ps.tile([P, half], F32, name="y%d" % h, tag="bank%d" % h) for h in range(2)]
         for g in range(PAGES):
             w_codes, w_scales = weights[g]
-            nc.tensor.matmul_mx(
-                out=y[:],
-                lhsT=w_codes[:].bitcast(FP8X4),
-                lhsT_scale=w_scales[:],
-                rhs=vw_got[:, g * DV : (g + 1) * DV].bitcast(FP8X4),
-                rhs_scale=vsc_plane[:].bitcast(U8)[:, g * DV : (g + 1) * DV],
-                start=(g == 0),
-                stop=(g == PAGES - 1),
-            )
+            for h in range(2):
+                cols = slice(g * DV + h * half, g * DV + (h + 1) * half)
+                nc.tensor.matmul_mx(
+                    out=ys[h][:],
+                    lhsT=w_codes[:].bitcast(FP8X4),
+                    lhsT_scale=w_scales[:],
+                    rhs=vw_got[:, cols].bitcast(FP8X4),
+                    rhs_scale=vsc_plane[:].bitcast(U8)[:, cols],
+                    start=(g == 0),
+                    stop=(g == PAGES - 1),
+                )
         result = sb.tile([P, DV], F32, name="result")
-        nc.scalar.activation(result[:], y[:], COPY, scale=1.0 / 16.0)
+        nc.scalar.activation(result[:, 0:half], ys[0][:], COPY, scale=1.0 / 16.0)
+        nc.vector.tensor_scalar(result[:, half:DV], ys[1][:], 1.0 / 16.0, None, MULT)
         nc.sync.dma_start(out[0], result[:])

@@ -25,8 +25,9 @@ PASSES = D // (P * PACK)
 BLOCKS = POOL_PAGES * PACK
 KS_ROW = P - 16 * PASSES
 KW_HEAD = 512
-KB_FILL = 40
-KB_HEAD = 20
+KB_ROW = P - 2 * POOL_PAGES
+KB_FILL = 48
+KB_HEAD = 16
 VS_FILL = 56
 
 FLOPS = 2 * NQ * N * D + 2 * NQ * N * DV
@@ -54,33 +55,33 @@ def tile_attend_pkv4_sigmoid_bias_kernel(tc, qT, k_words, k_scales, v_words, v_s
 
         offs_sb = lists.tile([P, N // 16], U16, name="offs_sb")
         voffs_sb = lists.tile([P, PAGES * DV // 16], U16, name="voffs_sb")
-        kb_rows = sb.tile([P, PAGE], F32, name="kb_rows")
+        kb_rows = shared.tile([P, PAGE], F32, name="kb_rows", offset=AT_KS_DEALT)
         vs_rows = sb.tile([P, PAGE], F32, name="vs_rows")
         vsc_win = sb.tile([P, POOL_PAGES * DV // 4], I32, name="vsc_win")
         ks_win = shared.tile([P, T // 4], I32, name="ks_win", offset=AT_KS_WIN)
         kb_win = shared.tile([P, T], F32, name="kb_win", offset=AT_KB_WIN)
         kb_blocks = kb_win[:].rearrange("p (b x) -> p b x", b=BLOCKS)
 
-        nc.vector.memset(kb_rows[:], 0.0)
-        nc.vector.memset(vs_rows[:], 0.0)
         nc.vector.memset(vsc_win[:], 0)
+        nc.vector.memset(vs_rows[:], 0.0)
+        nc.vector.memset(kb_rows[0:KB_ROW, :], 0.0)
         nc.vector.memset(ks_win[0:KS_ROW, :], 0)
         nc.vector.memset(kb_blocks[:, 0:KB_HEAD, KB_FILL:P], 0.0)
 
         kb_shifted = kb.rearrange("r x -> (r x)")[0 : 2 * (T + 2)].rearrange("(s y) -> s y", s=2)[:, 0:T]
 
         nc.scalar.dma_start(ks_win[KS_ROW:P, :], k_scales.rearrange("o f t -> f o t").bitcast(I32))
+        nc.scalar.dma_start(kb_rows[KB_ROW:P, :], kb_shifted.rearrange("s (u x) -> u s x", u=POOL_PAGES))
         nc.sync.dma_start(offs_sb[:], offs)
         nc.sync.dma_start(voffs_sb[:], voffs)
         kw_win = sb.tile([P, T], I32, name="kw_win")
         kw_hbm = k_words[0].rearrange("p t b -> p (t b)").bitcast(I32)
         nc.sync.dma_start(kw_win[:, 0:KW_HEAD], kw_hbm[:, 0:KW_HEAD])
-        nc.sync.dma_start(kb_rows[0:64:4, :], kb_shifted.rearrange("s (u x) -> u s x", u=POOL_PAGES))
-        nc.sync.dma_start(vs_rows[0:32:4, :], vs[0].rearrange("(u x) -> u x", u=POOL_PAGES))
         nc.sync.dma_start(
             vsc_win[0:64:4, :].rearrange("p (g e) -> p g e", g=POOL_PAGES),
             v_scales.rearrange("g f e -> f g e").bitcast(I32),
         )
+        nc.sync.dma_start(vs_rows[0:32:4, :], vs[0].rearrange("(u x) -> u x", u=POOL_PAGES))
         nc.sync.dma_start(kw_win[:, KW_HEAD:T], kw_hbm[:, KW_HEAD:T])
         q_rows = qT[0].rearrange("(o p j) q -> o p j q", o=PASSES, j=PACK)
         q_raws = []
@@ -103,18 +104,18 @@ def tile_attend_pkv4_sigmoid_bias_kernel(tc, qT, k_words, k_scales, v_words, v_s
             nc.tensor.transpose(vs_turned[:, t, :], vs_rows[:, t:PAGE:PACK], ident[:])
         nc.scalar.copy(
             kb_blocks[:, :, 0:KB_FILL].rearrange("p (r c) x -> p r c x", c=2),
-            kb_turned[:, :, 0:64:4].rearrange("p c r -> p r c").unsqueeze(3).to_broadcast([P, BLOCKS // 2, 2, KB_FILL]),
+            kb_turned[:, :, KB_ROW:P].rearrange("p c r -> p r c").unsqueeze(3).to_broadcast([P, BLOCKS // 2, 2, KB_FILL]),
         )
 
         ks_got = shared.tile([P, N], U8, name="ks_got", offset=AT_KS_GOT)
         nc.vector.tensor_copy(ks_got[:], ks_win[:].bitcast(U8).indirect(offs_sb[:]))
+        vsc_got = sb.tile([P, PAGES * DV // 4], I32, name="vsc_got")
+        nc.vector.tensor_copy(vsc_got[:].bitcast(U8), vsc_win[:].bitcast(U8).indirect(voffs_sb[:]))
         ks_dealt = shared.tile([P, N // 4], I32, name="ks_dealt", offset=AT_KS_DEALT)
         nc.vector.tensor_copy(
             ks_dealt[:].bitcast(U8).rearrange("p (g t m) -> p g t m", g=PAGES, t=PACK),
             ks_got[:].rearrange("p (g m t) -> p g t m", g=PAGES, t=PACK),
         )
-        vsc_got = shared.tile([P, PAGES * DV // 4], I32, name="vsc_got", offset=AT_KS_WIN)
-        nc.vector.tensor_copy(vsc_got[:].bitcast(U8), vsc_win[:].bitcast(U8).indirect(voffs_sb[:]))
         kb_got = shared.tile([P, N], F32, name="kb_got", offset=AT_KB_GOT)
         nc.vector.tensor_copy(kb_got[:], kb_win[:].indirect(offs_sb[:]))
         vs_win = shared.tile([P, T], F32, name="vs_win", offset=AT_VS_WIN)
@@ -189,7 +190,7 @@ def tile_attend_pkv4_sigmoid_bias_kernel(tc, qT, k_words, k_scales, v_words, v_s
         quantise_queries(0)
         for t in range(PACK):
             score_pass(0, t, 0, first_keys[0][:, t * 2 * P : (t + 1) * 2 * P])
-        kw_got1 = shared.tile([P, PAGE], U32, name="kw_got1", offset=AT_KS_DEALT)
+        kw_got1 = shared.tile([P, PAGE], U32, name="kw_got1", offset=AT_Q_RAW[0])
         words1 = gather_keys(kw_got1, 1)
         quantise_queries(1)
         for t in range(PACK):

@@ -26,9 +26,10 @@ BLOCKS = POOL_PAGES * PACK
 KS_ROW = P - 16 * PASSES
 KW_HEAD = 512
 KB_ROW = P - 2 * POOL_PAGES
-KB_FILL = 48
-KB_HEAD = 16
-VS_FILL = 56
+KB_FILL = 32
+KB_HEAD = 20
+VS_FILL = 64
+VECTOR_Q = 96
 
 FLOPS = 2 * NQ * N * D + 2 * NQ * N * DV
 BYTES = 4 * D * NQ + 4 * P * T + 32 * T + 4 * P * POOL_PAGES * DV + 16 * POOL_PAGES * DV + 8 * T + 2 * P * (N + PAGES * DV) // 16 + 4 * NQ * DV
@@ -40,7 +41,6 @@ AT_KB_WIN = 26624
 AT_Q_RAW = (43008, 47104)
 AT_KB_GOT = 53248
 AT_KS_WIN = 57344
-AT_PROB = 61440
 AT_KS_DEALT = 65536
 AT_FIRST_KEYS = 67584
 
@@ -55,7 +55,7 @@ def tile_attend_pkv4_sigmoid_bias_kernel(tc, qT, k_words, k_scales, v_words, v_s
 
         offs_sb = lists.tile([P, N // 16], U16, name="offs_sb")
         voffs_sb = lists.tile([P, PAGES * DV // 16], U16, name="voffs_sb")
-        kb_rows = shared.tile([P, PAGE], F32, name="kb_rows", offset=AT_KS_DEALT)
+        kb_rows = sb.tile([P, PAGE], F32, name="kb_rows")
         vs_rows = sb.tile([P, PAGE], F32, name="vs_rows")
         vsc_win = sb.tile([P, POOL_PAGES * DV // 4], I32, name="vsc_win")
         ks_win = shared.tile([P, T // 4], I32, name="ks_win", offset=AT_KS_WIN)
@@ -109,13 +109,13 @@ def tile_attend_pkv4_sigmoid_bias_kernel(tc, qT, k_words, k_scales, v_words, v_s
 
         ks_got = shared.tile([P, N], U8, name="ks_got", offset=AT_KS_GOT)
         nc.vector.tensor_copy(ks_got[:], ks_win[:].bitcast(U8).indirect(offs_sb[:]))
-        vsc_got = sb.tile([P, PAGES * DV // 4], I32, name="vsc_got")
-        nc.vector.tensor_copy(vsc_got[:].bitcast(U8), vsc_win[:].bitcast(U8).indirect(voffs_sb[:]))
         ks_dealt = shared.tile([P, N // 4], I32, name="ks_dealt", offset=AT_KS_DEALT)
         nc.vector.tensor_copy(
             ks_dealt[:].bitcast(U8).rearrange("p (g t m) -> p g t m", g=PAGES, t=PACK),
             ks_got[:].rearrange("p (g m t) -> p g t m", g=PAGES, t=PACK),
         )
+        vsc_got = shared.tile([P, PAGES * DV // 4], I32, name="vsc_got", offset=AT_KS_WIN)
+        nc.vector.tensor_copy(vsc_got[:].bitcast(U8), vsc_win[:].bitcast(U8).indirect(voffs_sb[:]))
         kb_got = shared.tile([P, N], F32, name="kb_got", offset=AT_KB_GOT)
         nc.vector.tensor_copy(kb_got[:], kb_win[:].indirect(offs_sb[:]))
         vs_win = shared.tile([P, T], F32, name="vs_win", offset=AT_VS_WIN)
@@ -139,29 +139,36 @@ def tile_attend_pkv4_sigmoid_bias_kernel(tc, qT, k_words, k_scales, v_words, v_s
         for u in (0, 2, 1, 3):
             nc.sync.dma_start(vsc_plane[32 * u : 32 * u + 4, :], vsc_got[16 * u : 16 * (u + 1) : 4, :])
 
-        q_bfs, q_ops = [], []
-        for o in range(PASSES):
-            q_bf = shared.tile([P, NQ, PACK], BF16, name="q_bf%d" % o, align_bytes=64, offset=AT_KB_WIN + 1024 * o)
-            nc.scalar.copy(
+        def cast_queries(copy, q_bf, o, first, count):
+            copy(
                 q_bf[:].rearrange("p (c i) j -> p c j i", i=4),
-                q_raws[o][:].rearrange("p j (c i) -> p c j i", i=4),
+                q_raws[o][:, :, first : first + count].rearrange("p j (c i) -> p c j i", i=4),
             )
-            q_bfs.append(q_bf)
+
+        q_first = shared.tile([P, NQ, PACK], BF16, name="q_first", align_bytes=64, offset=AT_KB_WIN)
+        cast_queries(nc.scalar.copy, q_first, 0, 0, NQ)
+        q_second = shared.tile([P, NQ // 2, PACK], BF16, name="q_second", align_bytes=64, offset=AT_KB_WIN + 1024)
+        cast_queries(nc.scalar.copy, q_second, 1, 0, NQ // 2)
+        q_third = shared.tile([P, NQ // 2, PACK], BF16, name="q_third", align_bytes=64, offset=AT_Q_RAW[0] + 1024)
+        q_ops = [
+            (sb.tile([P, NQ], U32, name="q_codes%d" % o, align_bytes=64), sb.tile([P, NQ], U8, name="q_scales%d" % o, align_bytes=64))
+            for o in range(PASSES)
+        ]
 
         def gather_keys(kw_got, g):
             cols = slice(g * PAGE // 16, (g + 1) * PAGE // 16)
             nc.vector.tensor_copy(kw_got[:], kw_win[:].bitcast(U32).indirect(offs_sb[:, cols]))
             return kw_got[:].bitcast(U16).rearrange("p (m t o) -> p o m t", t=PACK, o=PASSES)
 
-        def quantise_queries(o):
-            q_codes = sb.tile([P, NQ], U32, name="q_codes%d" % o, align_bytes=64)
-            q_scales = sb.tile([P, NQ], U8, name="q_scales%d" % o, align_bytes=64)
-            nc.vector.quantize_mx(out=q_codes[:].bitcast(FP8X4), scales=q_scales[:], in_=q_bfs[o][:].rearrange("p q j -> p (q j)"))
-            q_ops.append((q_codes, q_scales))
+        def quantise_queries(q_bf, o, first, count):
+            q_codes, q_scales = q_ops[o]
+            nc.vector.quantize_mx(
+                out=q_codes[:, first : first + count].bitcast(FP8X4),
+                scales=q_scales[:, first : first + count],
+                in_=q_bf[:].rearrange("p q j -> p (q j)"),
+            )
 
-        last = PACK - 1
-        probs = [shared.tile([P, PACK - g, NQ], F32, name="prob%d" % g, offset=AT_PROB + 2048 * g) for g in range(PAGES)]
-        last_prob = sb.tile([P, NQ], F32, name="last_prob")
+        probs = [sb.tile([P, PACK, NQ], F32, name="prob%d" % g) for g in range(PAGES)]
         scores = {}
 
         def score_pass(g, t, o, keys):
@@ -178,29 +185,30 @@ def tile_attend_pkv4_sigmoid_bias_kernel(tc, qT, k_words, k_scales, v_words, v_s
                 stop=(o == PASSES - 1),
             )
             if o == PASSES - 1:
-                nc.scalar.activation(last_prob[:] if (g, t) == (1, last) else probs[g][:, t, :], scores[g, t][:], SIGMOID, bias=kb_got[:, first : first + 1])
+                nc.scalar.activation(probs[g][:, t, :], scores[g, t][:], SIGMOID, bias=kb_got[:, first : first + 1])
 
-        kw_got0 = shared.tile([P, PAGE], U32, name="kw_got0", offset=AT_KB_WIN + 4096)
-        words0 = gather_keys(kw_got0, 0)
-        first_keys = []
-        for o in range(PASSES):
-            keys = shared.tile([P, 1024], U8, name="first_keys%d" % o, align_bytes=64, offset=AT_FIRST_KEYS + 8192 * o)
-            nc.vector.tensor_copy(keys[:].bitcast(U16).rearrange("p (t m) -> p m t", t=PACK), words0[:, o])
-            first_keys.append(keys)
-        quantise_queries(0)
+        words = []
+        for g in range(PAGES):
+            kw_got = shared.tile([P, PAGE], U32, name="kw_got%d" % g, offset=AT_KB_WIN + 4096 + 2048 * g)
+            words.append(gather_keys(kw_got, g))
+        first_keys = shared.tile([P, 1024], U8, name="first_keys", align_bytes=64, offset=AT_FIRST_KEYS)
+        nc.vector.tensor_copy(first_keys[:].bitcast(U16).rearrange("p (t m) -> p m t", t=PACK), words[0][:, 0])
+        quantise_queries(q_first, 0, 0, NQ)
         for t in range(PACK):
-            score_pass(0, t, 0, first_keys[0][:, t * 2 * P : (t + 1) * 2 * P])
-        kw_got1 = shared.tile([P, PAGE], U32, name="kw_got1", offset=AT_Q_RAW[0])
-        words1 = gather_keys(kw_got1, 1)
-        quantise_queries(1)
+            score_pass(0, t, 0, first_keys[:, t * 2 * P : (t + 1) * 2 * P])
+        cast_queries(nc.vector.tensor_copy, q_third, 1, NQ // 2, NQ // 2)
+        second_keys = shared.tile([P, 1024], U8, name="second_keys", align_bytes=64, offset=AT_Q_RAW[0])
+        nc.vector.tensor_copy(second_keys[:].bitcast(U16).rearrange("p (t m) -> p m t", t=PACK), words[0][:, 1])
+        quantise_queries(q_second, 1, 0, NQ // 2)
+        quantise_queries(q_third, 1, NQ // 2, NQ // 2)
         for t in range(PACK):
-            score_pass(0, t, 1, first_keys[1][:, t * 2 * P : (t + 1) * 2 * P])
-        later_keys = sb.tile([P, 2 * 1024], U8, name="later_keys", align_bytes=64)
+            score_pass(0, t, 1, second_keys[:, t * 2 * P : (t + 1) * 2 * P])
+        later_keys = shared.tile([P, 2 * 1024], U8, name="later_keys", align_bytes=64, offset=AT_Q_RAW[1])
         for pair in range(2):
             keys = later_keys[:, pair * 1024 : (pair + 1) * 1024]
             nc.vector.tensor_copy(
                 keys.bitcast(U16).rearrange("p (o u m) -> p o m u", o=PASSES, u=2),
-                words1[:, :, :, 2 * pair : 2 * pair + 2],
+                words[1][:, :, :, 2 * pair : 2 * pair + 2],
             )
             for u in range(2):
                 for o in range(PASSES):
@@ -215,19 +223,20 @@ def tile_attend_pkv4_sigmoid_bias_kernel(tc, qT, k_words, k_scales, v_words, v_s
 
         w_bfs = [
             sb.tile([P, NQ, PACK], BF16, name="w_bf0", align_bytes=64),
-            shared.tile([P, NQ, PACK], BF16, name="w_bf1", align_bytes=64, offset=AT_VW_WIN + 1024),
+            shared.tile([P, NQ, PACK], BF16, name="w_bf1", align_bytes=64, offset=AT_KB_GOT + 1024),
         ]
-        for g, engine, places in ((0, nc.gpsimd, PACK), (1, nc.vector, PACK - 1)):
+        for g, engine, queries in ((0, nc.gpsimd, NQ), (1, nc.vector, VECTOR_Q)):
             engine.tensor_tensor(
-                w_bfs[g][:, :, 0:places].rearrange("p (c i) t -> p c t i", i=4),
-                probs[g][:, 0:places, :].rearrange("p t (c i) -> p c t i", i=4),
-                vs_got[:, g].rearrange("p (t x) -> p t x", t=PACK)[:, 0:places, 0:4].unsqueeze(1).to_broadcast([P, NQ // 4, places, 4]),
+                w_bfs[g][:, 0:queries, :].rearrange("p (c i) t -> p c t i", i=4),
+                probs[g][:, :, 0:queries].rearrange("p t (c i) -> p c t i", i=4),
+                vs_got[:, g].rearrange("p (t x) -> p t x", t=PACK)[:, :, 0:4].unsqueeze(1).to_broadcast([P, queries // 4, PACK, 4]),
                 MULT,
             )
-        nc.vector.tensor_scalar(w_bfs[1][:, :, last], last_prob[:], vs_got[:, 1, last * P : last * P + 1], None, MULT)
+        for t in range(PACK):
+            nc.scalar.activation(w_bfs[1][:, VECTOR_Q:NQ, t], probs[1][:, t, VECTOR_Q:NQ], COPY, scale=vs_got[:, 1, t * P : t * P + 1])
         weights = []
         for g in range(PAGES):
-            w_codes = shared.tile([P, NQ], U32, name="w_codes%d" % g, align_bytes=64, offset=AT_PROB + 2048 + 512 * g)
+            w_codes = shared.tile([P, NQ], U32, name="w_codes%d" % g, align_bytes=64, offset=AT_KB_GOT + 512 * g)
             w_scales = sb.tile([P, NQ], U8, name="w_scales%d" % g, align_bytes=64)
             nc.vector.quantize_mx(out=w_codes[:].bitcast(FP8X4), scales=w_scales[:], in_=w_bfs[g][:].rearrange("p q t -> p (q t)"))
             weights.append((w_codes, w_scales))

@@ -197,13 +197,15 @@ def tile_attend_pkv4_sigmoid_bias_kernel(tc, qT, k_words, k_scales, v_words, v_s
         for t in range(PACK):
             score_pass(0, t, 0, first_keys[:, t * 2 * P : (t + 1) * 2 * P])
         cast_queries(nc.vector.tensor_copy, q_third, 1, NQ // 2, NQ // 2)
+        vs_first = shared.tile([P, PAGE], F32, name="vs_first", offset=AT_Q_RAW[1] + 1984)
+        nc.scalar.activation(vs_first[:], vs_win[:].indirect(offs_sb[:, 0 : PAGE // 16]), COPY)
         second_keys = shared.tile([P, 1024], U8, name="second_keys", align_bytes=64, offset=AT_Q_RAW[0])
         nc.vector.tensor_copy(second_keys[:].bitcast(U16).rearrange("p (t m) -> p m t", t=PACK), words[0][:, 1])
         quantise_queries(q_second, 1, 0, NQ // 2)
         quantise_queries(q_third, 1, NQ // 2, NQ // 2)
         for t in range(PACK):
             score_pass(0, t, 1, second_keys[:, t * 2 * P : (t + 1) * 2 * P])
-        later_keys = shared.tile([P, 2 * 1024], U8, name="later_keys", align_bytes=64, offset=AT_Q_RAW[1])
+        later_keys = shared.tile([P, 2 * 1024], U8, name="later_keys", align_bytes=64, offset=AT_Q_RAW[1] - 1984)
         for pair in range(2):
             keys = later_keys[:, pair * 1024 : (pair + 1) * 1024]
             nc.vector.tensor_copy(
@@ -214,26 +216,27 @@ def tile_attend_pkv4_sigmoid_bias_kernel(tc, qT, k_words, k_scales, v_words, v_s
                 for o in range(PASSES):
                     score_pass(1, 2 * pair + u, o, keys[:, (o * 2 + u) * 2 * P : (o * 2 + u + 1) * 2 * P])
 
-        vs_got = shared.tile([P, PAGES, PAGE], F32, name="vs_got", offset=AT_FIRST_KEYS)
-        for g in range(PAGES):
-            cols = slice(g * PAGE // 16, (g + 1) * PAGE // 16)
-            nc.vector.tensor_copy(vs_got[:, g], vs_win[:].indirect(offs_sb[:, cols]))
-        vw_got = sb.tile([P, PAGES * DV], U32, name="vw_got", align_bytes=64)
-        nc.vector.tensor_copy(vw_got[:], vw_win[:].bitcast(U32).indirect(voffs_sb[:]))
-
+        vs_gots = [vs_first, shared.tile([P, PAGE], F32, name="vs_second", offset=AT_FIRST_KEYS)]
+        nc.vector.tensor_copy(vs_gots[1][:], vs_win[:].indirect(offs_sb[:, PAGE // 16 : N // 16]))
         w_bfs = [
             sb.tile([P, NQ, PACK], BF16, name="w_bf0", align_bytes=64),
             shared.tile([P, NQ, PACK], BF16, name="w_bf1", align_bytes=64, offset=AT_KB_GOT + 1024),
         ]
-        for g, engine, queries in ((0, nc.gpsimd, NQ), (1, nc.vector, VECTOR_Q)):
-            engine.tensor_tensor(
+
+        def weigh(g, queries):
+            nc.vector.tensor_tensor(
                 w_bfs[g][:, 0:queries, :].rearrange("p (c i) t -> p c t i", i=4),
                 probs[g][:, :, 0:queries].rearrange("p t (c i) -> p c t i", i=4),
-                vs_got[:, g].rearrange("p (t x) -> p t x", t=PACK)[:, :, 0:4].unsqueeze(1).to_broadcast([P, queries // 4, PACK, 4]),
+                vs_gots[g][:].rearrange("p (t x) -> p t x", t=PACK)[:, :, 0:4].unsqueeze(1).to_broadcast([P, queries // 4, PACK, 4]),
                 MULT,
             )
+
+        weigh(0, NQ)
+        vw_got = sb.tile([P, PAGES * DV], U32, name="vw_got", align_bytes=64)
+        nc.vector.tensor_copy(vw_got[:], vw_win[:].bitcast(U32).indirect(voffs_sb[:]))
+        weigh(1, VECTOR_Q)
         for t in range(PACK):
-            nc.scalar.activation(w_bfs[1][:, VECTOR_Q:NQ, t], probs[1][:, t, VECTOR_Q:NQ], COPY, scale=vs_got[:, 1, t * P : t * P + 1])
+            nc.scalar.activation(w_bfs[1][:, VECTOR_Q:NQ, t], probs[1][:, t, VECTOR_Q:NQ], COPY, scale=vs_gots[1][:, t * P : t * P + 1])
         weights = []
         for g in range(PAGES):
             w_codes = shared.tile([P, NQ], U32, name="w_codes%d" % g, align_bytes=64, offset=AT_KB_GOT + 512 * g)

@@ -259,7 +259,8 @@ def tile_attend_pkv4_sigmoid_bias_kernel(tc, qT, k_words, k_scales, v_words, v_s
                     start=(g == 0),
                     stop=(g == PAGES - 1),
                 )
-        result = sb.tile([P, DV], F32, name="result")
-        nc.scalar.activation(result[:, 0:half], ys[0][:], COPY, scale=1.0 / 16.0)
-        nc.vector.tensor_scalar(result[:, half:DV], ys[1][:], 1.0 / 16.0, None, MULT)
-        nc.sync.dma_start(out[0], result[:])
+        results = [sb.tile([P, half], F32, name="result%d" % h) for h in range(2)]
+        nc.scalar.activation(results[0][:], ys[0][:], COPY, scale=1.0 / 16.0)
+        nc.vector.tensor_scalar(results[1][:], ys[1][:], 1.0 / 16.0, None, MULT)
+        for h in range(2):
+            nc.sync.dma_start(out[0][:, h * half : (h + 1) * half], results[h][:])

@@ -218,31 +218,46 @@ def tile_attend_pkv4_sigmoid_bias_kernel(tc, qT, k_words, k_scales, v_words, v_s
 
         vs_gots = [vs_first, shared.tile([P, PAGE], F32, name="vs_second", offset=AT_FIRST_KEYS)]
         nc.vector.tensor_copy(vs_gots[1][:], vs_win[:].indirect(offs_sb[:, PAGE // 16 : N // 16]))
-        w_bfs = [
-            sb.tile([P, NQ, PACK], BF16, name="w_bf0", align_bytes=64),
-            shared.tile([P, NQ, PACK], BF16, name="w_bf1", align_bytes=64, offset=AT_KB_GOT + 1024),
+        w_first = sb.tile([P, NQ, PACK], BF16, name="w_first", align_bytes=64)
+        w_late = [
+            shared.tile([P, NQ // 2, PACK], BF16, name="w_late%d" % i, align_bytes=64, offset=AT_KB_GOT + 1024 + 512 * i) for i in range(2)
+        ]
+        weights = [
+            (
+                shared.tile([P, NQ], U32, name="w_codes%d" % g, align_bytes=64, offset=AT_KB_GOT + 512 * g),
+                sb.tile([P, NQ], U8, name="w_scales%d" % g, align_bytes=64),
+            )
+            for g in range(PAGES)
         ]
 
-        def weigh(g, queries):
+        def weigh(w_bf, g, first, count):
             nc.vector.tensor_tensor(
-                w_bfs[g][:, 0:queries, :].rearrange("p (c i) t -> p c t i", i=4),
-                probs[g][:, :, 0:queries].rearrange("p t (c i) -> p c t i", i=4),
-                vs_gots[g][:].rearrange("p (t x) -> p t x", t=PACK)[:, :, 0:4].unsqueeze(1).to_broadcast([P, queries // 4, PACK, 4]),
+                w_bf.rearrange("p (c i) t -> p c t i", i=4),
+                probs[g][:, :, first : first + count].rearrange("p t (c i) -> p c t i", i=4),
+                vs_gots[g][:].rearrange("p (t x) -> p t x", t=PACK)[:, :, 0:4].unsqueeze(1).to_broadcast([P, count // 4, PACK, 4]),
                 MULT,
             )
 
-        weigh(0, NQ)
+        def quantise_weights(w_bf, g, first, count):
+            w_codes, w_scales = weights[g]
+            nc.vector.quantize_mx(
+                out=w_codes[:, first : first + count].bitcast(FP8X4),
+                scales=w_scales[:, first : first + count],
+                in_=w_bf[:].rearrange("p q t -> p (q t)"),
+            )
+
+        weigh(w_first[:], 0, 0, NQ)
         vw_got = sb.tile([P, PAGES * DV], U32, name="vw_got", align_bytes=64)
         nc.vector.tensor_copy(vw_got[:], vw_win[:].bitcast(U32).indirect(voffs_sb[:]))
-        weigh(1, VECTOR_Q)
+        weigh(w_late[0][:], 1, 0, NQ // 2)
+        weigh(w_late[1][:, 0 : VECTOR_Q - NQ // 2, :], 1, NQ // 2, VECTOR_Q - NQ // 2)
         for t in range(PACK):
-            nc.scalar.activation(w_bfs[1][:, VECTOR_Q:NQ, t], probs[1][:, t, VECTOR_Q:NQ], COPY, scale=vs_gots[1][:, t * P : t * P + 1])
-        weights = []
-        for g in range(PAGES):
-            w_codes = shared.tile([P, NQ], U32, name="w_codes%d" % g, align_bytes=64, offset=AT_KB_GOT + 512 * g)
-            w_scales = sb.tile([P, NQ], U8, name="w_scales%d" % g, align_bytes=64)
-            nc.vector.quantize_mx(out=w_codes[:].bitcast(FP8X4), scales=w_scales[:], in_=w_bfs[g][:].rearrange("p q t -> p (q t)"))
-            weights.append((w_codes, w_scales))
+            nc.scalar.activation(
+                w_late[1][:, VECTOR_Q - NQ // 2 : NQ // 2, t], probs[1][:, t, VECTOR_Q:NQ], COPY, scale=vs_gots[1][:, t * P : t * P + 1]
+            )
+        quantise_weights(w_first, 0, 0, NQ)
+        for i in range(2):
+            quantise_weights(w_late[i], 1, i * NQ // 2, NQ // 2)
 
         half = DV // 2
         ys = [ps.tile([P, half], F32, name="y%d" % h, tag="bank%d" % h) for h in range(2)]
@@ -262,5 +277,5 @@ def tile_attend_pkv4_sigmoid_bias_kernel(tc, qT, k_words, k_scales, v_words, v_s
         results = [sb.tile([P, half], F32, name="result%d" % h) for h in range(2)]
         nc.scalar.activation(results[0][:], ys[0][:], COPY, scale=1.0 / 16.0)
         nc.vector.tensor_scalar(results[1][:], ys[1][:], 1.0 / 16.0, None, MULT)
-        for h in range(2):
-            nc.sync.dma_start(out[0][:, h * half : (h + 1) * half], results[h][:])
+        for h, queue in enumerate((nc.scalar, nc.sync)):
+            queue.dma_start(out[0][:, h * half : (h + 1) * half], results[h][:])

@@ -277,5 +277,5 @@ def tile_attend_pkv4_sigmoid_bias_kernel(tc, qT, k_words, k_scales, v_words, v_s
         results = [sb.tile([P, half], F32, name="result%d" % h) for h in range(2)]
         nc.scalar.activation(results[0][:], ys[0][:], COPY, scale=1.0 / 16.0)
         nc.vector.tensor_scalar(results[1][:], ys[1][:], 1.0 / 16.0, None, MULT)
-        for h, queue in enumerate((nc.scalar, nc.sync)):
-            queue.dma_start(out[0][:, h * half : (h + 1) * half], results[h][:])
+        for h in range(2):
+            nc.sync.dma_start(out[0][:, h * half : (h + 1) * half], results[h][:])

@@ -26,9 +26,9 @@ BLOCKS = POOL_PAGES * PACK
 KS_ROW = P - 16 * PASSES
 KW_HEAD = 512
 KB_ROW = P - 2 * POOL_PAGES
-KB_FILL = 32
-KB_HEAD = 20
-VS_FILL = 64
+KB_FILL = 64
+KB_HEAD = 16
+VS_FILL = 40
 VECTOR_Q = 96
 
 FLOPS = 2 * NQ * N * D + 2 * NQ * N * DV

@@ -30,13 +30,14 @@ KB_FILL = 64
 KB_HEAD = 16
 VS_FILL = 40
 VECTOR_Q = 96
+DMA_ALIGN = 256
 
 FLOPS = 2 * NQ * N * D + 2 * NQ * N * DV
 BYTES = 4 * D * NQ + 4 * P * T + 32 * T + 4 * P * POOL_PAGES * DV + 16 * POOL_PAGES * DV + 8 * T + 2 * P * (N + PAGES * DV) // 16 + 4 * NQ * DV
 
 AT_VS_WIN = 0
 AT_KS_GOT = 16320
-AT_VW_WIN = 17280
+AT_VW_WIN = 17152
 AT_KB_WIN = 26624
 AT_Q_RAW = (43008, 47104)
 AT_KB_GOT = 53248
@@ -55,9 +56,9 @@ def tile_attend_pkv4_sigmoid_bias_kernel(tc, qT, k_words, k_scales, v_words, v_s
 
         offs_sb = lists.tile([P, N // 16], U16, name="offs_sb")
         voffs_sb = lists.tile([P, PAGES * DV // 16], U16, name="voffs_sb")
-        kb_rows = sb.tile([P, PAGE], F32, name="kb_rows")
-        vs_rows = sb.tile([P, PAGE], F32, name="vs_rows")
-        vsc_win = sb.tile([P, POOL_PAGES * DV // 4], I32, name="vsc_win")
+        kb_rows = sb.tile([P, PAGE], F32, name="kb_rows", align_bytes=DMA_ALIGN)
+        vs_rows = sb.tile([P, PAGE], F32, name="vs_rows", align_bytes=DMA_ALIGN)
+        vsc_win = sb.tile([P, POOL_PAGES * DV // 4], I32, name="vsc_win", align_bytes=DMA_ALIGN)
         ks_win = shared.tile([P, T // 4], I32, name="ks_win", offset=AT_KS_WIN)
         kb_win = shared.tile([P, T], F32, name="kb_win", offset=AT_KB_WIN)
         kb_blocks = kb_win[:].rearrange("p (b x) -> p b x", b=BLOCKS)
@@ -74,7 +75,7 @@ def tile_attend_pkv4_sigmoid_bias_kernel(tc, qT, k_words, k_scales, v_words, v_s
         nc.scalar.dma_start(kb_rows[KB_ROW:P, :], kb_shifted.rearrange("s (u x) -> u s x", u=POOL_PAGES))
         nc.sync.dma_start(offs_sb[:], offs)
         nc.sync.dma_start(voffs_sb[:], voffs)
-        kw_win = sb.tile([P, T], I32, name="kw_win")
+        kw_win = sb.tile([P, T], I32, name="kw_win", align_bytes=DMA_ALIGN)
         kw_hbm = k_words[0].rearrange("p t b -> p (t b)").bitcast(I32)
         nc.sync.dma_start(kw_win[:, 0:KW_HEAD], kw_hbm[:, 0:KW_HEAD])
         nc.sync.dma_start(
@@ -125,12 +126,12 @@ def tile_attend_pkv4_sigmoid_bias_kernel(tc, qT, k_words, k_scales, v_words, v_s
             vs_blocks[:, :, 0:VS_FILL].rearrange("p (u t) x -> p u t x", t=PACK),
             vs_turned[:, :, 0:32:4].rearrange("p t u -> p u t").unsqueeze(3).to_broadcast([P, POOL_PAGES, PACK, VS_FILL]),
         )
-        ks_plane = sb.tile([P, PASSES * N // 4], I32, name="ks_plane", align_bytes=64)
+        ks_plane = sb.tile([P, PASSES * N // 4], I32, name="ks_plane", align_bytes=DMA_ALIGN)
         for u in (0, 2, 1, 3):
             nc.sync.dma_start(ks_plane[32 * u : 32 * u + 4, :], ks_dealt[KS_ROW + 8 * u : KS_ROW + 8 * (u + 1), :])
         ks_planes = [ks_plane[:].bitcast(U8)[:, o * N : (o + 1) * N] for o in range(PASSES)]
 
-        vw_win = shared.tile([P, POOL_PAGES * DV], I32, name="vw_win", offset=AT_VW_WIN)
+        vw_win = shared.tile([P, POOL_PAGES * DV], I32, name="vw_win", align_bytes=DMA_ALIGN, offset=AT_VW_WIN)
         nc.sync.dma_start(
             vw_win[:].rearrange("p (g e) -> p g e", g=POOL_PAGES),
             v_words.rearrange("g p e b -> p g (e b)").bitcast(I32),
@@ -274,7 +275,7 @@ def tile_attend_pkv4_sigmoid_bias_kernel(tc, qT, k_words, k_scales, v_words, v_s
                     start=(g == 0),
                     stop=(g == PAGES - 1),
                 )
-        results = [sb.tile([P, half], F32, name="result%d" % h) for h in range(2)]
+        results = [sb.tile([P, half], F32, name="result%d" % h, align_bytes=DMA_ALIGN) for h in range(2)]
         nc.scalar.activation(results[0][:], ys[0][:], COPY, scale=1.0 / 16.0)
         nc.vector.tensor_scalar(results[1][:], ys[1][:], 1.0 / 16.0, None, MULT)
         for h in range(2):

@@ -198,7 +198,7 @@ def tile_attend_pkv4_sigmoid_bias_kernel(tc, qT, k_words, k_scales, v_words, v_s
         for t in range(PACK):
             score_pass(0, t, 0, first_keys[:, t * 2 * P : (t + 1) * 2 * P])
         cast_queries(nc.vector.tensor_copy, q_third, 1, NQ // 2, NQ // 2)
-        vs_first = shared.tile([P, PAGE], F32, name="vs_first", offset=AT_Q_RAW[1] + 1984)
+        vs_first = shared.tile([P, PAGE], F32, name="vs_first", offset=AT_KB_WIN + 8192)
         nc.scalar.activation(vs_first[:], vs_win[:].indirect(offs_sb[:, 0 : PAGE // 16]), COPY)
         second_keys = shared.tile([P, 1024], U8, name="second_keys", align_bytes=64, offset=AT_Q_RAW[0])
         nc.vector.tensor_copy(second_keys[:].bitcast(U16).rearrange("p (t m) -> p m t", t=PACK), words[0][:, 1])

@@ -26,9 +26,10 @@ BLOCKS = POOL_PAGES * PACK
 KS_ROW = P - 16 * PASSES
 KW_HEAD = 512
 KB_ROW = P - 2 * POOL_PAGES
-KB_FILL = 64
-KB_HEAD = 16
-VS_FILL = 40
+KB_FILL = 40
+KB_HEAD = 13
+KB_TAIL = 25
+VS_FILL = 64
 VECTOR_Q = 96
 DMA_ALIGN = 256
 
@@ -91,11 +92,18 @@ def tile_attend_pkv4_sigmoid_bias_kernel(tc, qT, k_words, k_scales, v_words, v_s
             nc.sync.dma_start(q_raw[:], q_rows[o])
             q_raws.append(q_raw)
 
+        warm_in = sb.tile([32, 8], F32, name="warm_in")
+        nc.gpsimd.memset(warm_in[:], 0.0)
         ident = sb.tile([P, P], F32, name="ident")
         make_identity(nc, ident[:])
-        nc.gpsimd.memset(kb_blocks[:, KB_HEAD - 1 : BLOCKS, KB_FILL:P], 0.0)
+        nc.gpsimd.memset(kb_blocks[:, KB_HEAD - 1 : KB_TAIL, KB_FILL:P], 0.0)
         warm = sb.tile([32, 8], F32, name="warm")
-        nc.scalar.activation(warm[:], ident[0:32, 0:8], SIGMOID)
+        nc.scalar.activation(warm[:], warm_in[:], SIGMOID)
+
+        nc.scalar.copy(
+            kb_blocks[:, KB_TAIL:BLOCKS, KB_FILL:P],
+            kb_rows[:, KB_FILL:P].unsqueeze(1).to_broadcast([P, BLOCKS - KB_TAIL, P - KB_FILL]),
+        )
 
         kb_turned = ps.tile([P, 2, P], F32, name="kb_turned", tag="bank6")
         for c in range(2):
@@ -221,12 +229,12 @@ def tile_attend_pkv4_sigmoid_bias_kernel(tc, qT, k_words, k_scales, v_words, v_s
         nc.vector.tensor_copy(vs_gots[1][:], vs_win[:].indirect(offs_sb[:, PAGE // 16 : N // 16]))
         w_first = sb.tile([P, NQ, PACK], BF16, name="w_first", align_bytes=64)
         w_late = [
-            shared.tile([P, NQ // 2, PACK], BF16, name="w_late%d" % i, align_bytes=64, offset=AT_KB_GOT + 1024 + 512 * i) for i in range(2)
+            shared.tile([P, NQ // 2, PACK], BF16, name="w_late%d" % i, align_bytes=64, offset=AT_KS_WIN - 448 + 640 * i) for i in range(2)
         ]
         weights = [
             (
-                shared.tile([P, NQ], U32, name="w_codes%d" % g, align_bytes=64, offset=AT_KB_GOT + 512 * g),
-                sb.tile([P, NQ], U8, name="w_scales%d" % g, align_bytes=64),
+                sb.tile([P, NQ], U32, name="w_codes%d" % g, align_bytes=64),
+                shared.tile([P, NQ], U8, name="w_scales%d" % g, align_bytes=64, offset=AT_KS_WIN + 64 + 1024 * g),
             )
             for g in range(PAGES)
         ]

from contextlib import ExitStack

import concourse.mybir as mybir
from concourse.masks import make_identity

F32 = mybir.dt.float32
BF16 = mybir.dt.bfloat16
I32 = mybir.dt.int32
U32 = mybir.dt.uint32
U16 = mybir.dt.uint16
U8 = mybir.dt.uint8
FP8X4 = mybir.dt.float8_e4m3fn_x4
FP4X4 = mybir.dt.float4_e2m1fn_x4
SIGMOID = mybir.ActivationFunctionType.Sigmoid
COPY = mybir.ActivationFunctionType.Copy
MULT = mybir.AluOpType.mult

P = 128
PACK = 4
N, T, D, DV, NQ = 1024, 4096, 1024, 256, 128
PAGE = 512
PAGES = N // PAGE
POOL_PAGES = T // PAGE
PASSES = D // (P * PACK)
BLOCKS = POOL_PAGES * PACK
KS_ROW = P - 16 * PASSES
KW_HEAD = 512
KB_ROW = P - 2 * POOL_PAGES
KB_FILL = 40
KB_HEAD = 13
KB_TAIL = 25
VS_FILL = 64
VECTOR_Q = 96
DMA_ALIGN = 256

FLOPS = 2 * NQ * N * D + 2 * NQ * N * DV
BYTES = 4 * D * NQ + 4 * P * T + 32 * T + 4 * P * POOL_PAGES * DV + 16 * POOL_PAGES * DV + 8 * T + 2 * P * (N + PAGES * DV) // 16 + 4 * NQ * DV

AT_VS_WIN = 0
AT_KS_GOT = 16320
AT_VW_WIN = 17152
AT_KB_WIN = 26624
AT_Q_RAW = (43008, 47104)
AT_KB_GOT = 53248
AT_KS_WIN = 57344
AT_KS_DEALT = 65536
AT_FIRST_KEYS = 67584


def tile_attend_pkv4_sigmoid_bias_kernel(tc, qT, k_words, k_scales, v_words, v_scales, vs, kb, offs, voffs, out):
    nc = tc.nc
    with ExitStack() as ctx:
        lists = ctx.enter_context(tc.tile_pool(name="lists", bufs=1))
        sb = ctx.enter_context(tc.tile_pool(name="sb", bufs=1))
        shared = ctx.enter_context(tc.tile_pool(name="shared", bufs=1))
        ps = ctx.enter_context(tc.psum_pool(name="ps", bufs=1))

        offs_sb = lists.tile([P, N // 16], U16, name="offs_sb")
        voffs_sb = lists.tile([P, PAGES * DV // 16], U16, name="voffs_sb")
        kb_rows = sb.tile([P, PAGE], F32, name="kb_rows", align_bytes=DMA_ALIGN)
        vs_rows = sb.tile([P, PAGE], F32, name="vs_rows", align_bytes=DMA_ALIGN)
        vsc_win = sb.tile([P, POOL_PAGES * DV // 4], I32, name="vsc_win", align_bytes=DMA_ALIGN)
        ks_win = shared.tile([P, T // 4], I32, name="ks_win", offset=AT_KS_WIN)
        kb_win = shared.tile([P, T], F32, name="kb_win", offset=AT_KB_WIN)
        kb_blocks = kb_win[:].rearrange("p (b x) -> p b x", b=BLOCKS)

        nc.vector.memset(vsc_win[:], 0)
        nc.vector.memset(vs_rows[:], 0.0)
        nc.vector.memset(kb_rows[0:KB_ROW, :], 0.0)
        nc.vector.memset(ks_win[0:KS_ROW, :], 0)
        nc.vector.memset(kb_blocks[:, 0:KB_HEAD, KB_FILL:P], 0.0)

        kb_shifted = kb.rearrange("r x -> (r x)")[0 : 2 * (T + 2)].rearrange("(s y) -> s y", s=2)[:, 0:T]

        nc.scalar.dma_start(ks_win[KS_ROW:P, :], k_scales.rearrange("o f t -> f o t").bitcast(I32))
        nc.scalar.dma_start(kb_rows[KB_ROW:P, :], kb_shifted.rearrange("s (u x) -> u s x", u=POOL_PAGES))
        nc.sync.dma_start(offs_sb[:], offs)
        nc.sync.dma_start(voffs_sb[:], voffs)
        kw_win = sb.tile([P, T], I32, name="kw_win", align_bytes=DMA_ALIGN)
        kw_hbm = k_words[0].rearrange("p t b -> p (t b)").bitcast(I32)
        nc.sync.dma_start(kw_win[:, 0:KW_HEAD], kw_hbm[:, 0:KW_HEAD])
        nc.sync.dma_start(
            vsc_win[0:64:4, :].rearrange("p (g e) -> p g e", g=POOL_PAGES),
            v_scales.rearrange("g f e -> f g e").bitcast(I32),
        )
        nc.sync.dma_start(vs_rows[0:32:4, :], vs[0].rearrange("(u x) -> u x", u=POOL_PAGES))
        nc.sync.dma_start(kw_win[:, KW_HEAD:T], kw_hbm[:, KW_HEAD:T])
        q_rows = qT[0].rearrange("(o p j) q -> o p j q", o=PASSES, j=PACK)
        q_raws = []
        for o in range(PASSES):
            q_raw = shared.tile([P, PACK, NQ], F32, name="q_raw%d" % o, offset=AT_Q_RAW[o])
            nc.sync.dma_start(q_raw[:], q_rows[o])
            q_raws.append(q_raw)

        warm_in = sb.tile([32, 8], F32, name="warm_in")
        nc.gpsimd.memset(warm_in[:], 0.0)
        ident = sb.tile([P, P], F32, name="ident")
        make_identity(nc, ident[:])
        nc.gpsimd.memset(kb_blocks[:, KB_HEAD - 1 : KB_TAIL, KB_FILL:P], 0.0)
        warm = sb.tile([32, 8], F32, name="warm")
        nc.scalar.activation(warm[:], warm_in[:], SIGMOID)

        nc.scalar.copy(
            kb_blocks[:, KB_TAIL:BLOCKS, KB_FILL:P],
            kb_rows[:, KB_FILL:P].unsqueeze(1).to_broadcast([P, BLOCKS - KB_TAIL, P - KB_FILL]),
        )

        kb_turned = ps.tile([P, 2, P], F32, name="kb_turned", tag="bank6")
        for c in range(2):
            nc.tensor.transpose(kb_turned[:, c, :], kb_rows[:, c:PAGE:PACK], ident[:])
        vs_turned = ps.tile([P, PACK, P], F32, name="vs_turned", tag="bank7")
        for t in range(PACK):
            nc.tensor.transpose(vs_turned[:, t, :], vs_rows[:, t:PAGE:PACK], ident[:])
        nc.scalar.copy(
            kb_blocks[:, :, 0:KB_FILL].rearrange("p (r c) x -> p r c x", c=2),
            kb_turned[:, :, KB_ROW:P].rearrange("p c r -> p r c").unsqueeze(3).to_broadcast([P, BLOCKS // 2, 2, KB_FILL]),
        )

        ks_got = shared.tile([P, N], U8, name="ks_got", offset=AT_KS_GOT)
        nc.vector.tensor_copy(ks_got[:], ks_win[:].bitcast(U8).indirect(offs_sb[:]))
        ks_dealt = shared.tile([P, N // 4], I32, name="ks_dealt", offset=AT_KS_DEALT)
        nc.vector.tensor_copy(
            ks_dealt[:].bitcast(U8).rearrange("p (g t m) -> p g t m", g=PAGES, t=PACK),
            ks_got[:].rearrange("p (g m t) -> p g t m", g=PAGES, t=PACK),
        )
        vsc_got = shared.tile([P, PAGES * DV // 4], I32, name="vsc_got", offset=AT_KS_WIN)
        nc.vector.tensor_copy(vsc_got[:].bitcast(U8), vsc_win[:].bitcast(U8).indirect(voffs_sb[:]))
        kb_got = shared.tile([P, N], F32, name="kb_got", offset=AT_KB_GOT)
        nc.vector.tensor_copy(kb_got[:], kb_win[:].indirect(offs_sb[:]))
        vs_win = shared.tile([P, T], F32, name="vs_win", offset=AT_VS_WIN)
        vs_blocks = vs_win[:].rearrange("p (b x) -> p b x", b=BLOCKS)
        nc.gpsimd.memset(vs_blocks[:, :, VS_FILL:P], 0.0)
        nc.scalar.copy(
            vs_blocks[:, :, 0:VS_FILL].rearrange("p (u t) x -> p u t x", t=PACK),
            vs_turned[:, :, 0:32:4].rearrange("p t u -> p u t").unsqueeze(3).to_broadcast([P, POOL_PAGES, PACK, VS_FILL]),
        )
        ks_plane = sb.tile([P, PASSES * N // 4], I32, name="ks_plane", align_bytes=DMA_ALIGN)
        for u in (0, 2, 1, 3):
            nc.sync.dma_start(ks_plane[32 * u : 32 * u + 4, :], ks_dealt[KS_ROW + 8 * u : KS_ROW + 8 * (u + 1), :])
        ks_planes = [ks_plane[:].bitcast(U8)[:, o * N : (o + 1) * N] for o in range(PASSES)]

        vw_win = shared.tile([P, POOL_PAGES * DV], I32, name="vw_win", align_bytes=DMA_ALIGN, offset=AT_VW_WIN)
        nc.sync.dma_start(
            vw_win[:].rearrange("p (g e) -> p g e", g=POOL_PAGES),
            v_words.rearrange("g p e b -> p g (e b)").bitcast(I32),
        )
        vsc_plane = shared.tile([P, PAGES * DV // 4], I32, name="vsc_plane", align_bytes=64, offset=AT_KB_WIN + 2048)
        for u in (0, 2, 1, 3):
            nc.sync.dma_start(vsc_plane[32 * u : 32 * u + 4, :], vsc_got[16 * u : 16 * (u + 1) : 4, :])

        def cast_queries(copy, q_bf, o, first, count):
            copy(
                q_bf[:].rearrange("p (c i) j -> p c j i", i=4),
                q_raws[o][:, :, first : first + count].rearrange("p j (c i) -> p c j i", i=4),
            )

        q_first = shared.tile([P, NQ, PACK], BF16, name="q_first", align_bytes=64, offset=AT_KB_WIN)
        cast_queries(nc.scalar.copy, q_first, 0, 0, NQ)
        q_second = shared.tile([P, NQ // 2, PACK], BF16, name="q_second", align_bytes=64, offset=AT_KB_WIN + 1024)
        cast_queries(nc.scalar.copy, q_second, 1, 0, NQ // 2)
        q_third = shared.tile([P, NQ // 2, PACK], BF16, name="q_third", align_bytes=64, offset=AT_Q_RAW[0] + 1024)
        q_ops = [
            (sb.tile([P, NQ], U32, name="q_codes%d" % o, align_bytes=64), sb.tile([P, NQ], U8, name="q_scales%d" % o, align_bytes=64))
            for o in range(PASSES)
        ]

        def gather_keys(kw_got, g):
            cols = slice(g * PAGE // 16, (g + 1) * PAGE // 16)
            nc.vector.tensor_copy(kw_got[:], kw_win[:].bitcast(U32).indirect(offs_sb[:, cols]))
            return kw_got[:].bitcast(U16).rearrange("p (m t o) -> p o m t", t=PACK, o=PASSES)

        def quantise_queries(q_bf, o, first, count):
            q_codes, q_scales = q_ops[o]
            nc.vector.quantize_mx(
                out=q_codes[:, first : first + count].bitcast(FP8X4),
                scales=q_scales[:, first : first + count],
                in_=q_bf[:].rearrange("p q j -> p (q j)"),
            )

        probs = [sb.tile([P, PACK, NQ], F32, name="prob%d" % g) for g in range(PAGES)]
        scores = {}

        def score_pass(g, t, o, keys):
            if o == 0:
                scores[g, t] = ps.tile([P, NQ], F32, name="score%d" % (PACK * g + t), tag="bank%d" % (PACK * g + t))
            first = g * PAGE + t * P
            nc.tensor.matmul_mx(
                out=scores[g, t][:],
                lhsT=keys.bitcast(FP4X4),
                lhsT_scale=ks_planes[o][:, first : first + P],
                rhs=q_ops[o][0][:].bitcast(FP8X4),
                rhs_scale=q_ops[o][1][:],
                start=(o == 0),
                stop=(o == PASSES - 1),
            )
            if o == PASSES - 1:
                nc.scalar.activation(probs[g][:, t, :], scores[g, t][:], SIGMOID, bias=kb_got[:, first : first + 1])

        words = []
        for g in range(PAGES):
            kw_got = shared.tile([P, PAGE], U32, name="kw_got%d" % g, offset=AT_KB_WIN + 4096 + 2048 * g)
            words.append(gather_keys(kw_got, g))
        first_keys = shared.tile([P, 1024], U8, name="first_keys", align_bytes=64, offset=AT_FIRST_KEYS)
        nc.vector.tensor_copy(first_keys[:].bitcast(U16).rearrange("p (t m) -> p m t", t=PACK), words[0][:, 0])
        quantise_queries(q_first, 0, 0, NQ)
        for t in range(PACK):
            score_pass(0, t, 0, first_keys[:, t * 2 * P : (t + 1) * 2 * P])
        cast_queries(nc.vector.tensor_copy, q_third, 1, NQ // 2, NQ // 2)
        vs_first = shared.tile([P, PAGE], F32, name="vs_first", offset=AT_KB_WIN + 8192)
        nc.scalar.activation(vs_first[:], vs_win[:].indirect(offs_sb[:, 0 : PAGE // 16]), COPY)
        second_keys = shared.tile([P, 1024], U8, name="second_keys", align_bytes=64, offset=AT_Q_RAW[0])
        nc.vector.tensor_copy(second_keys[:].bitcast(U16).rearrange("p (t m) -> p m t", t=PACK), words[0][:, 1])
        quantise_queries(q_second, 1, 0, NQ // 2)
        quantise_queries(q_third, 1, NQ // 2, NQ // 2)
        for t in range(PACK):
            score_pass(0, t, 1, second_keys[:, t * 2 * P : (t + 1) * 2 * P])
        later_keys = shared.tile([P, 2 * 1024], U8, name="later_keys", align_bytes=64, offset=AT_Q_RAW[1] - 1984)
        for pair in range(2):
            keys = later_keys[:, pair * 1024 : (pair + 1) * 1024]
            nc.vector.tensor_copy(
                keys.bitcast(U16).rearrange("p (o u m) -> p o m u", o=PASSES, u=2),
                words[1][:, :, :, 2 * pair : 2 * pair + 2],
            )
            for u in range(2):
                for o in range(PASSES):
                    score_pass(1, 2 * pair + u, o, keys[:, (o * 2 + u) * 2 * P : (o * 2 + u + 1) * 2 * P])

        vs_gots = [vs_first, shared.tile([P, PAGE], F32, name="vs_second", offset=AT_FIRST_KEYS)]
        nc.vector.tensor_copy(vs_gots[1][:], vs_win[:].indirect(offs_sb[:, PAGE // 16 : N // 16]))
        w_first = sb.tile([P, NQ, PACK], BF16, name="w_first", align_bytes=64)
        w_late = [
            shared.tile([P, NQ // 2, PACK], BF16, name="w_late%d" % i, align_bytes=64, offset=AT_KS_WIN - 448 + 640 * i) for i in range(2)
        ]
        weights = [
            (
                sb.tile([P, NQ], U32, name="w_codes%d" % g, align_bytes=64),
                shared.tile([P, NQ], U8, name="w_scales%d" % g, align_bytes=64, offset=AT_KS_WIN + 64 + 1024 * g),
            )
            for g in range(PAGES)
        ]

        def weigh(w_bf, g, first, count):
            nc.vector.tensor_tensor(
                w_bf.rearrange("p (c i) t -> p c t i", i=4),
                probs[g][:, :, first : first + count].rearrange("p t (c i) -> p c t i", i=4),
                vs_gots[g][:].rearrange("p (t x) -> p t x", t=PACK)[:, :, 0:4].unsqueeze(1).to_broadcast([P, count // 4, PACK, 4]),
                MULT,
            )

        def quantise_weights(w_bf, g, first, count):
            w_codes, w_scales = weights[g]
            nc.vector.quantize_mx(
                out=w_codes[:, first : first + count].bitcast(FP8X4),
                scales=w_scales[:, first : first + count],
                in_=w_bf[:].rearrange("p q t -> p (q t)"),
            )

        weigh(w_first[:], 0, 0, NQ)
        vw_got = sb.tile([P, PAGES * DV], U32, name="vw_got", align_bytes=64)
        nc.vector.tensor_copy(vw_got[:], vw_win[:].bitcast(U32).indirect(voffs_sb[:]))
        weigh(w_late[0][:], 1, 0, NQ // 2)
        weigh(w_late[1][:, 0 : VECTOR_Q - NQ // 2, :], 1, NQ // 2, VECTOR_Q - NQ // 2)
        for t in range(PACK):
            nc.scalar.activation(
                w_late[1][:, VECTOR_Q - NQ // 2 : NQ // 2, t], probs[1][:, t, VECTOR_Q:NQ], COPY, scale=vs_gots[1][:, t * P : t * P + 1]
            )
        quantise_weights(w_first, 0, 0, NQ)
        for i in range(2):
            quantise_weights(w_late[i], 1, i * NQ // 2, NQ // 2)

        half = DV // 2
        ys = [ps.tile([P, half], F32, name="y%d" % h, tag="bank%d" % h) for h in range(2)]
        for g in range(PAGES):
            w_codes, w_scales = weights[g]
            for h in range(2):
                cols = slice(g * DV + h * half, g * DV + (h + 1) * half)
                nc.tensor.matmul_mx(
                    out=ys[h][:],
                    lhsT=w_codes[:].bitcast(FP8X4),
                    lhsT_scale=w_scales[:],
                    rhs=vw_got[:, cols].bitcast(FP8X4),
                    rhs_scale=vsc_plane[:].bitcast(U8)[:, cols],
                    start=(g == 0),
                    stop=(g == PAGES - 1),
                )
        results = [sb.tile([P, half], F32, name="result%d" % h, align_bytes=DMA_ALIGN) for h in range(2)]
        nc.scalar.activation(results[0][:], ys[0][:], COPY, scale=1.0 / 16.0)
        nc.vector.tensor_scalar(results[1][:], ys[1][:], 1.0 / 16.0, None, MULT)
        for h in range(2):
            nc.sync.dma_start(out[0][:, h * half : (h + 1) * half], results[h][:])
